import numpy as np, ml_dtypes
CORES = [35,38,43,46]
N = 4
BF = ml_dtypes.bfloat16
def gentries(a):
    return np.ascontiguousarray(a.reshape(8, 16, -1).transpose(0, 2, 1)).reshape(8, -1)
def gtable(e):
    e = np.asarray(e); return np.ascontiguousarray(e.reshape(8, -1, 16).transpose(0, 2, 1)).reshape(128, -1).astype(np.int32)
NM, LN, T, S = 4096, 256, 3, 1
LIMS = (13, 11, 12)
WT = np.array([1, 16, 256, 37, 411, 93, 777, 165, 1029, 251, 1313, 339, 1583, 503, 1847, 618], np.int32)
KA = np.array([3, 61, 118, 207, 346, 419, 530, 677, 742, 895, 1011, 1164, 1283, 1450, 1629, 1874], np.int32)
LO = min(LIMS)
def parts(rng):
    lo = rng.choice(np.array([0.7, 0.85, 0.95], np.float32), (N, 8, 1, 1, 1)); h = lo + (1 - lo) * rng.random((N, 8, 1, 2, NM), dtype=np.float32)
    wr = np.minimum((16 * h * rng.random((N, 8, 16, 2, NM), dtype=np.float32)).astype(np.int32), 15)
    da = rng.integers(0, 16, (N, 8, 16, 2, NM), dtype=np.int32)
    ls = rng.integers(0, NM, (N, 8, LN, 16)); ls = np.where(rng.random((N, 8, LN, 1)) < 0.3, ls >> 3, ls)
    z = rng.integers(0, 16, (N, 8, 16, LN))
    ls[:, :, 1::8] = ls[:, :, 0::8]; z[..., 1::8] = z[..., 0::8]
    return wr, da, ls, z
def pack(wr, da, ls, z):
    return {"pg": np.ascontiguousarray((16 * wr + da).reshape(N, 128, 2 * NM)).astype(np.float32).astype(BF),
            "nm": np.stack([gtable(a.reshape(8, -1)) for a in ls]), "zv": np.ascontiguousarray(z.reshape(N, 128, LN)).astype(np.float32).astype(BF)}
def setup_inputs(rng):
    wr, da, ls, z = parts(rng)
    return pack(wr, da, ls, z)
def setup_inputs_spread(rng):
    wr, da, ls, z = parts(rng)
    p = np.exp2(rng.integers(-2, 3, (N, 8, 1, 2, NM))).astype(np.float32)
    wr = np.minimum((16 * rng.random((N, 8, 16, 2, NM), dtype=np.float32) ** p).astype(np.int32), 15)
    da = da & rng.choice(np.array([0, 1, 3, 8, 12, 15], np.int32), (N, 8, 16, 1, NM))
    ls = np.minimum((NM * rng.random((N, 8, LN, 16)) ** rng.choice(np.array([1.0, 2.0, 4.0]), (N, 8, LN, 1))).astype(np.int64), NM - 1)
    z = z & rng.choice(np.array([0, 1, 4, 7, 15, 15]), (N, 8, 16, LN))
    return pack(wr, da, ls, z)
def setup_inputs_ends(rng):
    kind = rng.choice(6, (N, 8, NM), p=np.array([0.12, 0.08, 0.06, 0.06, 0.38, 0.3])); k = kind[:, :, None, None, :]
    e = rng.integers(0, 2, (N, 8, 16, 2, NM), dtype=np.int16); both = rng.random((N, 8, 16, 1, NM), dtype=np.float32) < 0.4
    side = np.array([0, 1], np.int16).reshape(1, 1, 1, 2, 1)
    top = np.where(both, np.int16(1), e); top = np.where(k == 3, side, top); top = np.where(k == 2, 1 - side, top); top = np.where(k == 1, np.int16(1), top); top = np.where(k == 0, np.int16(0), top)
    under = np.where(rng.random((N, 8, 1, 1, NM)) < 0.5, LIMS[0] - 1, LO - 1).astype(np.int16)
    wr = np.where(k == 5, under, 15 * top).astype(np.int32); da = 15 * np.where(k == 5, e, top).astype(np.int32)
    u0 = int(15 * np.add.reduce(WT)) & (NM - 1); cm = ((u0 * u0 >> 5) + KA.astype(np.int64) * u0) & (NM - 1)
    for q in range(N):
        for g in range(8):
            if g in (2, 7): wr[q, g][:, :, cm] = LIMS[0] - 1
            a, b = (NM - 1, 0) if g in (1, 4) else (0, NM - 1)
            wr[q, g][:, :, a] = 0; da[q, g][:, :, a] = 0; wr[q, g][:, :, b] = 15; da[q, g][:, :, b] = 15
    wr[:, 6, :, :, 1:3] = 15; da[:, 6, :, :, 1:3] = 15
    pos = np.argsort(rng.random((N, 8, LN, 16)), axis=-1) < 10
    ls = np.where(pos, (NM - 1) * rng.integers(0, 2, pos.shape), rng.integers(0, NM, pos.shape))
    z = 15 * rng.integers(0, 2, (N, 8, 16, LN)); o = rng.integers(0, 8, (N, 8, 1, LN)); z = np.where(o == 0, 0, np.where(o == 1, 15, z))
    for q in range(N):
        some = np.setdiff1d(np.nonzero(kind[q, 7] == 5)[0], np.append(cm, [0, NM - 1]))
        ls[q, 7] = np.where(pos[q, 7], 0, rng.choice(some, (LN, 16)))
        ls[q, 7, LN - 1] = np.where(np.arange(16) % 2 == 1, NM - 1, 0)
        ls[q, 6, LN - 1, 0] = 2; ls[q, 6, LN - 1, 1] = 1; ls[q, 6, LN - 1, 2] = NM - 1
    z[:, 7, :, LN - 1] = 0; z[:, 6, :, LN - 1] = 0
    return pack(wr, da, ls, z)
def setup_inputs_corners(rng):
    wr, da, ls, z = parts(rng); rot = int(rng.integers(0, 8)); sh = (16, 2, NM)
    z[..., ::5] = 0; z[..., 2::5] = 15
    for q in range(N):
        for g in range(8):
            j = (g + q + rot) % 8; a = wr[q, g]; d = da[q, g]
            if j == 0:
                a[...] = rng.integers(0, LO, sh)
                n = np.append(np.sort(rng.permutation(NM - 1)[:3]), NM - 1); i = int(rng.integers(0, 16))
                d[:, :, n[:2]] = 15; d[i, :, n[0]] = 14; d[:, :, n[2:]] = 0; d[15 - i, :, n[2]] = 1
                ls[q, g, 0::10, 3] = n[0]; ls[q, g, 0::10, 15] = n[1]; ls[q, g, 2::10, 0] = n[3]; ls[q, g, 2::10, 9] = n[2]
            if j == 1:
                a[...] = 15; d[:, :, int(rng.integers(0, 64))::64] = 15
            if j == 2: a[...] = np.where(rng.random(sh) < 0.25, rng.choice(np.array([LO - 1, LO, LIMS[0] - 1, LIMS[0]]), sh), rng.integers(0, 4, sh))
            if j == 3:
                a[:, 0] = rng.integers(14, 16, (16, NM)); a[:, 1] = rng.integers(0, LO, (16, NM))
                d[:, :, ::2] = 0; z[q, g, :, ::2] = 0; ls[q, g, ::16] -= ls[q, g, ::16] & 1
            if j == 4: d[...] = rng.integers(0, 16, (16, 1, 1))
            if j == 5: a[:, 1] = a[:, 0]
            if j == 6:
                fresh = rng.permutation(NM)[:NM >> 4]; a[...] = 15; a[:, :, fresh] = rng.integers(0, LO, (16, 2, NM >> 4))
            if j == 7: ls[q, g] = rng.choice(np.array([0, 1, NM - 2, NM - 1]), (LN, 16))
    return pack(wr, da, ls, z)
def hang(rng, a, d, w, u):
    y = rng.integers(0, 16, (16, len(w))); y[:3] = 0
    v = (u - np.add.reduce(WT.astype(np.int64)[:, None] * y, axis=0)) & (NM - 1)
    y[0] = v & 15; y[1] = (v >> 4) & 15; y[2] = v >> 8
    a[:, :, w] = 15; d[:, :, w] = y[:, None, :]
def firsts():
    u = np.arange(NM, dtype=np.int64)
    return ((u * u >> 5)[:, None] + KA.astype(np.int64) * u[:, None]) & (NM - 1)
def mates(rng, a, w):
    v = np.add.reduce(a.reshape(32, NM), axis=0).astype(np.int64); v[w] = 1 << 20
    c = firsts()
    low = np.min(v[c] * NM + c, axis=1); b = np.where(low >= NM << 20, -1, low & (NM - 1))
    val, first = np.unique(b, return_index=True)
    return rng.permutation(first[val >= 0])
def setup_inputs_crowd(rng):
    wr, da, ls, z = parts(rng); pr = rng.permutation(N)
    for q in range(N):
        for g in range(8):
            a = wr[q, g]; d = da[q, g]; a[...] = rng.integers(0, 3, (16, 2, NM)); j = (g + q) % 8
            o = rng.permutation(NM)
            if j == 6: o = o[o > 0]
            w = o[:LN]
            if q == pr[0] or q == pr[1]:
                old = o[LN:LN + (NM >> 3)]; a[:, :, old] = 15; d[:, :, old] = 15 * rng.integers(0, 2, (16, 1, len(old)))
                hang(rng, a, d, w, np.resize(mates(rng, a, np.append(w, old)), LN)); ls[q, g] = w[:, None]
                if q == pr[1] and g == 7: ls[q, g, LN - 1] = w[0]
            elif j < 2:
                us = np.resize(mates(rng, a, w), LN); hang(rng, a, d, w[:2], us[:2]); ls[q, g] = w[0]
                if j == 1: ls[q, g, LN - 1] = w[1]
            elif j < 4:
                us = np.resize(mates(rng, a, w), LN); one = np.full(LN, us[0])
                if j == 3: one[LN - 1] = us[1]
                hang(rng, a, d, w, one); ls[q, g] = w[:, None]
            elif j < 6:
                ls[q, g] = w[:, None]
                if j == 5: ls[q, g, LN - 1] = w[0]
            elif j == 6:
                a[:, :, 0] = 0; us = np.nonzero(np.any(firsts() == 0, axis=1))[0]
                hang(rng, a, d, w, np.full(LN, int(rng.choice(us)))); ls[q, g] = w[:, None]
            else:
                a[...] = rng.integers(LIMS[0] - 2, LIMS[0], (16, 2, NM)); sp = o[LN:LN + (NM >> 2)]; a[:, :, sp] = 0
                a[rng.integers(0, 16, len(sp)), rng.integers(0, 2, len(sp)), sp] = 15
                hang(rng, a, d, w, rng.permutation(NM)[:LN]); ls[q, g] = w[:, None]
    return pack(wr, da, ls, z)
def check_inputs(d):
    bad = []
    for k, hi in (("pg", 255), ("nm", NM - 1), ("zv", 15)):
        x = np.asarray(d[k]).astype(np.float32)
        if not np.all((x >= 0) & (x <= hi) & (x == np.floor(x))): bad.append("range of " + k)
    return bad
def pick(a, ix):
    return np.take_along_axis(a, ix[:, :, None, :], 3)
def reference(pg, nm, zv):
    v = pg.astype(np.float32).astype(np.int32).reshape(N, 8, 16, 2, NM); wr = v >> 4; da = v & 15
    ls = np.stack([gentries(a) for a in nm]).astype(np.int32)
    z = zv.astype(np.float32).astype(np.int32).reshape(N, 8, 16, LN)
    A = np.zeros((N, 1, 1, 1), np.int32); low = np.tril(np.ones((LN, LN), bool), -1); NONE = 1 << 30
    for t in range(T):
        lim = LIMS[t]
        if t > 0: ls = np.roll(ls, S, axis=0); z = np.roll(z, S, axis=0)
        f = wr[:, :, :, 0]; s = wr[:, :, :, 1]
        y = np.where(f <= s, da[:, :, :, 0], da[:, :, :, 1])
        lk = ls.reshape(N, 8, LN, 16)
        sc = np.add.reduce(np.abs(pick(y, ls).reshape(N, 8, 16, LN, 16) - z[..., None]), axis=2).astype(np.int32)
        w = NM - 1 - (np.max(sc * NM + (NM - 1 - lk), axis=3) & (NM - 1))
        yw = pick(y, w); fw = pick(f, w); sw = pick(s, w)
        u = (np.add.reduce(WT[:, None] * yw, axis=2) & (NM - 1)).astype(np.int32)
        faulty = np.any((fw >= lim) & (sw >= lim), axis=2)
        c = ((u * u >> 5)[..., None] + KA * u[..., None] + A) & (NM - 1)
        cx = c.reshape(N, 8, LN * 16)
        m1 = np.minimum(fw[..., None], pick(s, cx).reshape(N, 8, 16, LN, 16)); m2 = np.minimum(pick(f, cx).reshape(N, 8, 16, LN, 16), sw[..., None])
        ok = np.max(np.maximum(m1, m2), axis=2) < lim
        best = np.min(np.where(ok, np.add.reduce(m1 + m2, axis=2) * NM + c, NONE), axis=3)
        has = faulty & (best < NONE); cl = np.where(has, best & (NM - 1), -1)
        wa, wb, ca, cb = w[:, :, :, None], w[:, :, None, :], cl[:, :, :, None], cl[:, :, None, :]
        hit = (wa == wb) | (wa == cb) | (ca == wb) | ((ca == cb) & (ca >= 0))
        com = ~np.any(hit & low, axis=3)
        q, g, l = np.nonzero(com & ~faulty); n = w[q, g, l]
        zn = z[q, g, :, l][:, :, None]; od = da[q, g, :, :, n]; ow = wr[q, g, :, :, n]
        nw = np.minimum(15, ow + (od != zn))
        ex = com & has; q2, g2, l2 = np.nonzero(ex); n2 = w[q2, g2, l2]; o2 = cl[q2, g2, l2]
        a1 = wr[q2, g2, :, 1, n2]; b1 = wr[q2, g2, :, 1, o2]; ya = y[q2, g2, :, n2]; yb = y[q2, g2, :, o2]
        wr[q, g, :, :, n] = nw; da[q, g, :, :, n] = zn
        wr[q2, g2, :, 1, n2] = b1; wr[q2, g2, :, 1, o2] = a1
        da[q2, g2, :, :, n2] = ya[:, :, None]; da[q2, g2, :, :, o2] = yb[:, :, None]
        A = np.add.reduce(ex.reshape(N, -1).astype(np.int32), axis=1).astype(np.int32).reshape(N, 1, 1, 1)
        k = np.arange(16 * LN, dtype=np.int32).reshape(LN, 16)
        ls = (((lk * (2 * (u & 1023) + 1)[..., None] >> 5) + lk + 37 * k) & (NM - 1)).reshape(N, 8, 16 * LN)
        z = np.abs(z - yw)
    e = 16 * wr + da
    return {"ys": np.ascontiguousarray(e[:, :, :, 1].reshape(N, 128, NM)).astype(np.float32).astype(BF),
            "yf": np.add.reduce(e[:, :, :, 0].reshape(N, 128, NM >> 6, 64), axis=2).astype(np.float32),
            "yn": np.stack([gtable(a) for a in ls]).astype(np.float32),
            "yz": np.ascontiguousarray(z.reshape(N, 128, LN)).astype(np.float32).astype(BF)}

@@ -1,0 +1,631 @@
+import math
+import numpy as np
+from concourse.bass import DstId, RemoteDMATransfer
+from concourse.mybir import AluOpType as A, AxisListType, ActivationFunctionType as AF
+
+NM, LN, NV = 4096, 256, 3
+LIMS = (13, 11, 12)
+WT = (1, 16, 256, 37, 411, 93, 777, 165, 1029, 251, 1313, 339, 1583, 503, 1847, 618)
+KA = (3, 61, 118, 207, 346, 419, 530, 677, 742, 895, 1011, 1164, 1283, 1450, 1629, 1874)
+TS = NM + 2 * LN
+OY, OG2, OE2, OG1, OE1 = 0, TS, 2 * TS, 3 * TS, 4 * TS
+LN2 = math.log(2.0)
+RND = 3064.5
+PIECES = (512, 512, 1024, 1024, 1024)
+OPT = {"nh": 2, "va": ((0, 1, 4, 5), (0, 4), (0, 4)), "vc": ((0, 8), (0, 8), (0, 8)), "wbs": 1, "ne": 1, "wn": 1, "tz": 1,
+       "seed": 0, "noise": 3000.0, "iters": 150, "look": 300.0, "lam": 20.0, "frac": 0.1, "boost": 2000.0, "ga": 1.56, "sca": 3.8, "hop": 110.0}
+BOOST = ("cl", "cl2", "fr", "gn", "ne", "wn", "tz", "wl2")
+
+B, F, I, U, H = "bfloat16", "float32", "int32", "uint16", "float16"
+SB = {
+    "tb": (5 * TS, B), "io32": (TS, F), "wq": (2048, B), "wb": (8192, B), "sel": (1024, B), "tt": (1024, B),
+    "ab": (4096, B), "ga": (4096, B), "gb": (8192, B), "mm": (8192, B), "xx": (2048, F), "eb": (2048, B),
+    "pi": (1, I), "pj": (4, I), "pf": (16, F), "rd": (128, I), "wr": (16, F), "rr": (512, U), "il": (32, U),
+    "ids": (1408, B), "sm": (144, F), "idf": (128, F), "zp": (144, B), "zn": (144, B), "zw": (144, H),
+    "i16": (16, F), "m8": (8, F), "tile": (16, U), "prm": (48, U), "hitl": (4, U), "d3": (48, F), "pc2": (16, F),
+    "k37": (256, F), "ka": (256, F), "th": (512, B), "keep": (512, B), "c1": (512, F), "c2": (512, F), "c3": (512, B), "c4": (512, B),
+    "nmi": (256, I), "npf": (256, F), "t1f": (256, F),
+    "off0": (256, U), "off1": (256, U), "off2": (256, U), "z0": (256, B), "z1": (256, B), "z2": (256, B),
+    "offo0": (256, U), "offo1": (256, U), "zo0": (256, B), "zo1": (256, B), "zo2": (256, B), "nf0": (256, F), "nf1": (256, F), "nf2": (256, F),
+    "run": (256, F), "r64": (256, F), "r32": (192, F), "ki": (16, I), "wi": (16, I), "wl": (32, U), "xf": (32, F),
+    "yh": (256, H), "yw": (256, B), "g1w": (256, B), "g2w": (256, B), "ui": (16, I), "uu": (16, I), "aa": (16, I),
+    "ca": (256, F), "cb": (256, I), "ci": (256, I), "co": (256, U), "cf": (256, F), "d1": (64, F), "d2": (64, F), "kc": (64, F),
+    "mg": (256, B), "fr": (256, B), "nfl": (256, B), "tz": (256, B), "ew": (512, B), "wqw": (512, B), "s2": (512, B), "ne": (512, B),
+    "wn": (512, B), "wr2": (512, B), "ex": (512, B), "gn": (512, B), "rl": (256, B), "ee": (512, B), "s1": (512, B),
+    "kj": (16, I), "ce": (16, I), "cl": (32, U), "bb": (48, F),
+    "g2c": (256, B), "wqc": (512, B), "w2c": (256, B), "yc": (256, B), "s3": (256, B),
+    "sc": (512, B), "hm": (48, F), "o1": (48, F), "o2": (48, F), "ol": (48, U), "exf": (16, B), "ac": (2, F),
+    "kk": (16, I), "k2": (16, F), "q1": (256, F), "q2": (256, I), "ni": (256, I), "nfn": (256, F), "yno": (256, F), "yfo": (64, F),
+}
+SMALL = ("has", "b1", "b2", "p1", "dk", "flb", "sq", "dz", "dum")
+IDS = (("id1", 1.0), ("idn", -1.0), ("id16", 0.0625), ("id20", -20.0), ("id256", -256.0), ("idm16", -16.0), ("id40", -2.0 ** 40), ("idp16", 16.0))
+SCRATCH = {n: ("sbuf", [128, w], d) for n, (w, d) in SB.items()}
+for _b in range(8):
+    SCRATCH["ps%d" % _b] = ("psum", [128, 512], F)
+SEMAPHORES = ["eV", "eS", "eP", "eG", "arr1", "arr2", "sent"] + ["d%d" % _i for _i in range(20)]
+INFO = {}
+
+
+def build(g, T, nxt, mk):
+    ops = []
+    V, S, P = g.vector, g.scalar, g.tensor
+    GA, SCA, NH = OPT["ga"], OPT["sca"], OPT["nh"]
+    QH, LH = 16 // NH, LN // NH
+
+    def op(e, fn, cost, r, w, lat=0.0, kind="c"):
+        ops.append({"e": e, "fn": fn, "c": cost, "r": list(r), "w": list(w), "lat": lat, "k": kind})
+
+    def vc(n):
+        return 45 + 0.83 * max(64, n)
+
+    def ts(o, i, s1, s2, o0, o1, n, r, w):
+        if o1 is None:
+            op("V", lambda: V.tensor_scalar(o, i, s1, None, o0), vc(n), r, w)
+        else:
+            op("V", lambda: V.tensor_scalar(o, i, s1, s2, o0, o1), vc(n), r, w)
+
+    def tt(o, a, b, o0, n, r, w):
+        op("V", lambda: V.tensor_tensor(o, a, b, o0), vc(n), r, w)
+
+    def cp(o, i, n, r, w):
+        op("V", lambda: V.tensor_copy(o, i), vc(n), r, w)
+
+    def act(o, i, f, n, r, w, bias=0.0, scale=1.0):
+        op("S", lambda: S.activation(o, i, f, bias=bias, scale=scale), 70 + 0.83 * n, r, w)
+
+    def mm(o, l, rh, st, sp, n, r, w, k=1):
+        op("P", lambda: P.matmul(o, l, rh, st, sp), 8 + 0.42 * k * max(64, n), r, w)
+
+    def mms(b, x0, n, terms):
+        for j, (l, rh, r) in enumerate(terms):
+            mm(ps[b][:, x0:x0 + n], C[l], rh, j == 0, j == len(terms) - 1, n, r + [l], [pk(b)])
+
+    def dma(o, i, nbytes, r, w, e="Y"):
+        op(e, lambda: (S if e == "S" else g.sync).dma_start(o, i), 60, r, w, lat=1800 + nbytes / 150.0, kind="d")
+
+    def iota(o, pat, base, cm, n, w):
+        op("G", lambda: g.iota(o, pat, base, cm, allow_small_or_imprecise_dtypes=True), 130 + 1.66 * n, [], w)
+
+    tb, io, pf = T.tb, T.io32, T.pf
+    C = {n: T.ids[:, 128 * j:128 * j + 128] for j, n in enumerate([x[0] for x in IDS] + ["bone", "bw", "ones"])}
+    ps = [T["ps%d" % b] for b in range(8)]
+
+    def sm(n, a=0, b=16):
+        j = 16 * SMALL.index(n)
+        return T.sm[:, j + a:j + b]
+
+    def pk(b):
+        return "ps%d" % b
+
+    def win(o, n=1):
+        return tb[:, o:o + n * TS]
+
+    def tk(*ns):
+        return ["%s.%d" % (n, k) for n in ns for k in range(9)]
+
+    def hk(n):
+        return ["%s%d" % (n, h) for h in range(NH)]
+
+    dma(T.nmi[:], T.nm[:], 131072, [], ["nmi"])
+    c0 = 0
+    for j, wd in enumerate(PIECES):
+        ks = range(c0 // 512, (c0 + wd) // 512)
+        dma(tb[:, OE2 + c0:OE2 + c0 + wd], T.pg[:, NM + c0:NM + c0 + wd], 256 * (2 * c0 + wd), [], ["E2.%d" % k for k in ks])
+        dma(tb[:, OE1 + c0:OE1 + c0 + wd], T.pg[:, c0:c0 + wd], 256 * (2 * c0 + 2 * wd), [], ["E1.%d" % k for k in ks], "S")
+        if j == 1:
+            dma(T.z0[:], T.zv[:], 256 * 2048, [], ["z0"])
+        c0 += wd
+
+    op("G", lambda: g.iota(T.pi[:], [[0, 1]], 0, 1), 135, [], ["pi"])
+    iota(io[:, 0:256], [[1, 256]], 0, 0, 256, ["io0"])
+    iota(T.pc2[:], [[128, 2], [2, 8]] if NH == 2 else [[1, 16]], 0, 0, 16, ["pc2"])
+    iota(T.c1[:], [[-48, 16], [0, 2], [-3, 16]], 0, 0, 512, ["c1"])
+    iota(T.c2[:], [[0, 32], [1, 16]], 0, 0, 512, ["c2"])
+    iota(T.c3[:], [[0, 512]], 1, 0, 512, ["c3"])
+    iota(T.k37[:], [[(9472 * QH) % NM, NH], [37, 16], [9472, QH]], 0, 0, 256, ["k37"])
+    iota(io[:, 256:TS], [[1, TS - 256]], 256, 0, TS - 256, ["io1"])
+    ts(T.pj[:, 0:1], T.pi[:], 15, None, A.bitwise_and, None, 1, ["pi"], ["pj0"])
+    ts(T.pj[:, 1:2], T.pi[:], 4, None, A.arith_shift_right, None, 1, ["pi"], ["pj1"])
+    ts(T.pj[:, 2:3], T.pi[:], QH - 1, None, A.bitwise_and, None, 1, ["pi"], ["pj2"])
+    pc, pm, pd, pq, zc, pm16, hc, kc37, rho, wc, ph, pa, pb = [pf[:, j:j + 1] for j in range(13)]
+    cp(pc, T.pi[:], 1, ["pi"], ["pc"])
+    cp(pf[:, 1:4], T.pj[:, 0:3], 3, ["pj0", "pj1", "pj2"], ["pm"])
+    ts(zc, pd, 16.0, 15.0, A.mult, A.add, 1, ["pm"], ["zc"])
+    ts(pm16, pm, 16.0, None, A.mult, None, 1, ["pm"], ["pm16"])
+    ts(hc, pm, 32.0, 31.0, A.mult, A.add, 1, ["pm"], ["hc"])
+    ts(kc37, pm, 592.0, None, A.mult, None, 1, ["pm"], ["kc37"])
+    ts(ph, pm, pq, 1.0 / QH, A.subtract, A.mult, 1, ["pm"], ["ph"])
+    ts(pa, pq, 16.0, ph, A.mult, A.add, 1, ["pm", "ph"], ["pa"])
+    ts(pb, ph, 128.0, pq, A.mult, A.add, 1, ["pm", "ph"], ["pb"])
+    act(rho, pm, AF.Exp, 1400, ["pm"], ["rho"], scale=-0.75 * LN2)
+    for n, s in IDS:
+        ts(C[n], io[:, 0:128], pc, s, A.is_equal, A.mult, 128, ["io0", "pc"], [n])
+    ts(T.idf[:], io[:, 0:128], pc, None, A.is_equal, None, 128, ["io0", "pc"], ["idf"])
+    ts(T.i16[:], io[:, 0:16], pm, None, A.is_equal, None, 16, ["io0", "pm"], ["i16"])
+    ts(T.m8[:], io[:, 0:8], pd, None, A.is_equal, None, 8, ["io0", "pm"], ["m8"])
+    ts(T.prm[:, 0:16], io[:, 0:16], pm16, None, A.add, None, 16, ["io0", "pm16"], ["prm1"])
+    ts(T.prm[:, 16:32], T.pc2[:], pa, None, A.add, None, 16, ["pc2", "pa"], ["prm2"])
+    ts(T.prm[:, 32:48], io[:, 0:16], float(QH), pb, A.mult, A.add, 16, ["io0", "pb"], ["prm3"])
+    ts(T.tile[:], io[:, 0:16], 0.0, pq, A.mult, A.add, 16, ["io0", "pm"], ["tile"])
+    ts(T.hitl[:], io[:, 0:4], 0.0, hc, A.mult, A.add, 4, ["io0", "hc"], ["hitl"])
+    ts(T.zp[:], io[:, 0:144], zc, 8192.0, A.is_equal, A.mult, 144, ["io0", "zc"], ["zp"])
+    ts(T.zn[:], io[:, 0:144], zc, -8192.0, A.is_equal, A.mult, 144, ["io0", "zc"], ["zn"])
+    for j in range(16):
+        act(T.wr[:, j:j + 1], io[:, 0:1], AF.Identity, 1, ["io0"], ["wr%d" % j], bias=float(WT[j]), scale=0.0)
+        act(T.ka[:, QH * j:QH * j + QH], io[:, 0:QH], AF.Identity, QH, ["io0"], ["ka%d" % j], bias=float(KA[j]), scale=0.0)
+    kak = ["ka%d" % j for j in range(16)]
+    tt(T.wr[:], T.wr[:], T.i16[:], A.mult, 32, ["wr%d" % j for j in range(16)] + ["i16"], ["wrm"])
+    op("V", lambda: V.tensor_reduce(wc, T.wr[:], AxisListType.X, A.add), vc(16), ["wrm"], ["wc"])
+    ts(T.zw[:], io[:, 0:144], zc, wc, A.is_equal, A.mult, 144, ["io0", "zc", "wc"], ["zw"])
+    ts(T.rd[:], io[:, 0:128], 0.0625, -0.46875, A.mult, A.add, 128, ["io0"], ["rd"])
+    ts(C["bone"], T.rd[:], pd, None, A.is_equal, None, 128, ["rd", "pm"], ["bone"])
+    ts(C["bw"], T.rd[:], pd, rho, A.is_equal, A.mult, 128, ["rd", "pm", "rho"], ["bw"])
+    op("V", lambda: V.memset(C["ones"], 1.0), vc(64), [], ["ones"])
+    ts(sm("dum"), io[:, 0:16], 16.0, pm, A.mult, A.add, 16, ["io0", "pm"], ["dum"])
+    for j, x in enumerate((TS + NM, NM, NM)):
+        ts(T.d3[:, 16 * j:16 * j + 16], sm("dum"), float(x), None, A.add, None, 16, ["dum"], ["d3%d" % j])
+    ts(sm("dz"), sm("dum"), float(NM + LN - 8192), None, A.add, None, 16, ["dum"], ["dz"])
+    ts(T.k37[:], T.k37[:], kc37, 32.0, A.add, A.mult, 256, ["k37", "kc37"], ["k37"])
+    act(T.c4[:], T.c1[:], AF.Exp, 512, ["c1"], ["c4"], bias=90 * LN2 + math.log(2.57), scale=LN2 / 4)
+    ts(T.th[:], T.c2[:], pm, 2.0 ** 95, A.not_equal, A.mult, 512, ["c2", "pm"], ["th"])
+    op("G", lambda: g.affine_select(T.keep[:], T.c3[:], [[0, 16], [1, 32]], A.is_gt, 0.0, 0, 0), 1020, ["c3"], ["keep"])
+    for n, o in (("Y", OY), ("G2", OG2), ("E2", OE2), ("G1", OG1), ("E1", OE1)):
+        iota(tb[:, o + NM:o + TS], [[0, 512]], 0, 0, 512, [n + ".8"])
+
+    def turn(src, ksrc, bank, dst, kdst):
+        for j in range(8):
+            o = T.xx[:, 256 * j:256 * j + 256]
+            if j % 2:
+                ts(o, src, T.m8[:, j:j + 1], None, A.mult, None, 256, [ksrc, "m8"], ["xx%d" % j])
+            else:
+                act(o, src, AF.Identity, 256, [ksrc, "m8"], ["xx%d" % j], scale=T.m8[:, j:j + 1])
+        for q in range(16):
+            mm(ps[bank][:, 16 * q:16 * q + 16], T.xx[:, q:2048:16], T.i16[:], True, True, 64, ["xx%d" % j for j in range(8)] + ["i16"], [pk(bank)], 4)
+        act(dst, ps[bank][:, 0:256], AF.Identity, 256, [pk(bank)], [kdst])
+
+    cp(T.npf[:], T.nmi[:].indirect(T.prm[:, 0:16]), GA * 256, ["nmi", "prm1"], ["npf"])
+    turn(T.npf[:], "npf", 7, T.t1f[:], "t1f")
+    cp(T.off0[:], T.t1f[:].indirect(T.prm[:, 16:32]), GA * 256, ["t1f", "prm2"], ["off0"])
+
+    for k in range(8):
+        b = k % 2
+        a0 = 512 * k
+        e1, e2 = tb[:, OE1 + a0:OE1 + a0 + 512], tb[:, OE2 + a0:OE2 + a0 + 512]
+        w2, w1 = T.wq[:, 1024 * b:1024 * b + 512], T.wq[:, 1024 * b + 512:1024 * b + 1024]
+        k1, k2, q1, q2 = "E1.%d" % k, "E2.%d" % k, "wq1%d" % b, "wq2%d" % b
+        ts(w2, e2, RND + 16, None, A.add, None, 256, [k2], [q2])
+        ts(w1, e1, RND, None, A.add, None, 256, [k1], [q1])
+        mms(b, 0, 512, [("id1", w1, [q1]), ("idn", w2, [q2])])
+        sel, tq = T.sel[:, 512 * b:512 * b + 512], T.tt[:, 512 * b:512 * b + 512]
+        act(sel, ps[b][:], AF.Relu, 512, [pk(b)], ["sel%d" % b], bias=16.0, scale=2.0)
+        mms(2 + b, 0, 512, [("id1", e2, [k2]), ("id1", w2, [q2]), ("idn", w1, [q1])])
+        tt(tq, ps[2 + b][:], e1, A.min, 512, [pk(2 + b), k1], ["tt%d" % b])
+        mms(4, 0, 512, [("idn", w1, [q1]), ("id1", tq, ["tt%d" % b]), ("id1", sel, ["sel%d" % b])])
+        act(tb[:, OY + a0:OY + a0 + 512], ps[4][:], AF.Identity, 512, ["ps4"], ["Y.%d" % k], bias=3072.0)
+        for s, o, n, x0, kq in ((0, OG2, "G2", w2, q2), (1, OG1, "G1", w1, q1)):
+            x = T.wb[:, 1024 * k + 512 * s:1024 * k + 512 * s + 512]
+            kx = "wb%d.%d" % (k, s)
+            if (2 * k + s) % 4 < OPT["wbs"]:
+                act(x, x0, AF.Identity, 512, [kq], [kx], bias=-193.0 + s, scale=0.0625)
+            else:
+                ts(x, x0, 0.0625, -193.0 + s, A.mult, A.add, 256, [kq], [kx])
+            act(ps[5 + s][:], x, AF.Exp, 512, [kx], [pk(5 + s)], bias=-67 * LN2, scale=7 * LN2)
+            tt(tb[:, o + a0:o + a0 + 512], ps[5 + s][:], x, A.max, 512, [pk(5 + s), kx], ["%s.%d" % (n, k)])
+
+    def fold(ph_, j, src, n, ksrc, out, kout, first=None):
+        run, r64, kr = T.run[:, 64 * ph_:64 * ph_ + 64], T.r64[:, 64 * ph_:64 * ph_ + 64], "run%d" % ph_
+        if j == 0:
+            if first is None:
+                cp(run, src[:, 0:64], 64, [ksrc], [kr])
+            else:
+                tt(T.run[:, 64 * ph_:64 * ph_ + QH], src[:, 0:QH], first[0], A.min, 32, [ksrc, first[1]], [kr])
+                cp(T.run[:, 64 * ph_ + QH:64 * ph_ + 64], src[:, QH:64], 48, [ksrc], [kr + "b"])
+        elif j < 4 // NH - 1:
+            tt(run, src[:, 0:64], run, A.min, n, [ksrc, kr, kr + "b"], [kr, kr + "b"])
+        else:
+            tt(r64, src[:, 0:64], run, A.min, n, [ksrc, kr, kr + "b"], ["r64%d" % ph_])
+            a, b = 64 * ph_, 48 * ph_
+            tt(T.r32[:, b:b + 32], T.r64[:, a:a + 32], T.r64[:, a + 32:a + 64], A.min, 64, ["r64%d" % ph_], ["r32%d" % ph_])
+            if NH == 1:
+                tt(out, T.r32[:, b:b + 16], T.r32[:, b + 16:b + 32], A.min, 32, ["r32%d" % ph_], [kout])
+            else:
+                tt(T.r32[:, b + 32:b + 48], T.r32[:, b:b + 16], T.r32[:, b + 16:b + 32], A.min, 32, ["r32%d" % ph_], ["r16%d" % ph_])
+                tt(out, T.r32[:, b + 32:b + 40], T.r32[:, b + 40:b + 48], A.min, 16, ["r16%d" % ph_], [kout])
+
+    MB = 512 // LH
+    for t in range(NV):
+        last = t == NV - 1
+        lim = LIMS[t]
+        glim = 0.9 * 2.0 ** (7 * lim - 67)
+        off, z, nf, zo = T["off%d" % t], T["z%d" % t], T["nf%d" % t], T["zo%d" % t]
+        ko, kz, kn, kzo = "off%d" % t, "z%d" % t, "nf%d" % t, "zo%d" % t
+        if t > 0:
+            op(None, "arr%d" % t, 0, ["sent%d" % (t - 1)], [ko, kz], lat=500, kind="x")
+        cp(nf[:], off[:], 256, [ko], [kn])
+        for h in range(NH):
+            lr = slice(LH * h, LH * h + LH)
+            qr = slice(QH * h, QH * h + QH)
+            zh = z[:, lr]
+            sh = str(h)
+            for u in range(8 // NH * h, 8 // NH * (h + 1)):
+                a0 = 512 * u
+                gk = ["ga%d.%d" % (u, v) for v in range(MB)]
+                if u in OPT["va"][t]:
+                    for v in range(MB):
+                        tt(T.ga[:, a0 + LH * v:a0 + LH * v + LH], win(OY).indirect(off[:, 32 * u + QH * v:32 * u + QH * v + QH]), zh, A.subtract,
+                           GA * LH, tk("Y") + [ko, kz], [gk[v]])
+                    act(T.ab[:, a0:a0 + 512], T.ga[:, a0:a0 + 512], AF.Abs, 512, gk, ["ab%d" % u])
+                else:
+                    b = u % 2
+                    act(T.ga[:, a0:a0 + 512], win(OY).indirect(off[:, 32 * u:32 * u + 32]), AF.Identity, GA * 512, tk("Y") + [ko], gk)
+                    for v in range(MB):
+                        mms(b, LH * v, LH, [("idn", zh, [kz]), ("id1", T.ga[:, a0 + LH * v:a0 + LH * v + LH], gk)])
+                    act(T.ab[:, a0:a0 + 512], ps[b][:], AF.Abs, 512, [pk(b)], ["ab%d" % u])
+                if u % 2:
+                    j = u // 2
+                    b = 2 + j % 2
+                    mm(ps[b][:, 0:64], T.idf[:], nf[:, 64 * j:64 * j + 64], True, False, 64, ["idf", kn], [pk(b)], 4)
+                    for r in range(16):
+                        mm(ps[b][:, 0:64], T.zn[:, 15 - r:143 - r], T.ab[:, 1024 * j + r:1024 * j + 1024:16], False, r == 15, 64, ["zn", "ab%d" % (u - 1), "ab%d" % u], [pk(b)])
+                    fold(h, j - 4 // NH * h, ps[b], 64, pk(b), T.ki[:, qr], "ki" + sh)
+            ts(T.wi[:, qr], T.ki[:, qr], 8191, None, A.bitwise_and, None, 16, ["ki" + sh], ["wi" + sh])
+            wl = T.wl[:, qr]
+            cp(wl, T.wi[:, qr], 16, ["wi" + sh], ["wl" + sh])
+            cp(T.yh[:, lr], win(OY).indirect(wl), GA * LH, tk("Y") + ["wl" + sh], ["yh" + sh])
+            act(T.g1w[:, lr], win(OG1).indirect(wl), AF.Identity, GA * LH, tk("G1") + ["wl" + sh], ["g1w" + sh])
+            act(T.g2w[:, lr], win(OG2).indirect(wl), AF.Identity, GA * LH, tk("G2") + ["wl" + sh], ["g2w" + sh])
+            for r in range(16):
+                mm(ps[4][:, 0:QH], T.zw[:, 15 - r:143 - r], T.yh[:, LH * h + r:LH * h + LH:16], r == 0, r == 15, 16, ["zw", "yh" + sh], ["ps4"])
+            cp(T.ui[:, qr], ps[4][:, 0:QH], 16, ["ps4"], ["ui" + sh])
+            ts(T.uu[:, qr], T.ui[:, qr], 4095, None, A.bitwise_and, None, 16, ["ui" + sh], ["uu" + sh])
+            sq = sm("sq", QH * h, QH * h + QH)
+            tt(sq, T.uu[:, qr], T.uu[:, qr], A.mult, 32, ["uu" + sh], ["sq" + sh])
+            ts(T.aa[:, qr], sq, 0.03125, -0.375 if t == 0 else T.ac[:, 1:2], A.mult, A.add, 16, ["sq" + sh] + (["ac1"] if t else []), ["aa" + sh])
+            for v, (x0, x1) in enumerate(((0, 64), (64, 256)) if NH == 1 else ((0, 128),)):
+                n = x1 - x0
+                tl, xr, kv = T.tile[:, 0:n // 16], slice(LH * h + x0, LH * h + x1), str(h + v)
+                tt(T.ca[:, xr], T.uu[:, qr].indirect(tl), T.ka[:, x0:x1], A.mult, GA * n, ["uu" + sh, "tile"] + kak, ["ca" + kv])
+                tt(T.cb[:, xr], T.aa[:, qr].indirect(tl), T.ca[:, xr], A.add, GA * n, ["aa" + sh, "tile", "ca" + kv], ["cb" + kv])
+                ts(T.ci[:, xr], T.cb[:, xr], 4095, None, A.bitwise_and, None, n, ["cb" + kv], ["ci" + kv])
+                cp(T.co[:, xr], T.ci[:, xr], n, ["ci" + kv], ["co" + kv])
+                if lim == 11:
+                    cp(T.cf[:, xr], T.ci[:, xr], n, ["ci" + kv], ["cf" + kv])
+            rb = 6 if h < NH - 1 else 0
+            for s, x, kx in ((0, T.g1w, "g1w"), (1, T.g2w, "g2w")):
+                for v in range(MB):
+                    mms(rb + s, LH * v, LH, [("id1", x[:, lr], [kx + sh])])
+            tt(T.mg[:, lr], ps[rb][:, 0:LH], T.g2w[:, lr], A.min, LH, [pk(rb), "g2w" + sh], ["mg" + sh])
+            for r in range(16):
+                mm(ps[5][:, 0:QH], T.zp[:, 15 - r:143 - r], T.mg[:, LH * h + r:LH * h + LH:16], r == 0, r == 15, 16, ["zp", "mg" + sh], ["ps5"])
+            ts(sm("flb", QH * h, QH * h + QH), ps[5][:, 0:QH], glim * 8192, 386.0 * 8192, A.is_ge, A.mult, 16, ["ps5"], ["flb" + sh])
+            tt(sm("dk", QH * h, QH * h + QH), sm("flb", QH * h, QH * h + QH), sm("dz", QH * h, QH * h + QH), A.add, 32, ["flb" + sh, "dz"], ["dk" + sh])
+        ts(T.wl[:, 16:32], T.wi[:], float(2 * TS), None, A.add, None, 16, hk("wi"), ["wl2"])
+        cp(T.xf[:, 0:32:2], T.wi[:], 16, hk("wi"), ["xfw"])
+        act(T.yw[:], win(OY).indirect(T.wl[:, 0:16]), AF.Identity, GA * 256, tk("Y") + hk("wl"), ["yw"])
+        mms(5, 0, 256, [("bone", T.mg[:], hk("mg"))])
+        ts(T.fr[:], ps[5][:, 0:256], glim, None, A.is_ge, None, 256, ["ps5"], ["fr"])
+        act(T.nfl[:], T.fr[:], AF.Identity, 256, ["fr"], ["nfl"], bias=1.0, scale=-1.0)
+        if not last:
+            tt(sm("p1"), sm("flb"), T.xf[:, 0:32:2], A.add, 32, hk("flb") + ["xfw"], ["p1"])
+        mms(4, 0, 256, [("id1", z[:], [kz]), ("idn", T.yw[:], ["yw"])])
+        act(zo[:], ps[4][:, 0:256], AF.Abs, 256, ["ps4"], [kzo])
+        ts(T.kk[:], T.uu[:], 1023, None, A.bitwise_and, None, 16, hk("uu"), ["kk"])
+        ts(T.k2[:], T.kk[:], 2.0, 33.0, A.mult, A.add, 16, ["kk"], ["k2"])
+        for h in range(NH):
+            tt(T.q1[:, LH * h:LH * h + LH], T.k2[:, QH * h:QH * h + QH].indirect(T.tile[:, 0:QH]), nf[:, LH * h:LH * h + LH], A.mult, GA * LH, ["k2", "tile", kn], ["q1%d" % h])
+        tt(T.q2[:], T.q1[:], T.k37[:], A.add, 512, hk("q1") + ["k37"], ["q2"])
+        ts(T.ni[:], T.q2[:], 5, 4095, A.arith_shift_right, A.bitwise_and, 256, ["q2"], ["ni"])
+        if not last:
+            oo = T["offo%d" % t]
+            cp(oo[:], T.ni[:], 256, ["ni"], ["offo%d" % t])
+
+            def send(t=t, oo=oo, zo=zo):
+                sem = T.sem["arr%d" % (t + 1)]
+                return g.remote_dma_fused([
+                    RemoteDMATransfer(dst_ids=[nxt], dma_engine_mask=mk[0], remote_sem=sem, src=oo[:], dst=T["off%d" % (t + 1)][:]),
+                    RemoteDMATransfer(dst_ids=[nxt], dma_engine_mask=mk[1], remote_sem=sem, src=zo[:], dst=T["z%d" % (t + 1)][:])],
+                    local_sem=T.sem.sent)
+            op("G", send, 1000, ["offo%d" % t, kzo], ["sent%d" % t], lat=5000, kind="r")
+        else:
+            dma(T.yz[:], zo[:], 65536, [kzo], ["yz"])
+            cp(T.nfn[:], T.ni[:].indirect(T.prm[:, 32:48]), GA * 256, ["ni", "prm3"], ["nfn"])
+        if OPT["tz"]:
+            mms(5, 0, 256, [("id1", z[:], [kz]), ("idn", T.yw[:], ["yw"]), ("id256", T.fr[:], ["fr"])])
+            act(T.tz[:], ps[5][:, 0:256], AF.Relu, 256, ["ps5"], ["tz"], bias=16.0)
+        else:
+            tt(T.tz[:], ps[4][:, 0:256], T.nfl[:], A.mult, 256, ["ps4", "nfl"], ["tz"])
+        act(T.ew[:], win(OE2, 3).indirect(T.wl[:]), AF.Identity, GA * 512, tk("E2", "G1", "E1") + hk("wl") + ["wl2"], ["ew"])
+        act(T.wqw[:], T.ew[:], AF.Identity, 512, ["ew"], ["wqw"], bias=RND)
+
+        def two(bank, terms):
+            for h in range(2):
+                mms(bank, 256 * h, 256, terms(h, slice(256 * h, 256 * h + 256)))
+        if not last:
+            two(5, lambda h, s: [("id1", z[:], [kz]), ("idm16", T.fr[:], ["fr"])] if h == 0 else [("id1", T.g2w[:], hk("g2w")), ("id40", T.nfl[:], ["nfl"])])
+            act(T.s1[:], ps[5][:], AF.Relu, 512, ["ps5"], ["s1"])
+        two(4, lambda h, s: [("id1", T.ew[:, s], ["ew"]), ("idn", T.wqw[:, s], ["wqw"]), ("idn", z[:], [kz])])
+        act(T.s2[:], ps[4][:], AF.Square, 512, ["ps4"], ["s2"], bias=3072.0)
+        two(5, lambda h, s: [("id1", T.s2[:, s], ["s2"]), ("id256", T.fr[:], ["fr"])])
+        if OPT["ne"]:
+            act(T.ne[:], ps[5][:], AF.Sign, 512, ["ps5"], ["ne"])
+            two(4, lambda h, s: [("id1", T.wqw[:, s], ["wqw"]), ("idp16", T.ne[:, s], ["ne"]), ("idp16", T.fr[:], ["fr"])])
+        else:
+            ts(T.ne[:], ps[5][:], 0.0, 16.0, A.is_gt, A.mult, 512, ["ps5"], ["ne"])
+            mms(4, 0, 512, [("id1", T.wqw[:], ["wqw"]), ("id1", T.ne[:], ["ne"])])
+        if OPT["wn"]:
+            act(T.wr2[:], ps[4][:], AF.Relu, 512, ["ps4"], ["wr2"], bias=3312.0, scale=-1.0)
+            act(T.wn[:], T.wr2[:], AF.Identity, 512, ["wr2"], ["wn"], bias=240.0, scale=-1.0)
+        else:
+            ts(T.wn[:], ps[4][:], -3072.0, 240.0, A.add, A.min, 512, ["ps4"], ["wn"])
+        two(5, lambda h, s: [("id16", T.wn[:, s], ["wn"]), ("id20", T.fr[:], ["fr"])])
+        act(T.rl[:], ps[5][:, 0:256], AF.Relu, 256, ["ps5"], ["rl"], scale=16.0)
+        if not last:
+            act(T.ex[:], ps[5][:], AF.Exp, 512, ["ps5"], ["ex"], bias=-67 * LN2, scale=7 * LN2)
+            tt(T.gn[:], ps[5][:], T.ex[:], A.max, 512, ["ps5", "ex"], ["gn"])
+        two(4, lambda h, s: [("id1", T.yw[:], ["yw"]), ("id1", T.tz[:], ["tz"])] + ([("idm16", T.nfl[:], ["nfl"])] if OPT["tz"] else []) +
+            [("id1", T.rl[:], ["rl"]) if h == 0 else ("id1", T.wn[:, s], ["wn"])])
+        act(T.ee[:], ps[4][:], AF.Identity, 512, ["ps4"], ["ee"])
+        if last:
+            turn(T.nfn[:], "nfn", 5, T.yno[:], "yno")
+            dma(T.yn[:], T.yno[:], 131072, ["yno"], ["yn"])
+        for j in range(4):
+            h = j * NH // 4
+            sh = str(h)
+            rb = 6 if h < NH - 1 else 0
+            kv = str(h) if NH == 2 else str(min(j, 1))
+            for s, o, n, x, kx in ((0, OG2, "G2", T.g1w, "g1w"), (1, OG1, "G1", T.g2w, "g2w")):
+                for e in range(2):
+                    u = 2 * (2 * j + s) + e
+                    a1, cc = 512 * u, 64 * j + 32 * e
+                    mkeys = ["mm%d.%d" % (u, v) for v in range(MB)]
+                    if u in OPT["vc"][t]:
+                        for v in range(MB):
+                            tt(T.mm[:, a1 + LH * v:a1 + LH * v + LH], win(o).indirect(T.co[:, cc + QH * v:cc + QH * v + QH]), x[:, LH * h:LH * h + LH], A.min, GA * LH,
+                               tk(n) + ["co" + kv, kx + sh], [mkeys[v]])
+                    else:
+                        act(T.gb[:, a1:a1 + 512], win(o).indirect(T.co[:, cc:cc + 32]), AF.Identity, GA * 512, tk(n) + ["co" + kv], ["gb%d" % u])
+                        tt(T.mm[:, a1:a1 + 512], ps[rb + s][:], T.gb[:, a1:a1 + 512], A.min, 512, [pk(rb + s), "gb%d" % u], mkeys)
+            b = 2 + j % 2
+            kb = pk(b)
+            if lim == 11:
+                mm(ps[b][:, 0:64], T.idf[:], T.cf[:, 64 * j:64 * j + 64], True, False, 64, ["idf", "cf" + kv], [kb], 4)
+            for s in range(2):
+                a0 = 1024 * (2 * j + s)
+                mkeys = ["mm%d.%d" % (2 * (2 * j + s) + e, v) for e in range(2) for v in range(MB)]
+                for r in range(16):
+                    mm(ps[b][:, 0:64], T.zp[:, 15 - r:143 - r], T.mm[:, a0 + r:a0 + 1024:16], lim != 11 and s == 0 and r == 0, s == 1 and r == 15, 64, ["zp"] + mkeys, [kb])
+            fo = (T.kj[:, QH * h:QH * h + QH], "kj" + sh, (sm("dk", QH * h, QH * h + QH), "dk" + sh))
+            if lim == 11:
+                fold(2 + h, j - 4 // NH * h, ps[b], 64, kb, *fo)
+            else:
+                x = ps[b][:, 0:64]
+                ts(T.d1[:], x, 1.5 * 2.0 ** 46, None, A.add, None, 64, [kb], ["d1"])
+                if lim == 13:
+                    ts(T.d2[:], x, 1.5 * 2.0 ** 53, None, A.add, None, 64, [kb], ["d2"])
+                ts(T.d1[:], T.d1[:], -1.5 * 2.0 ** 46, -1013.0 / 1024, A.add, A.mult, 64, ["d1"], ["d1"])
+                if lim == 13:
+                    ts(T.d2[:], T.d2[:], -1.5 * 2.0 ** 53, -1396.0 / 131072, A.add, A.mult, 64, ["d2"], ["d2"])
+                tt(T.d1[:], x, T.d1[:], A.add, 64, [kb, "d1"], ["d1"])
+                if lim == 13:
+                    tt(T.d1[:], T.d1[:], T.d2[:], A.add, 128, ["d1", "d2"], ["d1"])
+                tt(T.kc[:], T.d1[:], T.ci[:, 64 * j:64 * j + 64], A.add, 128, ["d1", "ci" + kv], ["kc"])
+                fold(2 + h, j - 4 // NH * h, T.kc, 128, "kc", *fo)
+        ts(T.ce[:], T.kj[:], 8191, None, A.bitwise_and, None, 16, hk("kj"), ["ce"])
+        cl = T.cl[:, 0:16]
+        cp(T.xf[:, 1:32:2], T.ce[:], 16, ["ce"], ["xfc"])
+        cp(T.il[:], T.xf[:], 32, ["xfw", "xfc"], ["il"])
+        cp(T.rr[:], io[:].indirect(T.il[:]), GA * 512, ["io0", "io1", "il"], ["rr"])
+        cp(cl, T.ce[:], 16, ["ce"], ["cl"])
+        ts(T.cl[:, 16:32], T.ce[:], float(2 * TS), None, A.add, None, 16, ["ce"], ["cl2"])
+        act(T.wqc[:], win(OE2, 3).indirect(T.cl[:]), AF.Identity, GA * 512, tk("E2", "G1", "E1") + ["cl", "cl2"], ["wqc"], bias=RND)
+        act(T.yc[:], win(OY).indirect(cl), AF.Identity, GA * 256, tk("Y") + ["cl"], ["yc"])
+        act(T.w2c[:], T.wqc[:, 0:256], AF.Identity, 256, ["wqc"], ["w2c"], bias=-3072.0)
+        if not last:
+            act(T.g2c[:], win(OG2).indirect(cl), AF.Identity, GA * 256, tk("G2") + ["cl"], ["g2c"])
+        mms(1, 0, 256, [("id1", T.wqc[:, 256:512], ["wqc"]), ("id1", T.yc[:], ["yc"])] + ([] if last else [("id1", T.gn[:, 256:512], ["gn"])]))
+        act(T.s3[:], ps[1][:, 0:256], AF.Identity, 256, ["ps1"], ["s3"], bias=-3072.0)
+        mm(ps[0][:], C["idn"], T.th[:], True, False, 512, ["idn", "th"], ["ps0"])
+        mm(ps[0][:], C["idn"], T.c4[:], False, False, 512, ["idn", "c4"], ["ps0"])
+        for i in range(32):
+            q = i // 2
+            n = 512 - 32 * q
+            e = T.eb[:, 512 * (i % 4):512 * (i % 4) + n]
+            ts(e, T.rr[:, 32 * q:512], T.xf[:, i:i + 1], 2.0 ** (90 - 12 * q), A.is_equal, A.mult, n / 2, ["rr", "xfw", "xfc"], ["eb%d" % (i % 4)])
+            mm(ps[0][:, 32 * q:512], C["bw"], e, False, i == 31, n, ["bw", "eb%d" % (i % 4)], ["ps0"])
+        if not last:
+            ts(sm("b1"), T.ce[:], float(TS), None, A.add, None, 16, ["ce"], ["b1"])
+            tt(T.bb[:, 0:16], sm("b1"), sm("p1"), A.min, 32, ["b1", "p1"], ["bba"])
+        ts(sm("b2"), T.kj[:], -385.0 * 8192, None, A.add, None, 16, hk("kj"), ["b2"])
+        tt(T.bb[:, 16:32], sm("b2"), T.xf[:, 0:32:2], A.max, 32, ["b2", "xfw"], ["bbb"])
+        cp(T.bb[:, 32:48], T.ce[:], 16, ["ce"], ["bbc"])
+        op("V", lambda: V.tensor_tensor_scan(T.sc[:], T.keep[:], ps[0][:], 0.0, A.mult, A.max), vc(512), ["keep", "ps0"], ["sc"])
+        lo = 16 if last else 0
+        ts(T.hm[:, lo:48], T.sc[:].indirect(T.hitl[:, 0:(48 - lo) // 16]), 0.0, 30000.0, A.is_gt, A.mult, 100, ["sc", "hitl"], ["hm"])
+        tt(T.o1[:, lo:48], T.hm[:, lo:48], T.bb[:, lo:48], A.max, 96, ["hm", "bba", "bbb", "bbc"], ["o1"])
+        tt(T.o2[:, lo:48], T.o1[:, lo:48], T.d3[:, lo:48], A.min, 96, ["o1", "d30", "d31", "d32"], ["o2"])
+        cp(T.ol[:, lo:48], T.o2[:, lo:48], 48, ["o2"], ["ol"])
+        l1, l2, l4 = T.ol[:, 0:16], T.ol[:, 16:32], T.ol[:, 32:48]
+        n = SCA * 256
+        if not last:
+            tt(win(OY, 2).indirect(l1), T.s1[:, 0:256], T.s1[:, 256:512], A.add, n, ["ol", "s1"], tk("Y", "G2"))
+            tt(win(OG2).indirect(l2), T.g2c[:], T.gn[:, 0:256], A.add, n, ["ol", "g2c", "gn"], tk("G2"))
+            cp(win(OG1, 2).indirect(l1), T.s3[:], n, ["ol", "s3"], tk("G1", "E1"))
+        tt(win(OE2).indirect(l2), T.w2c[:], T.ee[:, 0:256], A.add, n, ["ol", "w2c", "ee"], tk("E2"))
+        tt(win(OE2).indirect(l4), T.wn[:, 0:256], T.yc[:], A.add, n, ["ol", "wn", "yc"], tk("E2"))
+        cp(win(OE1).indirect(l2), T.ee[:, 256:512], n, ["ol", "ee"], tk("E1"))
+        if last:
+            cp(win(OE1).indirect(l4), T.s3[:], n, ["ol", "s3"], tk("E1"))
+        else:
+            ts(sm("has"), T.ce[:], float(NM), None, A.is_lt, None, 16, ["ce"], ["has"])
+            tt(T.exf[:], sm("has"), T.hm[:, 0:16], A.is_gt, 32, ["has", "hm"], ["exf"])
+            mms(4, 0, 16, [("ones", T.exf[:], ["exf"])])
+            op("V", lambda: V.tensor_reduce(T.ac[:, 0:1], ps[4][:, 0:16], AxisListType.X, A.add), vc(16), ["ps4"], ["ac0"])
+            ts(T.ac[:, 1:2], T.ac[:, 0:1], -0.375, None, A.add, None, 1, ["ac0"], ["ac1"])
+    dma(T.ys[:], tb[:, OE2:OE2 + NM], 1 << 20, tk("E2"), ["ys"])
+    mms(4, 0, 64, [("id1", tb[:, OE1 + 64 * j:OE1 + 64 * j + 64], tk("E1")) for j in range(64)])
+    act(T.yfo[:], ps[4][:, 0:64], AF.Identity, 64, ["ps4"], ["yfo"])
+    dma(T.yf[:], T.yfo[:], 32768, ["yfo"], ["yf"])
+    return ops
+
+
+def depend(ops):
+    lw, rd = {}, {}
+    for i, o in enumerate(ops):
+        raw, oth = set(), set()
+        for k in o["r"]:
+            if k in lw:
+                raw.add(lw[k])
+        for k in o["w"]:
+            if k in lw:
+                oth.add(lw[k])
+            oth.update(rd.get(k, ()))
+        for k in o["r"]:
+            if k.startswith("ps"):
+                oth.update(j for j in rd.get(k, ()) if ops[j]["e"] != o["e"])
+        for k in o["r"]:
+            rd.setdefault(k, []).append(i)
+        for k in o["w"]:
+            lw[k] = i
+            rd[k] = []
+        oth.discard(i)
+        o["raw"], o["dep"] = raw, raw | oth
+
+
+def schedule(ops):
+    n = len(ops)
+    fw = [[] for _ in ops]
+    bw = [[] for _ in ops]
+    for j, o in enumerate(ops):
+        for i in sorted(o["dep"]):
+            e = ops[i]["e"]
+            same = o["e"] == e and ops[i]["k"] == "c" and e == "P"
+            d = ops[i]["lat"] + (0 if same else OPT["hop"])
+            fw[i].append((j, d))
+            bw[j].append((i, d))
+    cost = [o["c"] for o in ops]
+    eng = [o["e"] for o in ops]
+    up = [1e9 - 1e6 * i if o["k"] == "d" and not o["r"] else OPT["boost"] if o["w"][0] in BOOST else 0.0 for i, o in enumerate(ops)]
+
+    def sweep(succ, pred, pr, rdy, look):
+        left = [len(p) for p in pred]
+        free = {e: 0.0 for e in eng}
+        cand = {e: set() for e in free}
+        for i in range(n):
+            if left[i] == 0:
+                cand[eng[i]].add(i)
+        order, t0 = [], [0.0] * n
+        for _ in range(n):
+            e, first = min(((e, min(max(rdy[i], free[e]) for i in c)) for e, c in cand.items() if c), key=lambda x: (x[1], str(x[0])))
+            i = max((i for i in cand[e] if rdy[i] <= first + look), key=lambda i: (pr[i] - OPT["lam"] * max(0.0, rdy[i] - first), -i))
+            cand[e].discard(i)
+            t0[i] = max(rdy[i], free[e])
+            fin = t0[i] + cost[i]
+            if e is not None:
+                free[e] = fin
+            order.append(i)
+            for j, d in succ[i]:
+                rdy[j] = max(rdy[j], fin + d)
+                left[j] -= 1
+                if left[j] == 0:
+                    cand[eng[j]].add(j)
+        return order, t0
+    pr = [0.0] * n
+    for i in range(n - 1, -1, -1):
+        pr[i] = cost[i] + max([pr[j] + d for j, d in fw[i]], default=ops[i]["lat"])
+    rng = np.random.default_rng(OPT["seed"])
+    best = None
+    for it in range(OPT["iters"] + 1):
+        order, t0 = sweep(fw, bw, [pr[i] + up[i] for i in range(n)], [0.0] * n, OPT["look"])
+        end = max(t0[i] + cost[i] + ops[i]["lat"] for i in range(n))
+        if best is None or end <= best[0]:
+            best = (end, order, t0)
+        nz = (rng.random(n) - 0.5) * OPT["noise"] * (rng.random(n) < OPT["frac"])
+        t0 = best[2]
+        _, b0 = sweep(bw, fw, [t0[i] + cost[i] + float(nz[i]) for i in range(n)], [0.0 if fw[i] else ops[i]["lat"] for i in range(n)], OPT["look"])
+        pr = [b0[i] + cost[i] for i in range(n)]
+    INFO["end"] = best[0]
+    for i, o in enumerate(ops):
+        o["t0"] = best[2][i]
+    return best[1]
+
+
+def rank_program(g, core, T, topo):
+    rank = T.rank_of(core)
+    if rank is None:
+        return
+    cores = list(T.cores)
+    to = cores[(rank + 1) % len(cores)]
+    fro = cores[(rank - 1) % len(cores)]
+    assert topo.may_write(core, to)
+    ad = topo.addr(to)
+    en = topo.engines(core, to)
+    hf = len(en) // 2
+    mk = [sum(1 << e for e in en[:hf]), sum(1 << e for e in en[hf:])]
+    nin = len(topo.engines(fro, core))
+    ops = build(g, T, DstId(rid=ad[0], pnc=ad[1]), mk)
+    depend(ops)
+    if "order" not in INFO:
+        INFO["order"] = schedule(ops)
+    order = INFO["order"]
+    queue = {"V": g.vector, "S": g.scalar, "P": g.tensor, "G": g, "Y": g.sync}
+    pos = {i: p for p, i in enumerate(order)}
+    need = {}
+    known = {e: {} for e in queue}
+    clock = {}
+    for i in order:
+        o = ops[i]
+        if o["k"] == "x":
+            clock[i] = {i: 0}
+            continue
+        best = {}
+        for j in o["dep"]:
+            d = ops[j]
+            if d["k"] == "r":
+                continue
+            if d["k"] != "c":
+                best[j] = (0, j)
+            elif d["e"] == o["e"] and o["k"] == "c" and o["e"] == "P":
+                continue
+            elif pos[j] > best.get(d["e"], (-1, 0))[0]:
+                best[d["e"]] = (pos[j], j)
+        kn = known[o["e"]]
+        ws = []
+        for e, (p, j) in sorted(best.items(), key=lambda x: -pos[x[1][1]]):
+            if p > kn.get(e, -1):
+                ws.append(j)
+                for k, v in clock[j].items():
+                    if v > kn.get(k, -1):
+                        kn[k] = v
+        need[i] = ws
+        clock[i] = dict(kn)
+        if o["k"] == "c":
+            clock[i][o["e"]] = pos[i]
+        else:
+            clock[i][i] = 0
+    wanted = set(j for ws in need.values() for j in ws)
+    cnt = {}
+    tok = {}
+    nd = 0
+    outs = []
+    for i in order:
+        o = ops[i]
+        if o["k"] == "x":
+            tok[i] = (T.sem[o["fn"]], nin)
+            continue
+        q = queue[o["e"]]
+        for j in need[i]:
+            q.wait_ge(tok[j][0], tok[j][1])
+        ins = o["fn"]()
+        if o["k"] == "d":
+            tok[i] = (T.sem["d%d" % nd], 16)
+            nd += 1
+            ins.then_inc(tok[i][0], 16)
+            if i not in wanted:
+                outs.append(i)
+        elif o["k"] == "c" and i in wanted:
+            cnt[o["e"]] = cnt.get(o["e"], 0) + 1
+            tok[i] = (T.sem["e" + o["e"]], cnt[o["e"]])
+            ins.then_inc(tok[i][0], 1)
+    for i in outs:
+        g.sync.wait_ge(tok[i][0], 16)
+    g.wait_ge(T.sem.sent, (NV - 1) * len(en))

@@ -7,42 +7,55 @@ NM, LN, NV = 4096, 256, 3
 LIMS = (13, 11, 12)
 WT = (1, 16, 256, 37, 411, 93, 777, 165, 1029, 251, 1313, 339, 1583, 503, 1847, 618)
 KA = (3, 61, 118, 207, 346, 419, 530, 677, 742, 895, 1011, 1164, 1283, 1450, 1629, 1874)
-TS = NM + 2 * LN
+TS = NM + 3 * LN
 OY, OG2, OE2, OG1, OE1 = 0, TS, 2 * TS, 3 * TS, 4 * TS
 LN2 = math.log(2.0)
-RND = 3064.5
-PIECES = (512, 512, 1024, 1024, 1024)
-OPT = {"nh": 2, "va": ((0, 1, 4, 5), (0, 4), (0, 4)), "vc": ((0, 8), (0, 8), (0, 8)), "wbs": 1, "ne": 1, "wn": 1, "tz": 1,
-       "seed": 0, "noise": 3000.0, "iters": 150, "look": 300.0, "lam": 20.0, "frac": 0.1, "boost": 2000.0, "ga": 1.56, "sca": 3.8, "hop": 110.0}
-BOOST = ("cl", "cl2", "fr", "gn", "ne", "wn", "tz", "wl2")
+W0 = 2880.0
+RND = W0 - 7.5
+X11, C11, C12 = 8000.0, W0 + 8192, 8192000.0
+EA = math.log(1024.0) / 16
+EB = math.log(X11) - EA * (W0 + 176)
+GLIM = {11: 51500.0, 12: 1e6, 13: 1e9}
+BIG = 2.0 ** 59
+OPT = {"pieces": (512, 1024, 1024, 1024, 256, 256), "ch": (512,) * 7 + (256, 256), "split": (1, 2, 1), "vz": ("Y",),
+       "nh": 1, "uv": 0, "ww": 12, "sb": (0, 1, 6, 7, 0, 1, 6, 7), "cut": ((0, 64), (64, 256)), "big": (2, 4, 6, 8, 10, 12),
+       "bk": {"sg": 0, "zo": 1, "tz": 1, "s1": 0, "s2": 4, "ne": 1, "wr2": 4, "rl": 0, "gn": 1, "nd": 4, "w2c": 6, "s3": 7, "cm": 5, "yn": 0},
+       "va": ((2, 3, 4), (0, 4), (0, 4)), "vr": ((0,), (1,), (1,)), "vc": ((0, 4, 8, 12), (0, 4, 8, 12), (0, 4, 8, 12)), "gv": (),
+       "seed": 0, "noise": 3000.0, "iters": 2, "moves": 40000, "temp": 40.0, "look": 300.0, "lam": 20.0, "frac": 0.1, "boost": 2000.0, "ga": 1.56, "sca": 3.8, "hop": 170.0, "xhop": 170.0,
+       "mul": {"G": 1.3, "P": 1.1}, "rl": (11000, 8000)}
+BOOST = ("cl", "cl2", "gn", "ne", "wn", "tz", "wl2")
 
 B, F, I, U, H = "bfloat16", "float32", "int32", "uint16", "float16"
+IDS = (("idn", -1.0), ("idp16", 16.0), ("idm128", -128.0), ("id8", 8.0), ("idH", BIG), ("idmH", -BIG))
 SB = {
-    "tb": (5 * TS, B), "io32": (TS, F), "wq": (2048, B), "wb": (8192, B), "sel": (1024, B), "tt": (1024, B),
-    "ab": (4096, B), "ga": (4096, B), "gb": (8192, B), "mm": (8192, B), "xx": (2048, F), "eb": (2048, B),
+    "tb": (5 * TS, B), "io32": (TS, F), "wq": (8192, B), "rq": (1024, B), "tt": (1024, B),
+    "ab": (4096, B), "ga": (4096, B), "gb": (8192, B), "mm": (8192, B), "eb": (8704, B),
     "pi": (1, I), "pj": (4, I), "pf": (16, F), "rd": (128, I), "wr": (16, F), "rr": (512, U), "il": (32, U),
-    "ids": (1408, B), "sm": (144, F), "idf": (128, F), "zp": (144, B), "zn": (144, B), "zw": (144, H),
-    "i16": (16, F), "m8": (8, F), "tile": (16, U), "prm": (48, U), "hitl": (4, U), "d3": (48, F), "pc2": (16, F),
+    "ids": (128 * (len(IDS) + 3), B), "cst": (192, B), "sm": (192, F), "idf": (128, F), "psw": (128, F),
+    "zp": (144, B), "zn": (144, B), "z2": (144, B), "zq": (144, B), "zw": (144, H),
+    "i16": (16, F), "tile": (16, U), "prm": (48, U), "hitl": (4, U), "d3": (48, F), "pc2": (80, F),
     "k37": (256, F), "ka": (256, F), "th": (512, B), "keep": (512, B), "c1": (512, F), "c2": (512, F), "c3": (512, B), "c4": (512, B),
-    "nmi": (256, I), "npf": (256, F), "t1f": (256, F),
-    "off0": (256, U), "off1": (256, U), "off2": (256, U), "z0": (256, B), "z1": (256, B), "z2": (256, B),
+    "nmi": (256, I), "tw": (512, F), "t1f": (256, F), "t2f": (256, F),
+    "off0": (256, U), "off1": (256, U), "off2": (256, U), "z0": (256, B), "z1": (256, B), "z2x": (256, B),
     "offo0": (256, U), "offo1": (256, U), "zo0": (256, B), "zo1": (256, B), "zo2": (256, B), "nf0": (256, F), "nf1": (256, F), "nf2": (256, F),
     "run": (256, F), "r64": (256, F), "r32": (192, F), "ki": (16, I), "wi": (16, I), "wl": (32, U), "xf": (32, F),
-    "yh": (256, H), "yw": (256, B), "g1w": (256, B), "g2w": (256, B), "ui": (16, I), "uu": (16, I), "aa": (16, I),
-    "ca": (256, F), "cb": (256, I), "ci": (256, I), "co": (256, U), "cf": (256, F), "d1": (64, F), "d2": (64, F), "kc": (64, F),
-    "mg": (256, B), "fr": (256, B), "nfl": (256, B), "tz": (256, B), "ew": (512, B), "wqw": (512, B), "s2": (512, B), "ne": (512, B),
-    "wn": (512, B), "wr2": (512, B), "ex": (512, B), "gn": (512, B), "rl": (256, B), "ee": (512, B), "s1": (512, B),
+    "yw": (256, B), "g1w": (256, B), "g2w": (256, B), "hu": (32, B), "aa": (16, I),
+    "ca": (256, F), "cb": (256, I), "ci": (256, I), "co": (256, U), "n1": (256, B), "n2": (256, B), "n3": (256, B), "n4": (256, F), "ui": (16, I), "uu": (16, I), "kc": (256, F),
+    "mg": (256, B), "sg": (256, B), "tz": (256, B), "ew": (512, B), "wqw": (512, B), "s2": (512, B), "ne": (512, B),
+    "wn": (512, B), "wr2": (512, B), "ex": (512, B), "gn": (512, B), "rl": (256, B), "nd": (256, B), "s1": (512, B),
     "kj": (16, I), "ce": (16, I), "cl": (32, U), "bb": (48, F),
-    "g2c": (256, B), "wqc": (512, B), "w2c": (256, B), "yc": (256, B), "s3": (256, B),
+    "g2c": (256, B), "wqc": (512, B), "wx": (1024, B), "nx": (512, B), "s3": (256, B), "sn": (512, B),
     "sc": (512, B), "hm": (48, F), "o1": (48, F), "o2": (48, F), "ol": (48, U), "exf": (16, B), "ac": (2, F),
-    "kk": (16, I), "k2": (16, F), "q1": (256, F), "q2": (256, I), "ni": (256, I), "nfn": (256, F), "yno": (256, F), "yfo": (64, F),
+    "q1": (256, F), "q2": (256, I), "ni": (256, I), "yno": (256, F), "yfo": (64, F),
 }
-SMALL = ("has", "b1", "b2", "p1", "dk", "flb", "sq", "dz", "dum")
-IDS = (("id1", 1.0), ("idn", -1.0), ("id16", 0.0625), ("id20", -20.0), ("id256", -256.0), ("idm16", -16.0), ("id40", -2.0 ** 40), ("idp16", 16.0))
+SMALL = ("b1", "b2", "p1", "dk", "flb", "sq", "dz", "u0", "dum", "uf", "k2")
 SCRATCH = {n: ("sbuf", [128, w], d) for n, (w, d) in SB.items()}
+SCRATCH["rr"] = ("sbuf", [128, 2, 256], U)
+SCRATCH["eb"] = ("sbuf", [128, 2, 4352], B)
 for _b in range(8):
     SCRATCH["ps%d" % _b] = ("psum", [128, 512], F)
-SEMAPHORES = ["eV", "eS", "eP", "eG", "arr1", "arr2", "sent"] + ["d%d" % _i for _i in range(20)]
+SCRATCH["ps5"] = ("psum", [128, 16, 2, 16], F)
+SEMAPHORES = ["eV", "eS", "eP", "eG", "arr1", "arr2", "sent"] + ["d%d" % _i for _i in range(24)]
 INFO = {}
 
 
@@ -50,7 +63,7 @@ def build(g, T, nxt, mk):
     ops = []
     V, S, P = g.vector, g.scalar, g.tensor
     GA, SCA, NH = OPT["ga"], OPT["sca"], OPT["nh"]
-    QH, LH = 16 // NH, LN // NH
+    QH, LH, MB = 16 // NH, LN // NH, 2 * NH
 
     def op(e, fn, cost, r, w, lat=0.0, kind="c"):
         ops.append({"e": e, "fn": fn, "c": cost, "r": list(r), "w": list(w), "lat": lat, "k": kind})
@@ -70,15 +83,27 @@ def build(g, T, nxt, mk):
     def cp(o, i, n, r, w):
         op("V", lambda: V.tensor_copy(o, i), vc(n), r, w)
 
-    def act(o, i, f, n, r, w, bias=0.0, scale=1.0):
-        op("S", lambda: S.activation(o, i, f, bias=bias, scale=scale), 70 + 0.83 * n, r, w)
+    def act(o, i, f, n, r, w, bias=0.0, scale=1.0, acc=None):
+        op("S", lambda: S.activation(o, i, f, bias=bias, scale=scale, accum_out=acc), 70 + 0.83 * n + (0 if acc is None else 140), r, w)
 
     def mm(o, l, rh, st, sp, n, r, w, k=1):
         op("P", lambda: P.matmul(o, l, rh, st, sp), 8 + 0.42 * k * max(64, n), r, w)
 
-    def mms(b, x0, n, terms):
+    def mmx(calls, n, r, w):
+        op("P", lambda: [P.matmul(*c) for c in calls][-1], len(calls) * (8 + 0.42 * max(64, n)), r, w)
+
+    def mma(left, calls, n, r, w, k=1):
+        left[0] += 1
+
+        def fn():
+            left[0] -= 1
+            return [P.matmul(c[0], c[1], c[2], False, left[0] == 0 and j == len(calls) - 1) for j, c in enumerate(calls)][-1]
+        op("P", fn, len(calls) * (8 + 0.42 * k * max(64, n)), r, w)
+        ops[-1]["acc"] = 1
+
+    def mms(b, x0, n, terms, st=True, sp=True):
         for j, (l, rh, r) in enumerate(terms):
-            mm(ps[b][:, x0:x0 + n], C[l], rh, j == 0, j == len(terms) - 1, n, r + [l], [pk(b)])
+            mm(ps[b][:, x0:x0 + n], C[l], rh, st and j == 0, sp and j == len(terms) - 1, n, r + [l], [pk(b)])
 
     def dma(o, i, nbytes, r, w, e="Y"):
         op(e, lambda: (S if e == "S" else g.sync).dma_start(o, i), 60, r, w, lat=1800 + nbytes / 150.0, kind="d")
@@ -87,8 +112,10 @@ def build(g, T, nxt, mk):
         op("G", lambda: g.iota(o, pat, base, cm, allow_small_or_imprecise_dtypes=True), 130 + 1.66 * n, [], w)
 
     tb, io, pf = T.tb, T.io32, T.pf
-    C = {n: T.ids[:, 128 * j:128 * j + 128] for j, n in enumerate([x[0] for x in IDS] + ["bone", "bw", "ones"])}
+    C = {n: T.ids[:, 128 * j:128 * j + 128] for j, n in enumerate([x[0] for x in IDS] + ["id1", "bone", "bw"])}
+    C["ones"] = T.c3[:, 0:128]
     ps = [T["ps%d" % b] for b in range(8)]
+    one = (T.c3[:, 0:256], ["ones"])
 
     def sm(n, a=0, b=16):
         j = 16 * SMALL.index(n)
@@ -101,146 +128,175 @@ def build(g, T, nxt, mk):
         return tb[:, o:o + n * TS]
 
     def tk(*ns):
-        return ["%s.%d" % (n, k) for n in ns for k in range(9)]
+        return ["%s.%s" % (n, k) for n in ns for k in list(range(len(CH))) + ["z"]]
+
+    CH = OPT["ch"]
+    CO = [sum(CH[:k]) for k in range(len(CH) + 1)]
+
+    def ck(n, a, b):
+        return ["%s.%d" % (n, k) for k in range(len(CH)) if CO[k] < b and CO[k + 1] > a]
 
     def hk(n):
         return ["%s%d" % (n, h) for h in range(NH)]
 
     dma(T.nmi[:], T.nm[:], 131072, [], ["nmi"])
     c0 = 0
-    for j, wd in enumerate(PIECES):
-        ks = range(c0 // 512, (c0 + wd) // 512)
-        dma(tb[:, OE2 + c0:OE2 + c0 + wd], T.pg[:, NM + c0:NM + c0 + wd], 256 * (2 * c0 + wd), [], ["E2.%d" % k for k in ks])
-        dma(tb[:, OE1 + c0:OE1 + c0 + wd], T.pg[:, c0:c0 + wd], 256 * (2 * c0 + 2 * wd), [], ["E1.%d" % k for k in ks], "S")
+    for j, wd in enumerate(OPT["pieces"]):
+        dma(tb[:, OE2 + c0:OE2 + c0 + wd], T.pg[:, NM + c0:NM + c0 + wd], 256 * (2 * c0 + wd), [], ck("E2", c0, c0 + wd))
+        dma(tb[:, OE1 + c0:OE1 + c0 + wd], T.pg[:, c0:c0 + wd], 256 * (2 * c0 + 2 * wd), [], ck("E1", c0, c0 + wd), "S")
         if j == 1:
             dma(T.z0[:], T.zv[:], 256 * 2048, [], ["z0"])
         c0 += wd
 
     op("G", lambda: g.iota(T.pi[:], [[0, 1]], 0, 1), 135, [], ["pi"])
     iota(io[:, 0:256], [[1, 256]], 0, 0, 256, ["io0"])
-    iota(T.pc2[:], [[128, 2], [2, 8]] if NH == 2 else [[1, 16]], 0, 0, 16, ["pc2"])
+    iota(T.c3[:], [[0, 512]], 1, 0, 512, ["ones"])
+    iota(T.pc2[:, 0:16], [[128, 2], [2, 8]] if NH == 2 else [[1, 16]], 0, 0, 16, ["pc2"])
+    iota(T.pc2[:, 16:32], [[32, 8], [256, 2]], 0, 0, 16, ["pc3"])
+    iota(T.pc2[:, 32:48], [[0, 8], [1, 2]], 0, 0, 16, ["pc4"])
     iota(T.c1[:], [[-48, 16], [0, 2], [-3, 16]], 0, 0, 512, ["c1"])
     iota(T.c2[:], [[0, 32], [1, 16]], 0, 0, 512, ["c2"])
-    iota(T.c3[:], [[0, 512]], 1, 0, 512, ["c3"])
     iota(T.k37[:], [[(9472 * QH) % NM, NH], [37, 16], [9472, QH]], 0, 0, 256, ["k37"])
-    iota(io[:, 256:TS], [[1, TS - 256]], 256, 0, TS - 256, ["io1"])
+    for j in range(4):
+        iota(io[:, 256 + 1152 * j:256 + 1152 * (j + 1)], [[1, 1152]], 256 + 1152 * j, 0, 1152, ["io1%d" % j])
+    iok = ["io0"] + ["io1%d" % j for j in range(4)]
+    for j in range(16):
+        iota(T.wr[:, j:j + 1], [[0, 1]], WT[j], 0, 1, ["wr%d" % j])
+        iota(T.ka[:, QH * j:QH * j + QH], [[0, QH]], KA[j], 0, QH, ["ka%d" % j])
+    kak = ["ka%d" % j for j in range(16)]
+    iota(T.cst[:], [[0, 192]], int(32 * W0 * 512 / 128), 0, 192, ["cst"])
+    for n, o in (("Y", OY), ("G2", OG2), ("E2", OE2), ("G1", OG1), ("E1", OE1)):
+        if n in OPT["vz"]:
+            op("V", lambda o=o: V.memset(tb[:, o + NM:o + TS], 0.0), vc(384), [], [n + ".z"])
+        else:
+            iota(tb[:, o + NM:o + TS], [[0, 768]], 0, 0, 768, [n + ".z"])
     ts(T.pj[:, 0:1], T.pi[:], 15, None, A.bitwise_and, None, 1, ["pi"], ["pj0"])
     ts(T.pj[:, 1:2], T.pi[:], 4, None, A.arith_shift_right, None, 1, ["pi"], ["pj1"])
     ts(T.pj[:, 2:3], T.pi[:], QH - 1, None, A.bitwise_and, None, 1, ["pi"], ["pj2"])
-    pc, pm, pd, pq, zc, pm16, hc, kc37, rho, wc, ph, pa, pb = [pf[:, j:j + 1] for j in range(13)]
+    ts(T.pj[:, 3:4], T.pi[:], 16, None, A.bitwise_and, None, 1, ["pi"], ["pj3"])
+    pc, pm, pd, pq, px, zc, hc, kc37, rho, wc, ph, pa, pb, pe, pg_, pw = [pf[:, j:j + 1] for j in range(16)]
     cp(pc, T.pi[:], 1, ["pi"], ["pc"])
-    cp(pf[:, 1:4], T.pj[:, 0:3], 3, ["pj0", "pj1", "pj2"], ["pm"])
-    ts(zc, pd, 16.0, 15.0, A.mult, A.add, 1, ["pm"], ["zc"])
-    ts(pm16, pm, 16.0, None, A.mult, None, 1, ["pm"], ["pm16"])
-    ts(hc, pm, 32.0, 31.0, A.mult, A.add, 1, ["pm"], ["hc"])
-    ts(kc37, pm, 592.0, None, A.mult, None, 1, ["pm"], ["kc37"])
+    cp(pf[:, 1:5], T.pj[:, 0:4], 4, ["pj0", "pj1", "pj2", "pj3"], ["pm"])
+    ID = AF.Identity
+    act(zc, pd, ID, 1, ["pm"], ["zc"], bias=15.0, scale=16.0)
+    act(hc, pm, ID, 1, ["pm"], ["hc"], bias=31.0, scale=32.0)
+    act(kc37, pm, ID, 1, ["pm"], ["kc37"], scale=592.0)
     ts(ph, pm, pq, 1.0 / QH, A.subtract, A.mult, 1, ["pm"], ["ph"])
-    ts(pa, pq, 16.0, ph, A.mult, A.add, 1, ["pm", "ph"], ["pa"])
-    ts(pb, ph, 128.0, pq, A.mult, A.add, 1, ["pm", "ph"], ["pb"])
+    act(pa, pq, ID, 1, ["pm", "ph"], ["pa"], bias=ph, scale=16.0)
+    act(pb, pm, ID, 1, ["pm"], ["pb"], scale=float(QH))
+    act(pe, px, ID, 1, ["pm"], ["pe"], bias=pm, scale=17.0)
+    act(pg_, px, ID, 1, ["pm"], ["pg"], scale=-32.0)
+    act(pw, px, ID, 1, ["pm", "pc"], ["pw"], bias=pc, scale=-2.0)
     act(rho, pm, AF.Exp, 1400, ["pm"], ["rho"], scale=-0.75 * LN2)
+    ts(C["id1"], io[:, 0:128], pc, None, A.is_equal, None, 128, ["io0", "pc"], ["id1"])
     for n, s in IDS:
-        ts(C[n], io[:, 0:128], pc, s, A.is_equal, A.mult, 128, ["io0", "pc"], [n])
-    ts(T.idf[:], io[:, 0:128], pc, None, A.is_equal, None, 128, ["io0", "pc"], ["idf"])
+        act(C[n], C["id1"], ID, 128, ["id1"], [n], scale=s)
+    act(T.idf[:], C["id1"], ID, 128, ["id1"], ["idf"])
+    ts(T.psw[:], io[:, 0:128], -16.0, pw, A.add, A.is_equal, 128, ["io0", "pw"], ["psw"])
     ts(T.i16[:], io[:, 0:16], pm, None, A.is_equal, None, 16, ["io0", "pm"], ["i16"])
-    ts(T.m8[:], io[:, 0:8], pd, None, A.is_equal, None, 8, ["io0", "pm"], ["m8"])
-    ts(T.prm[:, 0:16], io[:, 0:16], pm16, None, A.add, None, 16, ["io0", "pm16"], ["prm1"])
-    ts(T.prm[:, 16:32], T.pc2[:], pa, None, A.add, None, 16, ["pc2", "pa"], ["prm2"])
-    ts(T.prm[:, 32:48], io[:, 0:16], float(QH), pb, A.mult, A.add, 16, ["io0", "pb"], ["prm3"])
-    ts(T.tile[:], io[:, 0:16], 0.0, pq, A.mult, A.add, 16, ["io0", "pm"], ["tile"])
+    act(T.pc2[:, 32:48], T.pc2[:, 32:48], ID, 16, ["pc4", "pe", "pg"], ["pc4"], bias=pe, scale=pg_)
+    tt(T.pc2[:, 16:32], T.pc2[:, 16:32], T.pc2[:, 32:48], A.add, 32, ["pc3", "pc4"], ["pc3"])
+    cp(T.prm[:, 0:16], T.pc2[:, 16:32], 16, ["pc3"], ["prm1"])
+    ts(T.prm[:, 16:32], T.pc2[:, 0:16], pa, None, A.add, None, 16, ["pc2", "pa"], ["prm2"])
+    iota(T.pc2[:, 48:64], [[128, NH], [1, QH]], 0, 0, 16, ["pc5"])
+    ts(T.prm[:, 32:48], T.pc2[:, 48:64], pb, None, A.add, None, 16, ["pc5", "pb"], ["prm3"])
+    iota(T.pc2[:, 64:80], [[8, NH], [0, QH]], 0, 0, 16, ["pc6"])
+    ts(T.tile[:], T.pc2[:, 64:80], pq, None, A.add, None, 16, ["pc6", "pm"], ["tile"])
     ts(T.hitl[:], io[:, 0:4], 0.0, hc, A.mult, A.add, 4, ["io0", "hc"], ["hitl"])
     ts(T.zp[:], io[:, 0:144], zc, 8192.0, A.is_equal, A.mult, 144, ["io0", "zc"], ["zp"])
-    ts(T.zn[:], io[:, 0:144], zc, -8192.0, A.is_equal, A.mult, 144, ["io0", "zc"], ["zn"])
-    for j in range(16):
-        act(T.wr[:, j:j + 1], io[:, 0:1], AF.Identity, 1, ["io0"], ["wr%d" % j], bias=float(WT[j]), scale=0.0)
-        act(T.ka[:, QH * j:QH * j + QH], io[:, 0:QH], AF.Identity, QH, ["io0"], ["ka%d" % j], bias=float(KA[j]), scale=0.0)
-    kak = ["ka%d" % j for j in range(16)]
+    for n, s in (("zn", -1.0), ("z2", -2.0), ("zq", 0.0625)):
+        act(T[n][:], T.zp[:], ID, 144, ["zp"], [n], scale=s)
     tt(T.wr[:], T.wr[:], T.i16[:], A.mult, 32, ["wr%d" % j for j in range(16)] + ["i16"], ["wrm"])
     op("V", lambda: V.tensor_reduce(wc, T.wr[:], AxisListType.X, A.add), vc(16), ["wrm"], ["wc"])
     ts(T.zw[:], io[:, 0:144], zc, wc, A.is_equal, A.mult, 144, ["io0", "zc", "wc"], ["zw"])
     ts(T.rd[:], io[:, 0:128], 0.0625, -0.46875, A.mult, A.add, 128, ["io0"], ["rd"])
     ts(C["bone"], T.rd[:], pd, None, A.is_equal, None, 128, ["rd", "pm"], ["bone"])
-    ts(C["bw"], T.rd[:], pd, rho, A.is_equal, A.mult, 128, ["rd", "pm", "rho"], ["bw"])
-    op("V", lambda: V.memset(C["ones"], 1.0), vc(64), [], ["ones"])
-    ts(sm("dum"), io[:, 0:16], 16.0, pm, A.mult, A.add, 16, ["io0", "pm"], ["dum"])
-    for j, x in enumerate((TS + NM, NM, NM)):
-        ts(T.d3[:, 16 * j:16 * j + 16], sm("dum"), float(x), None, A.add, None, 16, ["dum"], ["d3%d" % j])
-    ts(sm("dz"), sm("dum"), float(NM + LN - 8192), None, A.add, None, 16, ["dum"], ["dz"])
-    ts(T.k37[:], T.k37[:], kc37, 32.0, A.add, A.mult, 256, ["k37", "kc37"], ["k37"])
+    act(C["bw"], C["bone"], ID, 128, ["bone", "rho"], ["bw"], scale=rho)
+    act(sm("dum"), io[:, 0:16], ID, 16, ["io0", "pm"], ["dum"], bias=pm, scale=16.0)
+    for j, x in enumerate((TS + NM, NM, NM + LN)):
+        act(T.d3[:, 16 * j:16 * j + 16], sm("dum"), ID, 16, ["dum"], ["d3%d" % j], bias=x * 2.0 ** -15, scale=2.0 ** -15)
+    act(sm("dz"), sm("dum"), ID, 16, ["dum"], ["dz"], bias=NM + 2 * LN - 8192.0)
+    act(T.k37[:], T.k37[:], ID, 256, ["k37", "kc37"], ["k37"], bias=kc37)
+    act(T.k37[:], T.k37[:], ID, 256, ["k37"], ["k37"], scale=32.0)
     act(T.c4[:], T.c1[:], AF.Exp, 512, ["c1"], ["c4"], bias=90 * LN2 + math.log(2.57), scale=LN2 / 4)
     ts(T.th[:], T.c2[:], pm, 2.0 ** 95, A.not_equal, A.mult, 512, ["c2", "pm"], ["th"])
-    op("G", lambda: g.affine_select(T.keep[:], T.c3[:], [[0, 16], [1, 32]], A.is_gt, 0.0, 0, 0), 1020, ["c3"], ["keep"])
-    for n, o in (("Y", OY), ("G2", OG2), ("E2", OE2), ("G1", OG1), ("E1", OE1)):
-        iota(tb[:, o + NM:o + TS], [[0, 512]], 0, 0, 512, [n + ".8"])
+    op("G", lambda: g.affine_select(T.keep[:], T.c3[:], [[0, 16], [1, 32]], A.is_gt, 0.0, 0, 0), 1020, ["ones"], ["keep"])
 
-    def turn(src, ksrc, bank, dst, kdst):
-        for j in range(8):
-            o = T.xx[:, 256 * j:256 * j + 256]
-            if j % 2:
-                ts(o, src, T.m8[:, j:j + 1], None, A.mult, None, 256, [ksrc, "m8"], ["xx%d" % j])
-            else:
-                act(o, src, AF.Identity, 256, [ksrc, "m8"], ["xx%d" % j], scale=T.m8[:, j:j + 1])
-        for q in range(16):
-            mm(ps[bank][:, 16 * q:16 * q + 16], T.xx[:, q:2048:16], T.i16[:], True, True, 64, ["xx%d" % j for j in range(8)] + ["i16"], [pk(bank)], 4)
-        act(dst, ps[bank][:, 0:256], AF.Identity, 256, [pk(bank)], [kdst])
+    def swap(src, ksrc, bank, dst, kdst):
+        mm(ps[bank][:, 0:256], T.psw[:], src, True, True, 256, ["psw", ksrc], [pk(bank)], 4)
+        act(T.tw[:, 256:512], ps[bank][:, 0:256], ID, 256, [pk(bank)], ["tw1"])
+        act(dst, T.tw[:].indirect(T.prm[:, 0:16]), ID, GA * 256, [ksrc, "tw1", "prm1"], [kdst])
 
-    cp(T.npf[:], T.nmi[:].indirect(T.prm[:, 0:16]), GA * 256, ["nmi", "prm1"], ["npf"])
-    turn(T.npf[:], "npf", 7, T.t1f[:], "t1f")
-    cp(T.off0[:], T.t1f[:].indirect(T.prm[:, 16:32]), GA * 256, ["t1f", "prm2"], ["off0"])
+    def turn(o, i, r, w):
+        op("V", lambda: V.transpose(o, i), vc(256), r, w)
 
-    for k in range(8):
+    cp(T.tw[:, 0:256], T.nmi[:], 256, ["nmi"], ["tw0"])
+    swap(T.tw[:, 0:256], "tw0", 7, T.t1f[:], "t1f")
+    turn(T.t2f[:], T.t1f[:], ["t1f"], ["t2f"])
+    cp(T.off0[:], T.t2f[:].indirect(T.prm[:, 16:32]), GA * 256, ["t2f", "prm2"], ["off0"])
+
+    for k, wd in enumerate(CH):
         b = k % 2
-        a0 = 512 * k
-        e1, e2 = tb[:, OE1 + a0:OE1 + a0 + 512], tb[:, OE2 + a0:OE2 + a0 + 512]
-        w2, w1 = T.wq[:, 1024 * b:1024 * b + 512], T.wq[:, 1024 * b + 512:1024 * b + 1024]
-        k1, k2, q1, q2 = "E1.%d" % k, "E2.%d" % k, "wq1%d" % b, "wq2%d" % b
-        ts(w2, e2, RND + 16, None, A.add, None, 256, [k2], [q2])
-        ts(w1, e1, RND, None, A.add, None, 256, [k1], [q1])
-        mms(b, 0, 512, [("id1", w1, [q1]), ("idn", w2, [q2])])
-        sel, tq = T.sel[:, 512 * b:512 * b + 512], T.tt[:, 512 * b:512 * b + 512]
-        act(sel, ps[b][:], AF.Relu, 512, [pk(b)], ["sel%d" % b], bias=16.0, scale=2.0)
-        mms(2 + b, 0, 512, [("id1", e2, [k2]), ("id1", w2, [q2]), ("idn", w1, [q1])])
-        tt(tq, ps[2 + b][:], e1, A.min, 512, [pk(2 + b), k1], ["tt%d" % b])
-        mms(4, 0, 512, [("idn", w1, [q1]), ("id1", tq, ["tt%d" % b]), ("id1", sel, ["sel%d" % b])])
-        act(tb[:, OY + a0:OY + a0 + 512], ps[4][:], AF.Identity, 512, ["ps4"], ["Y.%d" % k], bias=3072.0)
-        for s, o, n, x0, kq in ((0, OG2, "G2", w2, q2), (1, OG1, "G1", w1, q1)):
-            x = T.wb[:, 1024 * k + 512 * s:1024 * k + 512 * s + 512]
-            kx = "wb%d.%d" % (k, s)
-            if (2 * k + s) % 4 < OPT["wbs"]:
-                act(x, x0, AF.Identity, 512, [kq], [kx], bias=-193.0 + s, scale=0.0625)
-            else:
-                ts(x, x0, 0.0625, -193.0 + s, A.mult, A.add, 256, [kq], [kx])
-            act(ps[5 + s][:], x, AF.Exp, 512, [kx], [pk(5 + s)], bias=-67 * LN2, scale=7 * LN2)
-            tt(tb[:, o + a0:o + a0 + 512], ps[5 + s][:], x, A.max, 512, [pk(5 + s), kx], ["%s.%d" % (n, k)])
+        a0 = CO[k]
+        e1, e2 = tb[:, OE1 + a0:OE1 + a0 + wd], tb[:, OE2 + a0:OE2 + a0 + wd]
+        w2, w1 = T.wq[:, a0:a0 + wd], T.wq[:, NM + a0:NM + a0 + wd]
+        k1, k2, q1, q2 = "E1.%d" % k, "E2.%d" % k, "wq1.%d" % k, "wq2.%d" % k
+        ts(w2, e2, RND, None, A.add, None, wd / 2, [k2], [q2])
+        ts(w1, e1, RND, None, A.add, None, wd / 2, [k1], [q1])
+        rq, tq = T.rq[:, 512 * b:512 * b + wd], T.tt[:, 512 * b:512 * b + wd]
+        mms(b, 0, wd, [("idp16", T.c3[:, 0:wd], ["ones"]), ("id1", e2, [k2]), ("id1", w2, [q2]), ("idn", w1, [q1])])
+        tt(tq, ps[b][:, 0:wd], e1, A.min, wd, [pk(b), k1], ["tt%d" % b])
+        ts(rq, tq, RND, None, A.add, None, wd / 2, ["tt%d" % b], ["rq%d" % b])
+        mms(2 + b, 0, wd, [("id1", tq, ["tt%d" % b]), ("idn", rq, ["rq%d" % b])])
+        act(tb[:, OY + a0:OY + a0 + wd], ps[2 + b][:, 0:wd], ID, wd, [pk(2 + b)], ["Y.%d" % k], bias=W0)
+    for a0 in range(0, NM, 2048):
+        for s, o, n in ((0, OG2, "G2"), (1, OG1, "G1")):
+            kq = "wq%d" % (2 - s)
+            for a in range(a0, a0 + 2048, 1024):
+                act(tb[:, o + a:o + a + 1024], T.wq[:, NM * s + a:NM * s + a + 1024], AF.Exp, 1024, ck(kq, a, a + 1024), ck(n, a, a + 1024), bias=EB, scale=EA)
+            ks = ck(n, a0, a0 + 2048)
+            op("G", lambda o=o, a0=a0, s=s: g.dma_start(tb[:, o + a0:o + a0 + 2048], T.wq[:, NM * s + a0:NM * s + a0 + 2048], accum_op=A.add),
+               1000, ks + ck(kq, a0, a0 + 2048), ks, lat=6000, kind="d")
 
-    def fold(ph_, j, src, n, ksrc, out, kout, first=None):
-        run, r64, kr = T.run[:, 64 * ph_:64 * ph_ + 64], T.r64[:, 64 * ph_:64 * ph_ + 64], "run%d" % ph_
-        if j == 0:
-            if first is None:
-                cp(run, src[:, 0:64], 64, [ksrc], [kr])
-            else:
-                tt(T.run[:, 64 * ph_:64 * ph_ + QH], src[:, 0:QH], first[0], A.min, 32, [ksrc, first[1]], [kr])
-                cp(T.run[:, 64 * ph_ + QH:64 * ph_ + 64], src[:, QH:64], 48, [ksrc], [kr + "b"])
-        elif j < 4 // NH - 1:
-            tt(run, src[:, 0:64], run, A.min, n, [ksrc, kr, kr + "b"], [kr, kr + "b"])
+    def tree(x, src, ksrc, out, kout, last=None):
+        b = 48 * x
+        tt(T.r32[:, b:b + 32], src[0], src[1], A.min, 64, [ksrc], ["r32%d" % x])
+        if NH == 1 and last is None:
+            tt(out, T.r32[:, b:b + 16], T.r32[:, b + 16:b + 32], A.min, 32, ["r32%d" % x], [kout])
+            return
+        tt(T.r32[:, b + 32:b + 48], T.r32[:, b:b + 16], T.r32[:, b + 16:b + 32], A.min, 32, ["r32%d" % x], ["r16%d" % x])
+        if NH == 1:
+            tt(out, T.r32[:, b + 32:b + 48], last[0], A.min, 32, ["r16%d" % x, last[1]], [kout])
+        elif last is None:
+            tt(out, T.r32[:, b + 32:b + 40], T.r32[:, b + 40:b + 48], A.min, 16, ["r16%d" % x], [kout])
         else:
-            tt(r64, src[:, 0:64], run, A.min, n, [ksrc, kr, kr + "b"], ["r64%d" % ph_])
-            a, b = 64 * ph_, 48 * ph_
-            tt(T.r32[:, b:b + 32], T.r64[:, a:a + 32], T.r64[:, a + 32:a + 64], A.min, 64, ["r64%d" % ph_], ["r32%d" % ph_])
-            if NH == 1:
-                tt(out, T.r32[:, b:b + 16], T.r32[:, b + 16:b + 32], A.min, 32, ["r32%d" % ph_], [kout])
-            else:
-                tt(T.r32[:, b + 32:b + 48], T.r32[:, b:b + 16], T.r32[:, b + 16:b + 32], A.min, 32, ["r32%d" % ph_], ["r16%d" % ph_])
-                tt(out, T.r32[:, b + 32:b + 40], T.r32[:, b + 40:b + 48], A.min, 16, ["r16%d" % ph_], [kout])
+            tt(T.r32[:, b:b + 8], T.r32[:, b + 32:b + 40], T.r32[:, b + 40:b + 48], A.min, 16, ["r16%d" % x], ["r32%d" % x])
+            tt(out, T.r32[:, b:b + 8], last[0], A.min, 16, ["r32%d" % x, last[1]], [kout])
 
-    MB = 512 // LH
+    def rows(o, l, kl, src, ksrc, n, st, sp, b, left=None):
+        if left is not None:
+            mma(left, [(o, l[:, 15 - r:143 - r], src[0][:, src[1] + r:src[1] + 16 * n:16]) for r in range(16)], n, [kl] + ksrc, [pk(b)])
+            return
+        mmx([(o, l[:, 15 - r:143 - r], src[0][:, src[1] + r:src[1] + 16 * n:16], st and r == 0, sp and r == 15) for r in range(16)], n, [kl] + ksrc, [pk(b)])
+
+    def lin(name, out, f, bias, terms, n=512, scale=1.0, key=None):
+        b = BK[name]
+        for j, (x, l, rh, r) in enumerate(terms):
+            a0, a1 = ((0, 256), (256, 512), (0, 512))[x]
+            mm(ps[b][:, a0:a1], C[l], rh, j == 0, j == len(terms) - 1, a1 - a0, r + [l], [pk(b)])
+        act(out, ps[b][:, 0:n], f, n, [pk(b)], [key or name], bias=bias, scale=scale)
+
+    BK = OPT["bk"]
+    zs = (T.z0, T.z1, T.z2x)
     for t in range(NV):
         last = t == NV - 1
         lim = LIMS[t]
-        glim = 0.9 * 2.0 ** (7 * lim - 67)
-        off, z, nf, zo = T["off%d" % t], T["z%d" % t], T["nf%d" % t], T["zo%d" % t]
-        ko, kz, kn, kzo = "off%d" % t, "z%d" % t, "nf%d" % t, "zo%d" % t
+        off, z, nf, zo = T["off%d" % t], zs[t], T["nf%d" % t], T["zo%d" % t]
+        ko, kz, kn, kzo = "off%d" % t, "zz%d" % t, "nf%d" % t, "zo%d" % t
         if t > 0:
             op(None, "arr%d" % t, 0, ["sent%d" % (t - 1)], [ko, kz], lat=500, kind="x")
+        else:
+            kz = "z0"
         cp(nf[:], off[:], 256, [ko], [kn])
         for h in range(NH):
             lr = slice(LH * h, LH * h + LH)
@@ -249,71 +305,91 @@ def build(g, T, nxt, mk):
             sh = str(h)
             for u in range(8 // NH * h, 8 // NH * (h + 1)):
                 a0 = 512 * u
+                j = u // 2
                 gk = ["ga%d.%d" % (u, v) for v in range(MB)]
-                if u in OPT["va"][t]:
+                relu = j in OPT["vr"][t]
+                if relu or u in OPT["va"][t]:
                     for v in range(MB):
                         tt(T.ga[:, a0 + LH * v:a0 + LH * v + LH], win(OY).indirect(off[:, 32 * u + QH * v:32 * u + QH * v + QH]), zh, A.subtract,
                            GA * LH, tk("Y") + [ko, kz], [gk[v]])
-                    act(T.ab[:, a0:a0 + 512], T.ga[:, a0:a0 + 512], AF.Abs, 512, gk, ["ab%d" % u])
+                    if relu:
+                        ts(T.ab[:, a0:a0 + 512], T.ga[:, a0:a0 + 512], 0.0, None, A.max, None, 256, gk, ["ab%d" % u])
+                    else:
+                        act(T.ab[:, a0:a0 + 512], T.ga[:, a0:a0 + 512], AF.Abs, 512, gk, ["ab%d" % u])
                 else:
-                    b = u % 2
-                    act(T.ga[:, a0:a0 + 512], win(OY).indirect(off[:, 32 * u:32 * u + 32]), AF.Identity, GA * 512, tk("Y") + [ko], gk)
-                    for v in range(MB):
-                        mms(b, LH * v, LH, [("idn", zh, [kz]), ("id1", T.ga[:, a0 + LH * v:a0 + LH * v + LH], gk)])
+                    b = OPT["sb"][u]
+                    act(T.ga[:, a0:a0 + 512], win(OY).indirect(off[:, 32 * u:32 * u + 32]), ID, GA * 512, tk("Y") + [ko], gk)
+                    mm(ps[b][:], C["id1"], T.ga[:, a0:a0 + 512], True, False, 512, ["id1"] + gk, [pk(b)])
+                    mmx([(ps[b][:, LH * v:LH * v + LH], C["idn"], zh, False, v == MB - 1) for v in range(MB)], LH, ["idn", kz], [pk(b)])
                     act(T.ab[:, a0:a0 + 512], ps[b][:], AF.Abs, 512, [pk(b)], ["ab%d" % u])
                 if u % 2:
-                    j = u // 2
                     b = 2 + j % 2
                     mm(ps[b][:, 0:64], T.idf[:], nf[:, 64 * j:64 * j + 64], True, False, 64, ["idf", kn], [pk(b)], 4)
-                    for r in range(16):
-                        mm(ps[b][:, 0:64], T.zn[:, 15 - r:143 - r], T.ab[:, 1024 * j + r:1024 * j + 1024:16], False, r == 15, 64, ["zn", "ab%d" % (u - 1), "ab%d" % u], [pk(b)])
-                    fold(h, j - 4 // NH * h, ps[b], 64, pk(b), T.ki[:, qr], "ki" + sh)
+                    left = [0]
+                    if relu:
+                        rows(ps[b][:, 0:64], T.zp, "zp", (T.ga, 1024 * j), ["ga%d.%d" % (u - e, v) for e in range(2) for v in range(MB)], 64, False, False, b, left)
+                    rows(ps[b][:, 0:64], T.z2 if relu else T.zn, "z2" if relu else "zn", (T.ab, 1024 * j), ["ab%d" % (u - 1), "ab%d" % u], 64, False, True, b, left)
+                    if j % (4 // NH) == 0:
+                        cp(T.run[:, 64 * h:64 * h + 64], ps[b][:, 0:64], 64, [pk(b)], ["run" + sh])
+                    elif (j + 1) % (4 // NH):
+                        tt(T.run[:, 64 * h:64 * h + 64], ps[b][:, 0:64], T.run[:, 64 * h:64 * h + 64], A.min, 64, [pk(b), "run" + sh], ["run" + sh])
+                    else:
+                        tt(T.r64[:, 64 * h:64 * h + 64], ps[b][:, 0:64], T.run[:, 64 * h:64 * h + 64], A.min, 64, [pk(b), "run" + sh], ["r64" + sh])
+                        tree(h, (T.r64[:, 64 * h:64 * h + 32], T.r64[:, 64 * h + 32:64 * h + 64]), "r64" + sh, T.ki[:, qr], "ki" + sh)
             ts(T.wi[:, qr], T.ki[:, qr], 8191, None, A.bitwise_and, None, 16, ["ki" + sh], ["wi" + sh])
             wl = T.wl[:, qr]
             cp(wl, T.wi[:, qr], 16, ["wi" + sh], ["wl" + sh])
-            cp(T.yh[:, lr], win(OY).indirect(wl), GA * LH, tk("Y") + ["wl" + sh], ["yh" + sh])
-            act(T.g1w[:, lr], win(OG1).indirect(wl), AF.Identity, GA * LH, tk("G1") + ["wl" + sh], ["g1w" + sh])
-            act(T.g2w[:, lr], win(OG2).indirect(wl), AF.Identity, GA * LH, tk("G2") + ["wl" + sh], ["g2w" + sh])
-            for r in range(16):
-                mm(ps[4][:, 0:QH], T.zw[:, 15 - r:143 - r], T.yh[:, LH * h + r:LH * h + LH:16], r == 0, r == 15, 16, ["zw", "yh" + sh], ["ps4"])
-            cp(T.ui[:, qr], ps[4][:, 0:QH], 16, ["ps4"], ["ui" + sh])
-            ts(T.uu[:, qr], T.ui[:, qr], 4095, None, A.bitwise_and, None, 16, ["ui" + sh], ["uu" + sh])
-            sq = sm("sq", QH * h, QH * h + QH)
-            tt(sq, T.uu[:, qr], T.uu[:, qr], A.mult, 32, ["uu" + sh], ["sq" + sh])
+            act(T.yw[:, lr], win(OY).indirect(wl), ID, GA * LH, tk("Y") + ["wl" + sh], ["yw" + sh])
+            act(T.g1w[:, lr], win(OG1).indirect(wl), ID, GA * LH, tk("G1") + ["wl" + sh], ["g1w" + sh])
+            act(T.g2w[:, lr], win(OG2).indirect(wl), ID, GA * LH, tk("G2") + ["wl" + sh], ["g2w" + sh])
+            pu = ps[4][:, 0:QH]
+            rows(pu, T.zw, "zw", (T.yw, LH * h), ["yw" + sh], QH, True, True, 4)
+            hu, h2 = T.hu[:, qr], T.hu[:, 16 + QH * h:16 + QH * h + QH]
+            ua, ub = 192.0 * 4096, 192.0 * 1024
+            sq, uf, u0, k2 = [sm(x, QH * h, QH * h + QH) for x in ("sq", "uf", "u0", "k2")]
+            if OPT["uv"]:
+                cp(T.ui[:, qr], pu, 16, ["ps4"], ["ui" + sh])
+                uf = T.uu[:, qr]
+                ts(uf, T.ui[:, qr], 4095, None, A.bitwise_and, None, 16, ["ui" + sh], ["uf" + sh])
+                tt(sq, uf, uf, A.mult, 32, ["uf" + sh], ["sq" + sh])
+                ts(T.ui[:, qr], uf, 1023, None, A.bitwise_and, None, 16, ["uf" + sh], ["ui" + sh])
+                ts(k2, T.ui[:, qr], 2.0, 33.0, A.mult, A.add, 16, ["ui" + sh], ["k2" + sh])
+            else:
+                act(hu, pu, ID, QH, ["ps4"], ["hu" + sh], bias=ua - 2047.5)
+                act(u0, pu, ID, QH, ["ps4"], ["u0" + sh])
+                mm(pu, T.idf[:], u0, True, False, QH, ["idf", "u0" + sh], ["ps4"], 4)
+                mms(4, 0, QH, [("idn", hu, ["hu" + sh])], False)
+                act(sq, pu, AF.Square, QH, ["ps4"], ["sq" + sh], bias=ua)
+                act(uf, pu, ID, QH, ["ps4"], ["uf" + sh], bias=ua)
+                act(h2, pu, ID, QH, ["ps4"], ["h2" + sh], bias=ua + ub - 511.5)
+                mm(pu, T.idf[:], uf, True, False, QH, ["idf", "uf" + sh], ["ps4"], 4)
+                mms(4, 0, QH, [("idn", h2, ["h2" + sh])], False)
+                act(k2, pu, ID, QH, ["ps4"], ["k2" + sh], bias=33 + 2 * ub, scale=2.0)
             ts(T.aa[:, qr], sq, 0.03125, -0.375 if t == 0 else T.ac[:, 1:2], A.mult, A.add, 16, ["sq" + sh] + (["ac1"] if t else []), ["aa" + sh])
-            for v, (x0, x1) in enumerate(((0, 64), (64, 256)) if NH == 1 else ((0, 128),)):
+            for v, (x0, x1) in enumerate(OPT["cut"] if NH == 1 else ((0, 128),)):
                 n = x1 - x0
                 tl, xr, kv = T.tile[:, 0:n // 16], slice(LH * h + x0, LH * h + x1), str(h + v)
-                tt(T.ca[:, xr], T.uu[:, qr].indirect(tl), T.ka[:, x0:x1], A.mult, GA * n, ["uu" + sh, "tile"] + kak, ["ca" + kv])
+                tt(T.ca[:, xr], uf.indirect(tl), T.ka[:, x0:x1], A.mult, GA * n, ["uf" + sh, "tile"] + kak, ["ca" + kv])
                 tt(T.cb[:, xr], T.aa[:, qr].indirect(tl), T.ca[:, xr], A.add, GA * n, ["aa" + sh, "tile", "ca" + kv], ["cb" + kv])
                 ts(T.ci[:, xr], T.cb[:, xr], 4095, None, A.bitwise_and, None, n, ["cb" + kv], ["ci" + kv])
                 cp(T.co[:, xr], T.ci[:, xr], n, ["ci" + kv], ["co" + kv])
-                if lim == 11:
-                    cp(T.cf[:, xr], T.ci[:, xr], n, ["ci" + kv], ["cf" + kv])
-            rb = 6 if h < NH - 1 else 0
+            rb = 6 if h == 0 else 0
             for s, x, kx in ((0, T.g1w, "g1w"), (1, T.g2w, "g2w")):
-                for v in range(MB):
-                    mms(rb + s, LH * v, LH, [("id1", x[:, lr], [kx + sh])])
+                mmx([(ps[rb + s][:, LH * v:LH * v + LH], C["id1"], x[:, lr], True, True) for v in range(MB)], LH, ["id1", kx + sh], [pk(rb + s)])
             tt(T.mg[:, lr], ps[rb][:, 0:LH], T.g2w[:, lr], A.min, LH, [pk(rb), "g2w" + sh], ["mg" + sh])
-            for r in range(16):
-                mm(ps[5][:, 0:QH], T.zp[:, 15 - r:143 - r], T.mg[:, LH * h + r:LH * h + LH:16], r == 0, r == 15, 16, ["zp", "mg" + sh], ["ps5"])
-            ts(sm("flb", QH * h, QH * h + QH), ps[5][:, 0:QH], glim * 8192, 386.0 * 8192, A.is_ge, A.mult, 16, ["ps5"], ["flb" + sh])
+            rows(ps[5][:, 0, 0, 0:QH], T.zp, "zp", (T.mg, LH * h), ["mg" + sh], QH, True, True, 5)
+            ts(sm("flb", QH * h, QH * h + QH), ps[5][:, 0, 0, 0:QH], GLIM[lim] * 8192, 386.0 * 8192, A.is_ge, A.mult, 16, ["ps5"], ["flb" + sh])
             tt(sm("dk", QH * h, QH * h + QH), sm("flb", QH * h, QH * h + QH), sm("dz", QH * h, QH * h + QH), A.add, 32, ["flb" + sh, "dz"], ["dk" + sh])
-        ts(T.wl[:, 16:32], T.wi[:], float(2 * TS), None, A.add, None, 16, hk("wi"), ["wl2"])
         cp(T.xf[:, 0:32:2], T.wi[:], 16, hk("wi"), ["xfw"])
-        act(T.yw[:], win(OY).indirect(T.wl[:, 0:16]), AF.Identity, GA * 256, tk("Y") + hk("wl"), ["yw"])
-        mms(5, 0, 256, [("bone", T.mg[:], hk("mg"))])
-        ts(T.fr[:], ps[5][:, 0:256], glim, None, A.is_ge, None, 256, ["ps5"], ["fr"])
-        act(T.nfl[:], T.fr[:], AF.Identity, 256, ["fr"], ["nfl"], bias=1.0, scale=-1.0)
+        cp(T.rr[:, 0, :], io[:].indirect(T.wl[:, 0:16]), GA * 256, iok + hk("wl"), ["rrw"])
+        lin("sg", T.sg[:], AF.Sign, -GLIM[lim], [(0, "bone", T.mg[:], hk("mg"))], 256)
+        sg = (T.sg[:], ["sg"])
+        yw = (T.yw[:], hk("yw"))
         if not last:
             tt(sm("p1"), sm("flb"), T.xf[:, 0:32:2], A.add, 32, hk("flb") + ["xfw"], ["p1"])
-        mms(4, 0, 256, [("id1", z[:], [kz]), ("idn", T.yw[:], ["yw"])])
-        act(zo[:], ps[4][:, 0:256], AF.Abs, 256, ["ps4"], [kzo])
-        ts(T.kk[:], T.uu[:], 1023, None, A.bitwise_and, None, 16, hk("uu"), ["kk"])
-        ts(T.k2[:], T.kk[:], 2.0, 33.0, A.mult, A.add, 16, ["kk"], ["k2"])
-        for h in range(NH):
-            tt(T.q1[:, LH * h:LH * h + LH], T.k2[:, QH * h:QH * h + QH].indirect(T.tile[:, 0:QH]), nf[:, LH * h:LH * h + LH], A.mult, GA * LH, ["k2", "tile", kn], ["q1%d" % h])
-        tt(T.q2[:], T.q1[:], T.k37[:], A.add, 512, hk("q1") + ["k37"], ["q2"])
+        lin("zo", zo[:], AF.Abs, 0.0, [(0, "id1", z[:], [kz]), (0, "idn") + yw], 256, key=kzo)
+        tt(T.q1[:], sm("k2").indirect(T.tile[:]), nf[:], A.mult, GA * 256, hk("k2") + ["tile", kn], ["q1"])
+        tt(T.q2[:], T.q1[:], T.k37[:], A.add, 512, ["q1", "k37"], ["q2"])
         ts(T.ni[:], T.q2[:], 5, 4095, A.arith_shift_right, A.bitwise_and, 256, ["q2"], ["ni"])
         if not last:
             oo = T["offo%d" % t]
@@ -323,170 +399,190 @@ def build(g, T, nxt, mk):
                 sem = T.sem["arr%d" % (t + 1)]
                 return g.remote_dma_fused([
                     RemoteDMATransfer(dst_ids=[nxt], dma_engine_mask=mk[0], remote_sem=sem, src=oo[:], dst=T["off%d" % (t + 1)][:]),
-                    RemoteDMATransfer(dst_ids=[nxt], dma_engine_mask=mk[1], remote_sem=sem, src=zo[:], dst=T["z%d" % (t + 1)][:])],
+                    RemoteDMATransfer(dst_ids=[nxt], dma_engine_mask=mk[1], remote_sem=sem, src=zo[:], dst=zs[t + 1][:])],
                     local_sem=T.sem.sent)
-            op("G", send, 1000, ["offo%d" % t, kzo], ["sent%d" % t], lat=5000, kind="r")
+            op("G", send, 1000, ["offo%d" % t, kzo], ["sent%d" % t], lat=OPT["rl"][t], kind="r")
         else:
             dma(T.yz[:], zo[:], 65536, [kzo], ["yz"])
-            cp(T.nfn[:], T.ni[:].indirect(T.prm[:, 32:48]), GA * 256, ["ni", "prm3"], ["nfn"])
-        if OPT["tz"]:
-            mms(5, 0, 256, [("id1", z[:], [kz]), ("idn", T.yw[:], ["yw"]), ("id256", T.fr[:], ["fr"])])
-            act(T.tz[:], ps[5][:, 0:256], AF.Relu, 256, ["ps5"], ["tz"], bias=16.0)
-        else:
-            tt(T.tz[:], ps[4][:, 0:256], T.nfl[:], A.mult, 256, ["ps4", "nfl"], ["tz"])
-        act(T.ew[:], win(OE2, 3).indirect(T.wl[:]), AF.Identity, GA * 512, tk("E2", "G1", "E1") + hk("wl") + ["wl2"], ["ew"])
-        act(T.wqw[:], T.ew[:], AF.Identity, 512, ["ew"], ["wqw"], bias=RND)
-
-        def two(bank, terms):
-            for h in range(2):
-                mms(bank, 256 * h, 256, terms(h, slice(256 * h, 256 * h + 256)))
-        if not last:
-            two(5, lambda h, s: [("id1", z[:], [kz]), ("idm16", T.fr[:], ["fr"])] if h == 0 else [("id1", T.g2w[:], hk("g2w")), ("id40", T.nfl[:], ["nfl"])])
-            act(T.s1[:], ps[5][:], AF.Relu, 512, ["ps5"], ["s1"])
-        two(4, lambda h, s: [("id1", T.ew[:, s], ["ew"]), ("idn", T.wqw[:, s], ["wqw"]), ("idn", z[:], [kz])])
-        act(T.s2[:], ps[4][:], AF.Square, 512, ["ps4"], ["s2"], bias=3072.0)
-        two(5, lambda h, s: [("id1", T.s2[:, s], ["s2"]), ("id256", T.fr[:], ["fr"])])
-        if OPT["ne"]:
-            act(T.ne[:], ps[5][:], AF.Sign, 512, ["ps5"], ["ne"])
-            two(4, lambda h, s: [("id1", T.wqw[:, s], ["wqw"]), ("idp16", T.ne[:, s], ["ne"]), ("idp16", T.fr[:], ["fr"])])
-        else:
-            ts(T.ne[:], ps[5][:], 0.0, 16.0, A.is_gt, A.mult, 512, ["ps5"], ["ne"])
-            mms(4, 0, 512, [("id1", T.wqw[:], ["wqw"]), ("id1", T.ne[:], ["ne"])])
-        if OPT["wn"]:
-            act(T.wr2[:], ps[4][:], AF.Relu, 512, ["ps4"], ["wr2"], bias=3312.0, scale=-1.0)
-            act(T.wn[:], T.wr2[:], AF.Identity, 512, ["wr2"], ["wn"], bias=240.0, scale=-1.0)
-        else:
-            ts(T.wn[:], ps[4][:], -3072.0, 240.0, A.add, A.min, 512, ["ps4"], ["wn"])
-        two(5, lambda h, s: [("id16", T.wn[:, s], ["wn"]), ("id20", T.fr[:], ["fr"])])
-        act(T.rl[:], ps[5][:, 0:256], AF.Relu, 256, ["ps5"], ["rl"], scale=16.0)
-        if not last:
-            act(T.ex[:], ps[5][:], AF.Exp, 512, ["ps5"], ["ex"], bias=-67 * LN2, scale=7 * LN2)
-            tt(T.gn[:], ps[5][:], T.ex[:], A.max, 512, ["ps5", "ex"], ["gn"])
-        two(4, lambda h, s: [("id1", T.yw[:], ["yw"]), ("id1", T.tz[:], ["tz"])] + ([("idm16", T.nfl[:], ["nfl"])] if OPT["tz"] else []) +
-            [("id1", T.rl[:], ["rl"]) if h == 0 else ("id1", T.wn[:, s], ["wn"])])
-        act(T.ee[:], ps[4][:], AF.Identity, 512, ["ps4"], ["ee"])
-        if last:
-            turn(T.nfn[:], "nfn", 5, T.yno[:], "yno")
+            cp(T.t1f[:], T.ni[:].indirect(T.prm[:, 32:48]), GA * 256, ["ni", "prm3"], ["t1f"])
+            turn(T.tw[:, 0:256], T.t1f[:], ["t1f"], ["tw0"])
+            swap(T.tw[:, 0:256], "tw0", BK["yn"], T.yno[:], "yno")
             dma(T.yn[:], T.yno[:], 131072, ["yno"], ["yn"])
+        zz = (z[:], [kz])
+        lin("tz", T.tz[:], AF.Relu, -112.0, [(0, "id1") + zz, (0, "idn") + yw, (0, "idm128") + sg], 256)
+        act(T.ew[:, 0:256], win(OE2).indirect(T.wl[:, 0:16]), ID, GA * 256, tk("E2") + hk("wl"), ["ew0"])
+        act(T.ew[:, 256:512], win(OE1).indirect(T.wl[:, 0:16]), ID, GA * 256, tk("E1") + hk("wl"), ["ew1"])
+        act(T.wqw[:], T.ew[:], ID, 512, ["ew0", "ew1"], ["wqw"], bias=RND)
+        if not last:
+            lin("s1", T.s1[:], AF.Relu, 0.0, [(2, "idmH", T.c3[:], ["ones"]), (0, "idmH") + sg, (1, "idH") + sg, (0, "id1") + zz, (1, "id1", T.g2w[:], hk("g2w"))])
+        lin("s2", T.s2[:], AF.Square, W0, [(2, "id1", T.ew[:], ["ew0", "ew1"]), (0, "idn") + zz, (1, "idn") + zz, (2, "idn", T.wqw[:], ["wqw"])])
+        lin("ne", T.ne[:], AF.Sign, -128.0, [(2, "id1", T.s2[:], ["s2"]), (0, "idm128") + sg, (1, "idm128") + sg])
+        lin("wr2", T.wr2[:], AF.Relu, W0 + 232, [(2, "id1", T.wqw[:], ["wqw"]), (0, "id8") + sg, (1, "id8") + sg, (2, "idp16", T.ne[:], ["ne"])], scale=-1.0)
+        act(T.wx[:, 256:768], T.wr2[:], ID, 512, ["wr2"], ["wn"], bias=240.0, scale=-1.0)
+        lin("rl", T.rl[:], AF.Relu, 112.0, [(0, "idm128") + sg, (0, "idn", T.wr2[:, 0:256], ["wr2"])], 256)
+        if not last:
+            act(T.ex[:], T.wr2[:], AF.Exp, 512, ["wr2"], ["ex"], bias=EB + EA * (W0 + 240), scale=-EA)
+            lin("gn", T.gn[:], AF.Relu, W0 + 240, [(2, "idmH", T.c3[:], ["ones"]), (0, "idmH") + sg, (1, "idmH") + sg, (2, "idn", T.wr2[:], ["wr2"]), (2, "id1", T.ex[:], ["ex"])])
+        lin("nd", T.nx[:, 0:256], ID, -8.0, [(0, "id1") + yw, (0, "id8") + sg, (0, "id1", T.tz[:], ["tz"])], 256)
         for j in range(4):
             h = j * NH // 4
             sh = str(h)
-            rb = 6 if h < NH - 1 else 0
-            kv = str(h) if NH == 2 else str(min(j, 1))
+            lr = slice(LH * h, LH * h + LH)
+            rb = 6 if h == 0 else 0
+            kco = "co%d" % (h if NH == 2 else [v for v, x in enumerate(OPT["cut"]) if x[0] <= 64 * j][-1])
+            cik = ["ci" + sh] if NH == 2 else ["ci%d" % v for v in range(len(OPT["cut"]))]
             for s, o, n, x, kx in ((0, OG2, "G2", T.g1w, "g1w"), (1, OG1, "G1", T.g2w, "g2w")):
+                u0 = 2 * (2 * j + s)
+                both = u0 not in OPT["vc"][t] and u0 + 1 not in OPT["vc"][t] and u0 in OPT["big"]
+                if both:
+                    act(T.gb[:, 512 * u0:512 * u0 + 1024], win(o).indirect(T.co[:, 64 * j:64 * j + 64]), ID, GA * 1024, tk(n) + [kco], ["gb%d" % u0, "gb%d" % (u0 + 1)])
                 for e in range(2):
-                    u = 2 * (2 * j + s) + e
+                    u = u0 + e
                     a1, cc = 512 * u, 64 * j + 32 * e
                     mkeys = ["mm%d.%d" % (u, v) for v in range(MB)]
                     if u in OPT["vc"][t]:
                         for v in range(MB):
-                            tt(T.mm[:, a1 + LH * v:a1 + LH * v + LH], win(o).indirect(T.co[:, cc + QH * v:cc + QH * v + QH]), x[:, LH * h:LH * h + LH], A.min, GA * LH,
-                               tk(n) + ["co" + kv, kx + sh], [mkeys[v]])
+                            tt(T.mm[:, a1 + LH * v:a1 + LH * v + LH], win(o).indirect(T.co[:, cc + QH * v:cc + QH * v + QH]), x[:, lr], A.min, GA * LH,
+                               tk(n) + [kco, kx + sh], [mkeys[v]])
                     else:
-                        act(T.gb[:, a1:a1 + 512], win(o).indirect(T.co[:, cc:cc + 32]), AF.Identity, GA * 512, tk(n) + ["co" + kv], ["gb%d" % u])
+                        if not both:
+                            act(T.gb[:, a1:a1 + 512], win(o).indirect(T.co[:, cc:cc + 32]), ID, GA * 512, tk(n) + [kco], ["gb%d" % u])
                         tt(T.mm[:, a1:a1 + 512], ps[rb + s][:], T.gb[:, a1:a1 + 512], A.min, 512, [pk(rb + s), "gb%d" % u], mkeys)
-            b = 2 + j % 2
-            kb = pk(b)
-            if lim == 11:
-                mm(ps[b][:, 0:64], T.idf[:], T.cf[:, 64 * j:64 * j + 64], True, False, 64, ["idf", "cf" + kv], [kb], 4)
+            y = j // 3
+            b, wd = 2 + y, (192, 64)[y]
+            kb, sy, yr = pk(b), str(y), slice(192 * y, 192 * y + wd)
+            x = ps[b][:, 0:wd]
+            if j % 3 == 0:
+                mm(x, C["idm128"], T.cst[:, 0:wd], True, False, wd, ["idm128", "cst"], [kb])
+                named = y == 1 and lim == 11
+                left = [int(named)]
             for s in range(2):
-                a0 = 1024 * (2 * j + s)
                 mkeys = ["mm%d.%d" % (2 * (2 * j + s) + e, v) for e in range(2) for v in range(MB)]
-                for r in range(16):
-                    mm(ps[b][:, 0:64], T.zp[:, 15 - r:143 - r], T.mm[:, a0 + r:a0 + 1024:16], lim != 11 and s == 0 and r == 0, s == 1 and r == 15, 64, ["zp"] + mkeys, [kb])
-            fo = (T.kj[:, QH * h:QH * h + QH], "kj" + sh, (sm("dk", QH * h, QH * h + QH), "dk" + sh))
-            if lim == 11:
-                fold(2 + h, j - 4 // NH * h, ps[b], 64, kb, *fo)
+                rows(ps[b][:, 64 * (j % 3):64 * (j % 3) + 64], T.zq, "zq", (T.mm, 1024 * (2 * j + s)), mkeys, 64, False, False, b, left)
+            if named:
+                cp(T.kc[:, yr], T.ci[:, yr], 64, cik, ["kc1"])
+                mm(x, T.idf[:], T.kc[:, yr], False, True, 64, ["idf", "kc1"], [kb], 4)
+            if j < 2:
+                continue
+            k12 = 512 * (C12 - W0 - 192) if lim == 13 else 0
+            if lim == 13:
+                act(T.n1[:, yr], x, ID, wd, [kb], ["n1" + sy], bias=128.0, scale=1.0 / (512 * (C12 - W0)))
+                act(T.n4[:, yr], T.n1[:, yr], AF.Relu, wd, ["n1" + sy], ["n4" + sy], bias=160 * k12, scale=-k12)
+                tt(x, x, T.n4[:, yr], A.add, wd, [kb, "n4" + sy], [kb])
+            if lim > 11:
+                act(T.n3[:, yr], x, ID, wd, [kb], ["n3" + sy], bias=2.0 ** 22 * (192 - 0.375) - 32 * k12)
+                act(T.n4[:, yr], T.n3[:, yr], ID, wd, ["n3" + sy], ["n4" + sy], bias=192.0 * 8016 * 512 - 32 * k12, scale=-8016.0 / 8192)
+                tt(x, x, T.n4[:, yr], A.add, wd, [kb, "n4" + sy], [kb])
+            if not named:
+                tt(T.kc[:, yr], x, T.ci[:, yr], A.add, wd, [kb] + cik, ["kc" + sy])
+            if y == 0:
+                tt(T.kc[:, 0:16], T.kc[:, 0:16], sm("dk"), A.min, 32, ["kc0", "dk0"], ["kc0"])
+                tt(T.r64[:, 64:128], T.kc[:, 64:128], T.kc[:, 128:192], A.min, 128, ["kc0"], ["pre0"])
+                tt(T.r64[:, 128:192], T.r64[:, 64:128], T.kc[:, 0:64], A.min, 128, ["kc0", "pre0"], ["pre1"])
             else:
-                x = ps[b][:, 0:64]
-                ts(T.d1[:], x, 1.5 * 2.0 ** 46, None, A.add, None, 64, [kb], ["d1"])
-                if lim == 13:
-                    ts(T.d2[:], x, 1.5 * 2.0 ** 53, None, A.add, None, 64, [kb], ["d2"])
-                ts(T.d1[:], T.d1[:], -1.5 * 2.0 ** 46, -1013.0 / 1024, A.add, A.mult, 64, ["d1"], ["d1"])
-                if lim == 13:
-                    ts(T.d2[:], T.d2[:], -1.5 * 2.0 ** 53, -1396.0 / 131072, A.add, A.mult, 64, ["d2"], ["d2"])
-                tt(T.d1[:], x, T.d1[:], A.add, 64, [kb, "d1"], ["d1"])
-                if lim == 13:
-                    tt(T.d1[:], T.d1[:], T.d2[:], A.add, 128, ["d1", "d2"], ["d1"])
-                tt(T.kc[:], T.d1[:], T.ci[:, 64 * j:64 * j + 64], A.add, 128, ["d1", "ci" + kv], ["kc"])
-                fold(2 + h, j - 4 // NH * h, T.kc, 128, "kc", *fo)
+                tt(T.r64[:, 192:256], x if named else T.kc[:, yr], T.r64[:, 128:192], A.min, 64 if named else 128, [kb, "kc1", "pre1"], ["pre2"])
+                tree(2, (T.r64[:, 192:224], T.r64[:, 224:256]), "pre2", T.kj[:], "kj0")
         ts(T.ce[:], T.kj[:], 8191, None, A.bitwise_and, None, 16, hk("kj"), ["ce"])
         cl = T.cl[:, 0:16]
-        cp(T.xf[:, 1:32:2], T.ce[:], 16, ["ce"], ["xfc"])
-        cp(T.il[:], T.xf[:], 32, ["xfw", "xfc"], ["il"])
-        cp(T.rr[:], io[:].indirect(T.il[:]), GA * 512, ["io0", "io1", "il"], ["rr"])
+        xc = T.xf[:, 1:32:2]
+        cp(xc, T.ce[:], 16, ["ce"], ["xfc"])
         cp(cl, T.ce[:], 16, ["ce"], ["cl"])
-        ts(T.cl[:, 16:32], T.ce[:], float(2 * TS), None, A.add, None, 16, ["ce"], ["cl2"])
-        act(T.wqc[:], win(OE2, 3).indirect(T.cl[:]), AF.Identity, GA * 512, tk("E2", "G1", "E1") + ["cl", "cl2"], ["wqc"], bias=RND)
-        act(T.yc[:], win(OY).indirect(cl), AF.Identity, GA * 256, tk("Y") + ["cl"], ["yc"])
-        act(T.w2c[:], T.wqc[:, 0:256], AF.Identity, 256, ["wqc"], ["w2c"], bias=-3072.0)
+        cp(T.rr[:, 1, :], io[:].indirect(cl), GA * 256, iok + ["cl"], ["rr"])
+        act(T.wqc[:, 0:256], win(OE2).indirect(cl), ID, GA * 256, tk("E2") + ["cl"], ["wqc0"], bias=RND)
+        act(T.wqc[:, 256:512], win(OE1).indirect(cl), ID, GA * 256, tk("E1") + ["cl"], ["wqc1"], bias=RND)
+        yc = T.nx[:, 256:512]
+        act(yc, win(OY).indirect(cl), ID, GA * 256, tk("Y") + ["cl"], ["yc"])
+        lin("w2c", T.wx[:, 0:256], ID, -W0, [(0, "id1", T.rl[:], ["rl"]), (0, "id1", T.wqc[:, 0:256], ["wqc0"])], 256)
+        if last:
+            act(T.wx[:, 768:1024], T.wqc[:, 256:512], ID, 256, ["wqc1"], ["s3"], bias=-W0)
+        else:
+            act(T.g2c[:], win(OG2).indirect(cl), ID, GA * 256, tk("G2") + ["cl"], ["g2c"])
+            lin("s3", T.s3[:], ID, -W0, [(0, "id1", T.wqc[:, 256:512], ["wqc1"]), (0, "id1", yc, ["yc"]), (0, "id1", T.gn[:, 256:512], ["gn"])], 256)
+        pm_, km = ps[BK["cm"]], pk(BK["cm"])
+        mm(pm_[:], C["idn"], T.th[:], True, False, 512, ["idn", "th"], [km])
+        mm(pm_[:], C["idn"], T.c4[:], False, False, 512, ["idn", "c4"], [km])
+        left = [0]
+        for late in range(2):
+            e0 = 0
+            for i in range(32):
+                q = i // 2
+                n = 256 - 16 * q
+                e1 = e0 + n
+                wq_ = 2.0 ** (90 - 12 * q)
+                if i % 2 == 0 and q < OPT["ww"]:
+                    ke = ("ea%d", "eb%d")[late] % i
+                    ts(T.eb[:, late, e0:e1], T.rr[:, late, 16 * q:256], T.xf[:, i:i + 1], wq_, A.is_equal, A.mult, n / 2, [("rrw", "rr")[late], "xfw"], [ke])
+                    mma(left, [(pm_[:, q:16, late, :], C["bw"], T.eb[:, late, e0:e1])], n, ["bw", ke], [km])
+                elif late:
+                    ts(T.eb[:, :, e0:e1], T.rr[:, :, 16 * q:256], T.xf[:, i:i + 1], wq_, A.is_equal, A.mult, n, ["rr", "rrw", "xfw", "xfc"], ["eb%d" % i, "ea%d" % i])
+                    mma(left, [(pm_[:, q:16, s, :], C["bw"], T.eb[:, s, e0:e1]) for s in range(2)], n, ["bw", "eb%d" % i], [km])
+                e0 = e1
         if not last:
-            act(T.g2c[:], win(OG2).indirect(cl), AF.Identity, GA * 256, tk("G2") + ["cl"], ["g2c"])
-        mms(1, 0, 256, [("id1", T.wqc[:, 256:512], ["wqc"]), ("id1", T.yc[:], ["yc"])] + ([] if last else [("id1", T.gn[:, 256:512], ["gn"])]))
-        act(T.s3[:], ps[1][:, 0:256], AF.Identity, 256, ["ps1"], ["s3"], bias=-3072.0)
-        mm(ps[0][:], C["idn"], T.th[:], True, False, 512, ["idn", "th"], ["ps0"])
-        mm(ps[0][:], C["idn"], T.c4[:], False, False, 512, ["idn", "c4"], ["ps0"])
-        for i in range(32):
-            q = i // 2
-            n = 512 - 32 * q
-            e = T.eb[:, 512 * (i % 4):512 * (i % 4) + n]
-            ts(e, T.rr[:, 32 * q:512], T.xf[:, i:i + 1], 2.0 ** (90 - 12 * q), A.is_equal, A.mult, n / 2, ["rr", "xfw", "xfc"], ["eb%d" % (i % 4)])
-            mm(ps[0][:, 32 * q:512], C["bw"], e, False, i == 31, n, ["bw", "eb%d" % (i % 4)], ["ps0"])
-        if not last:
-            ts(sm("b1"), T.ce[:], float(TS), None, A.add, None, 16, ["ce"], ["b1"])
+            act(sm("b1"), xc, ID, 16, ["xfc"], ["b1"], bias=float(TS))
             tt(T.bb[:, 0:16], sm("b1"), sm("p1"), A.min, 32, ["b1", "p1"], ["bba"])
         ts(sm("b2"), T.kj[:], -385.0 * 8192, None, A.add, None, 16, hk("kj"), ["b2"])
         tt(T.bb[:, 16:32], sm("b2"), T.xf[:, 0:32:2], A.max, 32, ["b2", "xfw"], ["bbb"])
-        cp(T.bb[:, 32:48], T.ce[:], 16, ["ce"], ["bbc"])
-        op("V", lambda: V.tensor_tensor_scan(T.sc[:], T.keep[:], ps[0][:], 0.0, A.mult, A.max), vc(512), ["keep", "ps0"], ["sc"])
+        act(T.bb[:, 32:48], xc, ID, 16, ["xfc"], ["bbc"])
         lo = 16 if last else 0
-        ts(T.hm[:, lo:48], T.sc[:].indirect(T.hitl[:, 0:(48 - lo) // 16]), 0.0, 30000.0, A.is_gt, A.mult, 100, ["sc", "hitl"], ["hm"])
-        tt(T.o1[:, lo:48], T.hm[:, lo:48], T.bb[:, lo:48], A.max, 96, ["hm", "bba", "bbb", "bbc"], ["o1"])
+        act(T.hm[:, lo:48], T.bb[:, lo:48], ID, 48, ["bba", "bbb", "bbc"], ["hm"], scale=2.0 ** -15)
+        act(T.sn[:], pm_[:], AF.Sign, 512, [km], ["sn"])
+        op("V", lambda: V.tensor_tensor_scan(T.sc[:], T.keep[:], T.sn[:], 0.0, A.mult, A.max), vc(256), ["keep", "sn"], ["sc"])
+        tt(T.o1[:, lo:48], T.sc[:].indirect(T.hitl[:, 0:(48 - lo) // 16]), T.hm[:, lo:48], A.max, 100, ["sc", "hitl", "hm"], ["o1"])
         tt(T.o2[:, lo:48], T.o1[:, lo:48], T.d3[:, lo:48], A.min, 96, ["o1", "d30", "d31", "d32"], ["o2"])
-        cp(T.ol[:, lo:48], T.o2[:, lo:48], 48, ["o2"], ["ol"])
-        l1, l2, l4 = T.ol[:, 0:16], T.ol[:, 16:32], T.ol[:, 32:48]
-        n = SCA * 256
+        ts(T.ol[:, lo:48], T.o2[:, lo:48], 2.0 ** 15, None, A.mult, None, 48, ["o2"], ["ol"])
+        def scatter(o, nt, l0, n, a, a0, b, b0, r, w, parts):
+            for x in range(0, n, n // parts):
+                m = n // parts
+                out = win(o, nt).indirect(T.ol[:, l0 + x // 16:l0 + (x + m) // 16])
+                if b is None:
+                    cp(out, a[:, a0 + x:a0 + x + m], SCA * m, ["ol"] + r, w)
+                else:
+                    tt(out, a[:, a0 + x:a0 + x + m], b[:, b0 + x:b0 + x + m], A.add, SCA * m, ["ol"] + r, w)
+        sp = OPT["split"]
         if not last:
-            tt(win(OY, 2).indirect(l1), T.s1[:, 0:256], T.s1[:, 256:512], A.add, n, ["ol", "s1"], tk("Y", "G2"))
-            tt(win(OG2).indirect(l2), T.g2c[:], T.gn[:, 0:256], A.add, n, ["ol", "g2c", "gn"], tk("G2"))
-            cp(win(OG1, 2).indirect(l1), T.s3[:], n, ["ol", "s3"], tk("G1", "E1"))
-        tt(win(OE2).indirect(l2), T.w2c[:], T.ee[:, 0:256], A.add, n, ["ol", "w2c", "ee"], tk("E2"))
-        tt(win(OE2).indirect(l4), T.wn[:, 0:256], T.yc[:], A.add, n, ["ol", "wn", "yc"], tk("E2"))
-        cp(win(OE1).indirect(l2), T.ee[:, 256:512], n, ["ol", "ee"], tk("E1"))
-        if last:
-            cp(win(OE1).indirect(l4), T.s3[:], n, ["ol", "s3"], tk("E1"))
-        else:
-            ts(sm("has"), T.ce[:], float(NM), None, A.is_lt, None, 16, ["ce"], ["has"])
-            tt(T.exf[:], sm("has"), T.hm[:, 0:16], A.is_gt, 32, ["has", "hm"], ["exf"])
+            scatter(OY, 2, 0, 256, T.s1, 0, T.s1, 256, ["s1"], tk("Y", "G2"), 1)
+            scatter(OG2, 1, 16, 256, T.g2c, 0, T.gn, 0, ["g2c", "gn"], tk("G2"), sp[0])
+            scatter(OG1, 2, 0, 256, T.s3, 0, None, 0, ["s3"], tk("G1", "E1"), sp[0])
+        scatter(OE2, 1, 16, 512, T.wx, 0, T.nx, 0, ["w2c", "wn", "nd", "yc"], tk("E2"), 1 if last else sp[1])
+        scatter(OE1, 1, 16, 512 if last else 256, T.wx, 512, T.nx, 0, ["wn", "nd", "yc", "s3"], tk("E1"), 1 if last else sp[2])
+        if not last:
+            act(T.exf[:], T.o2[:, 32:48], AF.Sign, 16, ["o2"], ["exf"], bias=(NM - 0.5) * 2.0 ** -15, scale=-1.0)
             mms(4, 0, 16, [("ones", T.exf[:], ["exf"])])
-            op("V", lambda: V.tensor_reduce(T.ac[:, 0:1], ps[4][:, 0:16], AxisListType.X, A.add), vc(16), ["ps4"], ["ac0"])
-            ts(T.ac[:, 1:2], T.ac[:, 0:1], -0.375, None, A.add, None, 1, ["ac0"], ["ac1"])
+            act(sm("b1"), ps[4][:, 0:16], ID, 16, ["ps4"], ["ac0", "b1"], acc=T.ac[:, 0:1])
+            act(T.ac[:, 1:2], T.ac[:, 0:1], ID, 1, ["ac0"], ["ac1"], bias=1024 - 0.375, scale=0.5)
     dma(T.ys[:], tb[:, OE2:OE2 + NM], 1 << 20, tk("E2"), ["ys"])
-    mms(4, 0, 64, [("id1", tb[:, OE1 + 64 * j:OE1 + 64 * j + 64], tk("E1")) for j in range(64)])
-    act(T.yfo[:], ps[4][:, 0:64], AF.Identity, 64, ["ps4"], ["yfo"])
+    mmx([(ps[4][:, 0:64], C["id1"], tb[:, OE1 + 64 * j:OE1 + 64 * j + 64], j == 0, j == 63) for j in range(64)], 64, ["id1"] + tk("E1"), ["ps4"])
+    act(T.yfo[:], ps[4][:, 0:64], ID, 64, ["ps4"], ["yfo"])
     dma(T.yf[:], T.yfo[:], 32768, ["yfo"], ["yf"])
     return ops
 
 
 def depend(ops):
-    lw, rd = {}, {}
+    lw, rd, acc = {}, {}, {}
     for i, o in enumerate(ops):
         raw, oth = set(), set()
         for k in o["r"]:
             if k in lw:
                 raw.add(lw[k])
+            raw.update(acc.get(k, ()))
         for k in o["w"]:
             if k in lw:
                 oth.add(lw[k])
             oth.update(rd.get(k, ()))
+            if not o.get("acc"):
+                oth.update(acc.get(k, ()))
         for k in o["r"]:
             if k.startswith("ps"):
                 oth.update(j for j in rd.get(k, ()) if ops[j]["e"] != o["e"])
         for k in o["r"]:
             rd.setdefault(k, []).append(i)
         for k in o["w"]:
-            lw[k] = i
-            rd[k] = []
+            if o.get("acc"):
+                acc.setdefault(k, []).append(i)
+            else:
+                lw[k] = i
+                rd[k] = []
+                acc[k] = []
         oth.discard(i)
         o["raw"], o["dep"] = raw, raw | oth
 
@@ -499,10 +595,10 @@ def schedule(ops):
         for i in sorted(o["dep"]):
             e = ops[i]["e"]
             same = o["e"] == e and ops[i]["k"] == "c" and e == "P"
-            d = ops[i]["lat"] + (0 if same else OPT["hop"])
+            d = ops[i]["lat"] + (0 if same else OPT["hop"] if o["e"] == e else OPT["xhop"])
             fw[i].append((j, d))
             bw[j].append((i, d))
-    cost = [o["c"] for o in ops]
+    cost = [o["c"] * OPT["mul"].get(o["e"], 1.0) for o in ops]
     eng = [o["e"] for o in ops]
     up = [1e9 - 1e6 * i if o["k"] == "d" and not o["r"] else OPT["boost"] if o["w"][0] in BOOST else 0.0 for i, o in enumerate(ops)]
 
@@ -543,10 +639,69 @@ def schedule(ops):
         t0 = best[2]
         _, b0 = sweep(bw, fw, [t0[i] + cost[i] + float(nz[i]) for i in range(n)], [0.0 if fw[i] else ops[i]["lat"] for i in range(n)], OPT["look"])
         pr = [b0[i] + cost[i] for i in range(n)]
+    pred = [[(i, cost[i] + d) for i, d in p] for p in bw]
+    deps = [o["dep"] for o in ops]
+
+    def times(order):
+        t, by, free, prev, end, tip = [0.0] * n, [-1] * n, {}, {}, 0.0, -1
+        for j in order:
+            s, b = 0.0, -1
+            for i, d in pred[j]:
+                if t[i] + d > s:
+                    s, b = t[i] + d, i
+            e = eng[j]
+            if e is not None:
+                if free.get(e, -1.0) >= s:
+                    s, b = free[e], -2 - prev[e]
+                free[e], prev[e] = s + cost[j], j
+            t[j], by[j] = s, b
+            if s + cost[j] + ops[j]["lat"] > end:
+                end, tip = s + cost[j] + ops[j]["lat"], j
+        return end, t, by, tip
+    cur = list(best[1])
+    end, t0, by, tip = times(cur)
+    best = (end, list(cur), t0)
+    for it, (r1, r2, r3, r4) in enumerate(rng.random((OPT["moves"], 4)).tolist()):
+        links, j = [], tip
+        while j != -1:
+            if by[j] <= -2:
+                links.append((-2 - by[j], j))
+            j = by[j] if by[j] > -2 else -2 - by[j]
+        a, b = links[int(r1 * len(links))]
+        k = (1, 1, 2, 3, 5, 8)[int(r2 * 6)]
+        pa, pb = cur.index(a), cur.index(b)
+        if r3 < 0.5:
+            while k > 1 and pa > 0:
+                pa -= 1
+                k -= eng[cur[pa]] == eng[b]
+            seg, need = cur[pa:pb + 1], {b}
+            for x in reversed(seg):
+                if x in need:
+                    need |= deps[x]
+            new = [x for x in seg if x in need] + [x for x in seg if x not in need]
+        else:
+            while k > 1 and pb < n - 1:
+                pb += 1
+                k -= eng[cur[pb]] == eng[a]
+            seg, aft = cur[pa:pb + 1], {a}
+            for x in seg:
+                if deps[x] & aft:
+                    aft.add(x)
+            new = [x for x in seg if x not in aft] + [x for x in seg if x in aft]
+        new = cur[:pa] + new + cur[pb + 1:]
+        res = times(new)
+        if res[0] <= end - OPT["temp"] * math.log(1 - r4):
+            cur = new
+            end, t0, by, tip = res
+            if it % 20 == 0:
+                cur.sort(key=lambda x: t0[x])
+            if end < best[0]:
+                best = (end, list(cur), t0)
     INFO["end"] = best[0]
     for i, o in enumerate(ops):
         o["t0"] = best[2][i]
-    return best[1]
+    loads = [i for i, o in enumerate(ops) if o["k"] == "d" and not o["dep"]]
+    return loads + [i for i in best[1] if i not in loads]
 
 
 def rank_program(g, core, T, topo):

import math
import numpy as np
from concourse.bass import DstId, RemoteDMATransfer
from concourse.mybir import AluOpType as A, AxisListType, ActivationFunctionType as AF

NM, LN, NV = 4096, 256, 3
LIMS = (13, 11, 12)
WT = (1, 16, 256, 37, 411, 93, 777, 165, 1029, 251, 1313, 339, 1583, 503, 1847, 618)
KA = (3, 61, 118, 207, 346, 419, 530, 677, 742, 895, 1011, 1164, 1283, 1450, 1629, 1874)
TS = NM + 3 * LN
OY, OG2, OE2, OG1, OE1 = 0, TS, 2 * TS, 3 * TS, 4 * TS
LN2 = math.log(2.0)
W0 = 2880.0
RND = W0 - 7.5
X11, C11, C12 = 8000.0, W0 + 8192, 8192000.0
EA = math.log(1024.0) / 16
EB = math.log(X11) - EA * (W0 + 176)
GLIM = {11: 51500.0, 12: 1e6, 13: 1e9}
BIG = 2.0 ** 59
OPT = {"pieces": (512, 1024, 1024, 1024, 256, 256), "ch": (512,) * 7 + (256, 256), "split": (1, 2, 1), "vz": ("Y",),
       "nh": 1, "uv": 0, "ww": 12, "sb": (0, 1, 6, 7, 0, 1, 6, 7), "cut": ((0, 64), (64, 256)), "big": (2, 4, 6, 8, 10, 12),
       "bk": {"sg": 0, "zo": 1, "tz": 1, "s1": 0, "s2": 4, "ne": 1, "wr2": 4, "rl": 0, "gn": 1, "nd": 4, "w2c": 6, "s3": 7, "cm": 5, "yn": 0},
       "va": ((2, 3, 4), (0, 4), (0, 4)), "vr": ((0,), (1,), (1,)), "vc": ((0, 4, 8, 12), (0, 4, 8, 12), (0, 4, 8, 12)), "gv": (),
       "seed": 0, "noise": 3000.0, "iters": 2, "moves": 40000, "temp": 40.0, "look": 300.0, "lam": 20.0, "frac": 0.1, "boost": 2000.0, "ga": 1.56, "sca": 3.8, "hop": 170.0, "xhop": 170.0,
       "mul": {"G": 1.3, "P": 1.1}, "rl": (11000, 8000)}
BOOST = ("cl", "cl2", "gn", "ne", "wn", "tz", "wl2")

B, F, I, U, H = "bfloat16", "float32", "int32", "uint16", "float16"
IDS = (("idn", -1.0), ("idp16", 16.0), ("idm128", -128.0), ("id8", 8.0), ("idH", BIG), ("idmH", -BIG))
SB = {
    "tb": (5 * TS, B), "io32": (TS, F), "wq": (8192, B), "rq": (1024, B), "tt": (1024, B),
    "ab": (4096, B), "ga": (4096, B), "gb": (8192, B), "mm": (8192, B), "eb": (8704, B),
    "pi": (1, I), "pj": (4, I), "pf": (16, F), "rd": (128, I), "wr": (16, F), "rr": (512, U), "il": (32, U),
    "ids": (128 * (len(IDS) + 3), B), "cst": (192, B), "sm": (192, F), "idf": (128, F), "psw": (128, F),
    "zp": (144, B), "zn": (144, B), "z2": (144, B), "zq": (144, B), "zw": (144, H),
    "i16": (16, F), "tile": (16, U), "prm": (48, U), "hitl": (4, U), "d3": (48, F), "pc2": (80, F),
    "k37": (256, F), "ka": (256, F), "th": (512, B), "keep": (512, B), "c1": (512, F), "c2": (512, F), "c3": (512, B), "c4": (512, B),
    "nmi": (256, I), "tw": (512, F), "t1f": (256, F), "t2f": (256, F),
    "off0": (256, U), "off1": (256, U), "off2": (256, U), "z0": (256, B), "z1": (256, B), "z2x": (256, B),
    "offo0": (256, U), "offo1": (256, U), "zo0": (256, B), "zo1": (256, B), "zo2": (256, B), "nf0": (256, F), "nf1": (256, F), "nf2": (256, F),
    "run": (256, F), "r64": (256, F), "r32": (192, F), "ki": (16, I), "wi": (16, I), "wl": (32, U), "xf": (32, F),
    "yw": (256, B), "g1w": (256, B), "g2w": (256, B), "hu": (32, B), "aa": (16, I),
    "ca": (256, F), "cb": (256, I), "ci": (256, I), "co": (256, U), "n1": (256, B), "n2": (256, B), "n3": (256, B), "n4": (256, F), "ui": (16, I), "uu": (16, I), "kc": (256, F),
    "mg": (256, B), "sg": (256, B), "tz": (256, B), "ew": (512, B), "wqw": (512, B), "s2": (512, B), "ne": (512, B),
    "wn": (512, B), "wr2": (512, B), "ex": (512, B), "gn": (512, B), "rl": (256, B), "nd": (256, B), "s1": (512, B),
    "kj": (16, I), "ce": (16, I), "cl": (32, U), "bb": (48, F),
    "g2c": (256, B), "wqc": (512, B), "wx": (1024, B), "nx": (512, B), "s3": (256, B), "sn": (512, B),
    "sc": (512, B), "hm": (48, F), "o1": (48, F), "o2": (48, F), "ol": (48, U), "exf": (16, B), "ac": (2, F),
    "q1": (256, F), "q2": (256, I), "ni": (256, I), "yno": (256, F), "yfo": (64, F),
}
SMALL = ("b1", "b2", "p1", "dk", "flb", "sq", "dz", "u0", "dum", "uf", "k2")
SCRATCH = {n: ("sbuf", [128, w], d) for n, (w, d) in SB.items()}
SCRATCH["rr"] = ("sbuf", [128, 2, 256], U)
SCRATCH["eb"] = ("sbuf", [128, 2, 4352], B)
for _b in range(8):
    SCRATCH["ps%d" % _b] = ("psum", [128, 512], F)
SCRATCH["ps5"] = ("psum", [128, 16, 2, 16], F)
SEMAPHORES = ["eV", "eS", "eP", "eG", "arr1", "arr2", "sent"] + ["d%d" % _i for _i in range(24)]
INFO = {}


def build(g, T, nxt, mk):
    ops = []
    V, S, P = g.vector, g.scalar, g.tensor
    GA, SCA, NH = OPT["ga"], OPT["sca"], OPT["nh"]
    QH, LH, MB = 16 // NH, LN // NH, 2 * NH

    def op(e, fn, cost, r, w, lat=0.0, kind="c"):
        ops.append({"e": e, "fn": fn, "c": cost, "r": list(r), "w": list(w), "lat": lat, "k": kind})

    def vc(n):
        return 45 + 0.83 * max(64, n)

    def ts(o, i, s1, s2, o0, o1, n, r, w):
        if o1 is None:
            op("V", lambda: V.tensor_scalar(o, i, s1, None, o0), vc(n), r, w)
        else:
            op("V", lambda: V.tensor_scalar(o, i, s1, s2, o0, o1), vc(n), r, w)

    def tt(o, a, b, o0, n, r, w):
        op("V", lambda: V.tensor_tensor(o, a, b, o0), vc(n), r, w)

    def cp(o, i, n, r, w):
        op("V", lambda: V.tensor_copy(o, i), vc(n), r, w)

    def act(o, i, f, n, r, w, bias=0.0, scale=1.0, acc=None):
        op("S", lambda: S.activation(o, i, f, bias=bias, scale=scale, accum_out=acc), 70 + 0.83 * n + (0 if acc is None else 140), r, w)

    def mm(o, l, rh, st, sp, n, r, w, k=1):
        op("P", lambda: P.matmul(o, l, rh, st, sp), 8 + 0.42 * k * max(64, n), r, w)

    def mmx(calls, n, r, w):
        op("P", lambda: [P.matmul(*c) for c in calls][-1], len(calls) * (8 + 0.42 * max(64, n)), r, w)

    def mma(left, calls, n, r, w, k=1):
        left[0] += 1

        def fn():
            left[0] -= 1
            return [P.matmul(c[0], c[1], c[2], False, left[0] == 0 and j == len(calls) - 1) for j, c in enumerate(calls)][-1]
        op("P", fn, len(calls) * (8 + 0.42 * k * max(64, n)), r, w)
        ops[-1]["acc"] = 1

    def mms(b, x0, n, terms, st=True, sp=True):
        for j, (l, rh, r) in enumerate(terms):
            mm(ps[b][:, x0:x0 + n], C[l], rh, st and j == 0, sp and j == len(terms) - 1, n, r + [l], [pk(b)])

    def dma(o, i, nbytes, r, w, e="Y"):
        op(e, lambda: (S if e == "S" else g.sync).dma_start(o, i), 60, r, w, lat=1800 + nbytes / 150.0, kind="d")

    def iota(o, pat, base, cm, n, w):
        op("G", lambda: g.iota(o, pat, base, cm, allow_small_or_imprecise_dtypes=True), 130 + 1.66 * n, [], w)

    tb, io, pf = T.tb, T.io32, T.pf
    C = {n: T.ids[:, 128 * j:128 * j + 128] for j, n in enumerate([x[0] for x in IDS] + ["id1", "bone", "bw"])}
    C["ones"] = T.c3[:, 0:128]
    ps = [T["ps%d" % b] for b in range(8)]
    one = (T.c3[:, 0:256], ["ones"])

    def sm(n, a=0, b=16):
        j = 16 * SMALL.index(n)
        return T.sm[:, j + a:j + b]

    def pk(b):
        return "ps%d" % b

    def win(o, n=1):
        return tb[:, o:o + n * TS]

    def tk(*ns):
        return ["%s.%s" % (n, k) for n in ns for k in list(range(len(CH))) + ["z"]]

    CH = OPT["ch"]
    CO = [sum(CH[:k]) for k in range(len(CH) + 1)]

    def ck(n, a, b):
        return ["%s.%d" % (n, k) for k in range(len(CH)) if CO[k] < b and CO[k + 1] > a]

    def hk(n):
        return ["%s%d" % (n, h) for h in range(NH)]

    dma(T.nmi[:], T.nm[:], 131072, [], ["nmi"])
    c0 = 0
    for j, wd in enumerate(OPT["pieces"]):
        dma(tb[:, OE2 + c0:OE2 + c0 + wd], T.pg[:, NM + c0:NM + c0 + wd], 256 * (2 * c0 + wd), [], ck("E2", c0, c0 + wd))
        dma(tb[:, OE1 + c0:OE1 + c0 + wd], T.pg[:, c0:c0 + wd], 256 * (2 * c0 + 2 * wd), [], ck("E1", c0, c0 + wd), "S")
        if j == 1:
            dma(T.z0[:], T.zv[:], 256 * 2048, [], ["z0"])
        c0 += wd

    op("G", lambda: g.iota(T.pi[:], [[0, 1]], 0, 1), 135, [], ["pi"])
    iota(io[:, 0:256], [[1, 256]], 0, 0, 256, ["io0"])
    iota(T.c3[:], [[0, 512]], 1, 0, 512, ["ones"])
    iota(T.pc2[:, 0:16], [[128, 2], [2, 8]] if NH == 2 else [[1, 16]], 0, 0, 16, ["pc2"])
    iota(T.pc2[:, 16:32], [[32, 8], [256, 2]], 0, 0, 16, ["pc3"])
    iota(T.pc2[:, 32:48], [[0, 8], [1, 2]], 0, 0, 16, ["pc4"])
    iota(T.c1[:], [[-48, 16], [0, 2], [-3, 16]], 0, 0, 512, ["c1"])
    iota(T.c2[:], [[0, 32], [1, 16]], 0, 0, 512, ["c2"])
    iota(T.k37[:], [[(9472 * QH) % NM, NH], [37, 16], [9472, QH]], 0, 0, 256, ["k37"])
    for j in range(4):
        iota(io[:, 256 + 1152 * j:256 + 1152 * (j + 1)], [[1, 1152]], 256 + 1152 * j, 0, 1152, ["io1%d" % j])
    iok = ["io0"] + ["io1%d" % j for j in range(4)]
    for j in range(16):
        iota(T.wr[:, j:j + 1], [[0, 1]], WT[j], 0, 1, ["wr%d" % j])
        iota(T.ka[:, QH * j:QH * j + QH], [[0, QH]], KA[j], 0, QH, ["ka%d" % j])
    kak = ["ka%d" % j for j in range(16)]
    iota(T.cst[:], [[0, 192]], int(32 * W0 * 512 / 128), 0, 192, ["cst"])
    for n, o in (("Y", OY), ("G2", OG2), ("E2", OE2), ("G1", OG1), ("E1", OE1)):
        if n in OPT["vz"]:
            op("V", lambda o=o: V.memset(tb[:, o + NM:o + TS], 0.0), vc(384), [], [n + ".z"])
        else:
            iota(tb[:, o + NM:o + TS], [[0, 768]], 0, 0, 768, [n + ".z"])
    ts(T.pj[:, 0:1], T.pi[:], 15, None, A.bitwise_and, None, 1, ["pi"], ["pj0"])
    ts(T.pj[:, 1:2], T.pi[:], 4, None, A.arith_shift_right, None, 1, ["pi"], ["pj1"])
    ts(T.pj[:, 2:3], T.pi[:], QH - 1, None, A.bitwise_and, None, 1, ["pi"], ["pj2"])
    ts(T.pj[:, 3:4], T.pi[:], 16, None, A.bitwise_and, None, 1, ["pi"], ["pj3"])
    pc, pm, pd, pq, px, zc, hc, kc37, rho, wc, ph, pa, pb, pe, pg_, pw = [pf[:, j:j + 1] for j in range(16)]
    cp(pc, T.pi[:], 1, ["pi"], ["pc"])
    cp(pf[:, 1:5], T.pj[:, 0:4], 4, ["pj0", "pj1", "pj2", "pj3"], ["pm"])
    ID = AF.Identity
    act(zc, pd, ID, 1, ["pm"], ["zc"], bias=15.0, scale=16.0)
    act(hc, pm, ID, 1, ["pm"], ["hc"], bias=31.0, scale=32.0)
    act(kc37, pm, ID, 1, ["pm"], ["kc37"], scale=592.0)
    ts(ph, pm, pq, 1.0 / QH, A.subtract, A.mult, 1, ["pm"], ["ph"])
    act(pa, pq, ID, 1, ["pm", "ph"], ["pa"], bias=ph, scale=16.0)
    act(pb, pm, ID, 1, ["pm"], ["pb"], scale=float(QH))
    act(pe, px, ID, 1, ["pm"], ["pe"], bias=pm, scale=17.0)
    act(pg_, px, ID, 1, ["pm"], ["pg"], scale=-32.0)
    act(pw, px, ID, 1, ["pm", "pc"], ["pw"], bias=pc, scale=-2.0)
    act(rho, pm, AF.Exp, 1400, ["pm"], ["rho"], scale=-0.75 * LN2)
    ts(C["id1"], io[:, 0:128], pc, None, A.is_equal, None, 128, ["io0", "pc"], ["id1"])
    for n, s in IDS:
        act(C[n], C["id1"], ID, 128, ["id1"], [n], scale=s)
    act(T.idf[:], C["id1"], ID, 128, ["id1"], ["idf"])
    ts(T.psw[:], io[:, 0:128], -16.0, pw, A.add, A.is_equal, 128, ["io0", "pw"], ["psw"])
    ts(T.i16[:], io[:, 0:16], pm, None, A.is_equal, None, 16, ["io0", "pm"], ["i16"])
    act(T.pc2[:, 32:48], T.pc2[:, 32:48], ID, 16, ["pc4", "pe", "pg"], ["pc4"], bias=pe, scale=pg_)
    tt(T.pc2[:, 16:32], T.pc2[:, 16:32], T.pc2[:, 32:48], A.add, 32, ["pc3", "pc4"], ["pc3"])
    cp(T.prm[:, 0:16], T.pc2[:, 16:32], 16, ["pc3"], ["prm1"])
    ts(T.prm[:, 16:32], T.pc2[:, 0:16], pa, None, A.add, None, 16, ["pc2", "pa"], ["prm2"])
    iota(T.pc2[:, 48:64], [[128, NH], [1, QH]], 0, 0, 16, ["pc5"])
    ts(T.prm[:, 32:48], T.pc2[:, 48:64], pb, None, A.add, None, 16, ["pc5", "pb"], ["prm3"])
    iota(T.pc2[:, 64:80], [[8, NH], [0, QH]], 0, 0, 16, ["pc6"])
    ts(T.tile[:], T.pc2[:, 64:80], pq, None, A.add, None, 16, ["pc6", "pm"], ["tile"])
    ts(T.hitl[:], io[:, 0:4], 0.0, hc, A.mult, A.add, 4, ["io0", "hc"], ["hitl"])
    ts(T.zp[:], io[:, 0:144], zc, 8192.0, A.is_equal, A.mult, 144, ["io0", "zc"], ["zp"])
    for n, s in (("zn", -1.0), ("z2", -2.0), ("zq", 0.0625)):
        act(T[n][:], T.zp[:], ID, 144, ["zp"], [n], scale=s)
    tt(T.wr[:], T.wr[:], T.i16[:], A.mult, 32, ["wr%d" % j for j in range(16)] + ["i16"], ["wrm"])
    op("V", lambda: V.tensor_reduce(wc, T.wr[:], AxisListType.X, A.add), vc(16), ["wrm"], ["wc"])
    ts(T.zw[:], io[:, 0:144], zc, wc, A.is_equal, A.mult, 144, ["io0", "zc", "wc"], ["zw"])
    ts(T.rd[:], io[:, 0:128], 0.0625, -0.46875, A.mult, A.add, 128, ["io0"], ["rd"])
    ts(C["bone"], T.rd[:], pd, None, A.is_equal, None, 128, ["rd", "pm"], ["bone"])
    act(C["bw"], C["bone"], ID, 128, ["bone", "rho"], ["bw"], scale=rho)
    act(sm("dum"), io[:, 0:16], ID, 16, ["io0", "pm"], ["dum"], bias=pm, scale=16.0)
    for j, x in enumerate((TS + NM, NM, NM + LN)):
        act(T.d3[:, 16 * j:16 * j + 16], sm("dum"), ID, 16, ["dum"], ["d3%d" % j], bias=x * 2.0 ** -15, scale=2.0 ** -15)
    act(sm("dz"), sm("dum"), ID, 16, ["dum"], ["dz"], bias=NM + 2 * LN - 8192.0)
    act(T.k37[:], T.k37[:], ID, 256, ["k37", "kc37"], ["k37"], bias=kc37)
    act(T.k37[:], T.k37[:], ID, 256, ["k37"], ["k37"], scale=32.0)
    act(T.c4[:], T.c1[:], AF.Exp, 512, ["c1"], ["c4"], bias=90 * LN2 + math.log(2.57), scale=LN2 / 4)
    ts(T.th[:], T.c2[:], pm, 2.0 ** 95, A.not_equal, A.mult, 512, ["c2", "pm"], ["th"])
    op("G", lambda: g.affine_select(T.keep[:], T.c3[:], [[0, 16], [1, 32]], A.is_gt, 0.0, 0, 0), 1020, ["ones"], ["keep"])

    def swap(src, ksrc, bank, dst, kdst):
        mm(ps[bank][:, 0:256], T.psw[:], src, True, True, 256, ["psw", ksrc], [pk(bank)], 4)
        act(T.tw[:, 256:512], ps[bank][:, 0:256], ID, 256, [pk(bank)], ["tw1"])
        act(dst, T.tw[:].indirect(T.prm[:, 0:16]), ID, GA * 256, [ksrc, "tw1", "prm1"], [kdst])

    def turn(o, i, r, w):
        op("V", lambda: V.transpose(o, i), vc(256), r, w)

    cp(T.tw[:, 0:256], T.nmi[:], 256, ["nmi"], ["tw0"])
    swap(T.tw[:, 0:256], "tw0", 7, T.t1f[:], "t1f")
    turn(T.t2f[:], T.t1f[:], ["t1f"], ["t2f"])
    cp(T.off0[:], T.t2f[:].indirect(T.prm[:, 16:32]), GA * 256, ["t2f", "prm2"], ["off0"])

    for k, wd in enumerate(CH):
        b = k % 2
        a0 = CO[k]
        e1, e2 = tb[:, OE1 + a0:OE1 + a0 + wd], tb[:, OE2 + a0:OE2 + a0 + wd]
        w2, w1 = T.wq[:, a0:a0 + wd], T.wq[:, NM + a0:NM + a0 + wd]
        k1, k2, q1, q2 = "E1.%d" % k, "E2.%d" % k, "wq1.%d" % k, "wq2.%d" % k
        ts(w2, e2, RND, None, A.add, None, wd / 2, [k2], [q2])
        ts(w1, e1, RND, None, A.add, None, wd / 2, [k1], [q1])
        rq, tq = T.rq[:, 512 * b:512 * b + wd], T.tt[:, 512 * b:512 * b + wd]
        mms(b, 0, wd, [("idp16", T.c3[:, 0:wd], ["ones"]), ("id1", e2, [k2]), ("id1", w2, [q2]), ("idn", w1, [q1])])
        tt(tq, ps[b][:, 0:wd], e1, A.min, wd, [pk(b), k1], ["tt%d" % b])
        ts(rq, tq, RND, None, A.add, None, wd / 2, ["tt%d" % b], ["rq%d" % b])
        mms(2 + b, 0, wd, [("id1", tq, ["tt%d" % b]), ("idn", rq, ["rq%d" % b])])
        act(tb[:, OY + a0:OY + a0 + wd], ps[2 + b][:, 0:wd], ID, wd, [pk(2 + b)], ["Y.%d" % k], bias=W0)
    for a0 in range(0, NM, 2048):
        for s, o, n in ((0, OG2, "G2"), (1, OG1, "G1")):
            kq = "wq%d" % (2 - s)
            for a in range(a0, a0 + 2048, 1024):
                act(tb[:, o + a:o + a + 1024], T.wq[:, NM * s + a:NM * s + a + 1024], AF.Exp, 1024, ck(kq, a, a + 1024), ck(n, a, a + 1024), bias=EB, scale=EA)
            ks = ck(n, a0, a0 + 2048)
            op("G", lambda o=o, a0=a0, s=s: g.dma_start(tb[:, o + a0:o + a0 + 2048], T.wq[:, NM * s + a0:NM * s + a0 + 2048], accum_op=A.add),
               1000, ks + ck(kq, a0, a0 + 2048), ks, lat=6000, kind="d")

    def tree(x, src, ksrc, out, kout, last=None):
        b = 48 * x
        tt(T.r32[:, b:b + 32], src[0], src[1], A.min, 64, [ksrc], ["r32%d" % x])
        if NH == 1 and last is None:
            tt(out, T.r32[:, b:b + 16], T.r32[:, b + 16:b + 32], A.min, 32, ["r32%d" % x], [kout])
            return
        tt(T.r32[:, b + 32:b + 48], T.r32[:, b:b + 16], T.r32[:, b + 16:b + 32], A.min, 32, ["r32%d" % x], ["r16%d" % x])
        if NH == 1:
            tt(out, T.r32[:, b + 32:b + 48], last[0], A.min, 32, ["r16%d" % x, last[1]], [kout])
        elif last is None:
            tt(out, T.r32[:, b + 32:b + 40], T.r32[:, b + 40:b + 48], A.min, 16, ["r16%d" % x], [kout])
        else:
            tt(T.r32[:, b:b + 8], T.r32[:, b + 32:b + 40], T.r32[:, b + 40:b + 48], A.min, 16, ["r16%d" % x], ["r32%d" % x])
            tt(out, T.r32[:, b:b + 8], last[0], A.min, 16, ["r32%d" % x, last[1]], [kout])

    def rows(o, l, kl, src, ksrc, n, st, sp, b, left=None):
        if left is not None:
            mma(left, [(o, l[:, 15 - r:143 - r], src[0][:, src[1] + r:src[1] + 16 * n:16]) for r in range(16)], n, [kl] + ksrc, [pk(b)])
            return
        mmx([(o, l[:, 15 - r:143 - r], src[0][:, src[1] + r:src[1] + 16 * n:16], st and r == 0, sp and r == 15) for r in range(16)], n, [kl] + ksrc, [pk(b)])

    def lin(name, out, f, bias, terms, n=512, scale=1.0, key=None):
        b = BK[name]
        for j, (x, l, rh, r) in enumerate(terms):
            a0, a1 = ((0, 256), (256, 512), (0, 512))[x]
            mm(ps[b][:, a0:a1], C[l], rh, j == 0, j == len(terms) - 1, a1 - a0, r + [l], [pk(b)])
        act(out, ps[b][:, 0:n], f, n, [pk(b)], [key or name], bias=bias, scale=scale)

    BK = OPT["bk"]
    zs = (T.z0, T.z1, T.z2x)
    for t in range(NV):
        last = t == NV - 1
        lim = LIMS[t]
        off, z, nf, zo = T["off%d" % t], zs[t], T["nf%d" % t], T["zo%d" % t]
        ko, kz, kn, kzo = "off%d" % t, "zz%d" % t, "nf%d" % t, "zo%d" % t
        if t > 0:
            op(None, "arr%d" % t, 0, ["sent%d" % (t - 1)], [ko, kz], lat=500, kind="x")
        else:
            kz = "z0"
        cp(nf[:], off[:], 256, [ko], [kn])
        for h in range(NH):
            lr = slice(LH * h, LH * h + LH)
            qr = slice(QH * h, QH * h + QH)
            zh = z[:, lr]
            sh = str(h)
            for u in range(8 // NH * h, 8 // NH * (h + 1)):
                a0 = 512 * u
                j = u // 2
                gk = ["ga%d.%d" % (u, v) for v in range(MB)]
                relu = j in OPT["vr"][t]
                if relu or u in OPT["va"][t]:
                    for v in range(MB):
                        tt(T.ga[:, a0 + LH * v:a0 + LH * v + LH], win(OY).indirect(off[:, 32 * u + QH * v:32 * u + QH * v + QH]), zh, A.subtract,
                           GA * LH, tk("Y") + [ko, kz], [gk[v]])
                    if relu:
                        ts(T.ab[:, a0:a0 + 512], T.ga[:, a0:a0 + 512], 0.0, None, A.max, None, 256, gk, ["ab%d" % u])
                    else:
                        act(T.ab[:, a0:a0 + 512], T.ga[:, a0:a0 + 512], AF.Abs, 512, gk, ["ab%d" % u])
                else:
                    b = OPT["sb"][u]
                    act(T.ga[:, a0:a0 + 512], win(OY).indirect(off[:, 32 * u:32 * u + 32]), ID, GA * 512, tk("Y") + [ko], gk)
                    mm(ps[b][:], C["id1"], T.ga[:, a0:a0 + 512], True, False, 512, ["id1"] + gk, [pk(b)])
                    mmx([(ps[b][:, LH * v:LH * v + LH], C["idn"], zh, False, v == MB - 1) for v in range(MB)], LH, ["idn", kz], [pk(b)])
                    act(T.ab[:, a0:a0 + 512], ps[b][:], AF.Abs, 512, [pk(b)], ["ab%d" % u])
                if u % 2:
                    b = 2 + j % 2
                    mm(ps[b][:, 0:64], T.idf[:], nf[:, 64 * j:64 * j + 64], True, False, 64, ["idf", kn], [pk(b)], 4)
                    left = [0]
                    if relu:
                        rows(ps[b][:, 0:64], T.zp, "zp", (T.ga, 1024 * j), ["ga%d.%d" % (u - e, v) for e in range(2) for v in range(MB)], 64, False, False, b, left)
                    rows(ps[b][:, 0:64], T.z2 if relu else T.zn, "z2" if relu else "zn", (T.ab, 1024 * j), ["ab%d" % (u - 1), "ab%d" % u], 64, False, True, b, left)
                    if j % (4 // NH) == 0:
                        cp(T.run[:, 64 * h:64 * h + 64], ps[b][:, 0:64], 64, [pk(b)], ["run" + sh])
                    elif (j + 1) % (4 // NH):
                        tt(T.run[:, 64 * h:64 * h + 64], ps[b][:, 0:64], T.run[:, 64 * h:64 * h + 64], A.min, 64, [pk(b), "run" + sh], ["run" + sh])
                    else:
                        tt(T.r64[:, 64 * h:64 * h + 64], ps[b][:, 0:64], T.run[:, 64 * h:64 * h + 64], A.min, 64, [pk(b), "run" + sh], ["r64" + sh])
                        tree(h, (T.r64[:, 64 * h:64 * h + 32], T.r64[:, 64 * h + 32:64 * h + 64]), "r64" + sh, T.ki[:, qr], "ki" + sh)
            ts(T.wi[:, qr], T.ki[:, qr], 8191, None, A.bitwise_and, None, 16, ["ki" + sh], ["wi" + sh])
            wl = T.wl[:, qr]
            cp(wl, T.wi[:, qr], 16, ["wi" + sh], ["wl" + sh])
            act(T.yw[:, lr], win(OY).indirect(wl), ID, GA * LH, tk("Y") + ["wl" + sh], ["yw" + sh])
            act(T.g1w[:, lr], win(OG1).indirect(wl), ID, GA * LH, tk("G1") + ["wl" + sh], ["g1w" + sh])
            act(T.g2w[:, lr], win(OG2).indirect(wl), ID, GA * LH, tk("G2") + ["wl" + sh], ["g2w" + sh])
            pu = ps[4][:, 0:QH]
            rows(pu, T.zw, "zw", (T.yw, LH * h), ["yw" + sh], QH, True, True, 4)
            hu, h2 = T.hu[:, qr], T.hu[:, 16 + QH * h:16 + QH * h + QH]
            ua, ub = 192.0 * 4096, 192.0 * 1024
            sq, uf, u0, k2 = [sm(x, QH * h, QH * h + QH) for x in ("sq", "uf", "u0", "k2")]
            if OPT["uv"]:
                cp(T.ui[:, qr], pu, 16, ["ps4"], ["ui" + sh])
                uf = T.uu[:, qr]
                ts(uf, T.ui[:, qr], 4095, None, A.bitwise_and, None, 16, ["ui" + sh], ["uf" + sh])
                tt(sq, uf, uf, A.mult, 32, ["uf" + sh], ["sq" + sh])
                ts(T.ui[:, qr], uf, 1023, None, A.bitwise_and, None, 16, ["uf" + sh], ["ui" + sh])
                ts(k2, T.ui[:, qr], 2.0, 33.0, A.mult, A.add, 16, ["ui" + sh], ["k2" + sh])
            else:
                act(hu, pu, ID, QH, ["ps4"], ["hu" + sh], bias=ua - 2047.5)
                act(u0, pu, ID, QH, ["ps4"], ["u0" + sh])
                mm(pu, T.idf[:], u0, True, False, QH, ["idf", "u0" + sh], ["ps4"], 4)
                mms(4, 0, QH, [("idn", hu, ["hu" + sh])], False)
                act(sq, pu, AF.Square, QH, ["ps4"], ["sq" + sh], bias=ua)
                act(uf, pu, ID, QH, ["ps4"], ["uf" + sh], bias=ua)
                act(h2, pu, ID, QH, ["ps4"], ["h2" + sh], bias=ua + ub - 511.5)
                mm(pu, T.idf[:], uf, True, False, QH, ["idf", "uf" + sh], ["ps4"], 4)
                mms(4, 0, QH, [("idn", h2, ["h2" + sh])], False)
                act(k2, pu, ID, QH, ["ps4"], ["k2" + sh], bias=33 + 2 * ub, scale=2.0)
            ts(T.aa[:, qr], sq, 0.03125, -0.375 if t == 0 else T.ac[:, 1:2], A.mult, A.add, 16, ["sq" + sh] + (["ac1"] if t else []), ["aa" + sh])
            for v, (x0, x1) in enumerate(OPT["cut"] if NH == 1 else ((0, 128),)):
                n = x1 - x0
                tl, xr, kv = T.tile[:, 0:n // 16], slice(LH * h + x0, LH * h + x1), str(h + v)
                tt(T.ca[:, xr], uf.indirect(tl), T.ka[:, x0:x1], A.mult, GA * n, ["uf" + sh, "tile"] + kak, ["ca" + kv])
                tt(T.cb[:, xr], T.aa[:, qr].indirect(tl), T.ca[:, xr], A.add, GA * n, ["aa" + sh, "tile", "ca" + kv], ["cb" + kv])
                ts(T.ci[:, xr], T.cb[:, xr], 4095, None, A.bitwise_and, None, n, ["cb" + kv], ["ci" + kv])
                cp(T.co[:, xr], T.ci[:, xr], n, ["ci" + kv], ["co" + kv])
            rb = 6 if h == 0 else 0
            for s, x, kx in ((0, T.g1w, "g1w"), (1, T.g2w, "g2w")):
                mmx([(ps[rb + s][:, LH * v:LH * v + LH], C["id1"], x[:, lr], True, True) for v in range(MB)], LH, ["id1", kx + sh], [pk(rb + s)])
            tt(T.mg[:, lr], ps[rb][:, 0:LH], T.g2w[:, lr], A.min, LH, [pk(rb), "g2w" + sh], ["mg" + sh])
            rows(ps[5][:, 0, 0, 0:QH], T.zp, "zp", (T.mg, LH * h), ["mg" + sh], QH, True, True, 5)
            ts(sm("flb", QH * h, QH * h + QH), ps[5][:, 0, 0, 0:QH], GLIM[lim] * 8192, 386.0 * 8192, A.is_ge, A.mult, 16, ["ps5"], ["flb" + sh])
            tt(sm("dk", QH * h, QH * h + QH), sm("flb", QH * h, QH * h + QH), sm("dz", QH * h, QH * h + QH), A.add, 32, ["flb" + sh, "dz"], ["dk" + sh])
        cp(T.xf[:, 0:32:2], T.wi[:], 16, hk("wi"), ["xfw"])
        cp(T.rr[:, 0, :], io[:].indirect(T.wl[:, 0:16]), GA * 256, iok + hk("wl"), ["rrw"])
        lin("sg", T.sg[:], AF.Sign, -GLIM[lim], [(0, "bone", T.mg[:], hk("mg"))], 256)
        sg = (T.sg[:], ["sg"])
        yw = (T.yw[:], hk("yw"))
        if not last:
            tt(sm("p1"), sm("flb"), T.xf[:, 0:32:2], A.add, 32, hk("flb") + ["xfw"], ["p1"])
        lin("zo", zo[:], AF.Abs, 0.0, [(0, "id1", z[:], [kz]), (0, "idn") + yw], 256, key=kzo)
        tt(T.q1[:], sm("k2").indirect(T.tile[:]), nf[:], A.mult, GA * 256, hk("k2") + ["tile", kn], ["q1"])
        tt(T.q2[:], T.q1[:], T.k37[:], A.add, 512, ["q1", "k37"], ["q2"])
        ts(T.ni[:], T.q2[:], 5, 4095, A.arith_shift_right, A.bitwise_and, 256, ["q2"], ["ni"])
        if not last:
            oo = T["offo%d" % t]
            cp(oo[:], T.ni[:], 256, ["ni"], ["offo%d" % t])

            def send(t=t, oo=oo, zo=zo):
                sem = T.sem["arr%d" % (t + 1)]
                return g.remote_dma_fused([
                    RemoteDMATransfer(dst_ids=[nxt], dma_engine_mask=mk[0], remote_sem=sem, src=oo[:], dst=T["off%d" % (t + 1)][:]),
                    RemoteDMATransfer(dst_ids=[nxt], dma_engine_mask=mk[1], remote_sem=sem, src=zo[:], dst=zs[t + 1][:])],
                    local_sem=T.sem.sent)
            op("G", send, 1000, ["offo%d" % t, kzo], ["sent%d" % t], lat=OPT["rl"][t], kind="r")
        else:
            dma(T.yz[:], zo[:], 65536, [kzo], ["yz"])
            cp(T.t1f[:], T.ni[:].indirect(T.prm[:, 32:48]), GA * 256, ["ni", "prm3"], ["t1f"])
            turn(T.tw[:, 0:256], T.t1f[:], ["t1f"], ["tw0"])
            swap(T.tw[:, 0:256], "tw0", BK["yn"], T.yno[:], "yno")
            dma(T.yn[:], T.yno[:], 131072, ["yno"], ["yn"])
        zz = (z[:], [kz])
        lin("tz", T.tz[:], AF.Relu, -112.0, [(0, "id1") + zz, (0, "idn") + yw, (0, "idm128") + sg], 256)
        act(T.ew[:, 0:256], win(OE2).indirect(T.wl[:, 0:16]), ID, GA * 256, tk("E2") + hk("wl"), ["ew0"])
        act(T.ew[:, 256:512], win(OE1).indirect(T.wl[:, 0:16]), ID, GA * 256, tk("E1") + hk("wl"), ["ew1"])
        act(T.wqw[:], T.ew[:], ID, 512, ["ew0", "ew1"], ["wqw"], bias=RND)
        if not last:
            lin("s1", T.s1[:], AF.Relu, 0.0, [(2, "idmH", T.c3[:], ["ones"]), (0, "idmH") + sg, (1, "idH") + sg, (0, "id1") + zz, (1, "id1", T.g2w[:], hk("g2w"))])
        lin("s2", T.s2[:], AF.Square, W0, [(2, "id1", T.ew[:], ["ew0", "ew1"]), (0, "idn") + zz, (1, "idn") + zz, (2, "idn", T.wqw[:], ["wqw"])])
        lin("ne", T.ne[:], AF.Sign, -128.0, [(2, "id1", T.s2[:], ["s2"]), (0, "idm128") + sg, (1, "idm128") + sg])
        lin("wr2", T.wr2[:], AF.Relu, W0 + 232, [(2, "id1", T.wqw[:], ["wqw"]), (0, "id8") + sg, (1, "id8") + sg, (2, "idp16", T.ne[:], ["ne"])], scale=-1.0)
        act(T.wx[:, 256:768], T.wr2[:], ID, 512, ["wr2"], ["wn"], bias=240.0, scale=-1.0)
        lin("rl", T.rl[:], AF.Relu, 112.0, [(0, "idm128") + sg, (0, "idn", T.wr2[:, 0:256], ["wr2"])], 256)
        if not last:
            act(T.ex[:], T.wr2[:], AF.Exp, 512, ["wr2"], ["ex"], bias=EB + EA * (W0 + 240), scale=-EA)
            lin("gn", T.gn[:], AF.Relu, W0 + 240, [(2, "idmH", T.c3[:], ["ones"]), (0, "idmH") + sg, (1, "idmH") + sg, (2, "idn", T.wr2[:], ["wr2"]), (2, "id1", T.ex[:], ["ex"])])
        lin("nd", T.nx[:, 0:256], ID, -8.0, [(0, "id1") + yw, (0, "id8") + sg, (0, "id1", T.tz[:], ["tz"])], 256)
        for j in range(4):
            h = j * NH // 4
            sh = str(h)
            lr = slice(LH * h, LH * h + LH)
            rb = 6 if h == 0 else 0
            kco = "co%d" % (h if NH == 2 else [v for v, x in enumerate(OPT["cut"]) if x[0] <= 64 * j][-1])
            cik = ["ci" + sh] if NH == 2 else ["ci%d" % v for v in range(len(OPT["cut"]))]
            for s, o, n, x, kx in ((0, OG2, "G2", T.g1w, "g1w"), (1, OG1, "G1", T.g2w, "g2w")):
                u0 = 2 * (2 * j + s)
                both = u0 not in OPT["vc"][t] and u0 + 1 not in OPT["vc"][t] and u0 in OPT["big"]
                if both:
                    act(T.gb[:, 512 * u0:512 * u0 + 1024], win(o).indirect(T.co[:, 64 * j:64 * j + 64]), ID, GA * 1024, tk(n) + [kco], ["gb%d" % u0, "gb%d" % (u0 + 1)])
                for e in range(2):
                    u = u0 + e
                    a1, cc = 512 * u, 64 * j + 32 * e
                    mkeys = ["mm%d.%d" % (u, v) for v in range(MB)]
                    if u in OPT["vc"][t]:
                        for v in range(MB):
                            tt(T.mm[:, a1 + LH * v:a1 + LH * v + LH], win(o).indirect(T.co[:, cc + QH * v:cc + QH * v + QH]), x[:, lr], A.min, GA * LH,
                               tk(n) + [kco, kx + sh], [mkeys[v]])
                    else:
                        if not both:
                            act(T.gb[:, a1:a1 + 512], win(o).indirect(T.co[:, cc:cc + 32]), ID, GA * 512, tk(n) + [kco], ["gb%d" % u])
                        tt(T.mm[:, a1:a1 + 512], ps[rb + s][:], T.gb[:, a1:a1 + 512], A.min, 512, [pk(rb + s), "gb%d" % u], mkeys)
            y = j // 3
            b, wd = 2 + y, (192, 64)[y]
            kb, sy, yr = pk(b), str(y), slice(192 * y, 192 * y + wd)
            x = ps[b][:, 0:wd]
            if j % 3 == 0:
                mm(x, C["idm128"], T.cst[:, 0:wd], True, False, wd, ["idm128", "cst"], [kb])
                named = y == 1 and lim == 11
                left = [int(named)]
            for s in range(2):
                mkeys = ["mm%d.%d" % (2 * (2 * j + s) + e, v) for e in range(2) for v in range(MB)]
                rows(ps[b][:, 64 * (j % 3):64 * (j % 3) + 64], T.zq, "zq", (T.mm, 1024 * (2 * j + s)), mkeys, 64, False, False, b, left)
            if named:
                cp(T.kc[:, yr], T.ci[:, yr], 64, cik, ["kc1"])
                mm(x, T.idf[:], T.kc[:, yr], False, True, 64, ["idf", "kc1"], [kb], 4)
            if j < 2:
                continue
            k12 = 512 * (C12 - W0 - 192) if lim == 13 else 0
            if lim == 13:
                act(T.n1[:, yr], x, ID, wd, [kb], ["n1" + sy], bias=128.0, scale=1.0 / (512 * (C12 - W0)))
                act(T.n4[:, yr], T.n1[:, yr], AF.Relu, wd, ["n1" + sy], ["n4" + sy], bias=160 * k12, scale=-k12)
                tt(x, x, T.n4[:, yr], A.add, wd, [kb, "n4" + sy], [kb])
            if lim > 11:
                act(T.n3[:, yr], x, ID, wd, [kb], ["n3" + sy], bias=2.0 ** 22 * (192 - 0.375) - 32 * k12)
                act(T.n4[:, yr], T.n3[:, yr], ID, wd, ["n3" + sy], ["n4" + sy], bias=192.0 * 8016 * 512 - 32 * k12, scale=-8016.0 / 8192)
                tt(x, x, T.n4[:, yr], A.add, wd, [kb, "n4" + sy], [kb])
            if not named:
                tt(T.kc[:, yr], x, T.ci[:, yr], A.add, wd, [kb] + cik, ["kc" + sy])
            if y == 0:
                tt(T.kc[:, 0:16], T.kc[:, 0:16], sm("dk"), A.min, 32, ["kc0", "dk0"], ["kc0"])
                tt(T.r64[:, 64:128], T.kc[:, 64:128], T.kc[:, 128:192], A.min, 128, ["kc0"], ["pre0"])
                tt(T.r64[:, 128:192], T.r64[:, 64:128], T.kc[:, 0:64], A.min, 128, ["kc0", "pre0"], ["pre1"])
            else:
                tt(T.r64[:, 192:256], x if named else T.kc[:, yr], T.r64[:, 128:192], A.min, 64 if named else 128, [kb, "kc1", "pre1"], ["pre2"])
                tree(2, (T.r64[:, 192:224], T.r64[:, 224:256]), "pre2", T.kj[:], "kj0")
        ts(T.ce[:], T.kj[:], 8191, None, A.bitwise_and, None, 16, hk("kj"), ["ce"])
        cl = T.cl[:, 0:16]
        xc = T.xf[:, 1:32:2]
        cp(xc, T.ce[:], 16, ["ce"], ["xfc"])
        cp(cl, T.ce[:], 16, ["ce"], ["cl"])
        cp(T.rr[:, 1, :], io[:].indirect(cl), GA * 256, iok + ["cl"], ["rr"])
        act(T.wqc[:, 0:256], win(OE2).indirect(cl), ID, GA * 256, tk("E2") + ["cl"], ["wqc0"], bias=RND)
        act(T.wqc[:, 256:512], win(OE1).indirect(cl), ID, GA * 256, tk("E1") + ["cl"], ["wqc1"], bias=RND)
        yc = T.nx[:, 256:512]
        act(yc, win(OY).indirect(cl), ID, GA * 256, tk("Y") + ["cl"], ["yc"])
        lin("w2c", T.wx[:, 0:256], ID, -W0, [(0, "id1", T.rl[:], ["rl"]), (0, "id1", T.wqc[:, 0:256], ["wqc0"])], 256)
        if last:
            act(T.wx[:, 768:1024], T.wqc[:, 256:512], ID, 256, ["wqc1"], ["s3"], bias=-W0)
        else:
            act(T.g2c[:], win(OG2).indirect(cl), ID, GA * 256, tk("G2") + ["cl"], ["g2c"])
            lin("s3", T.s3[:], ID, -W0, [(0, "id1", T.wqc[:, 256:512], ["wqc1"]), (0, "id1", yc, ["yc"]), (0, "id1", T.gn[:, 256:512], ["gn"])], 256)
        pm_, km = ps[BK["cm"]], pk(BK["cm"])
        mm(pm_[:], C["idn"], T.th[:], True, False, 512, ["idn", "th"], [km])
        mm(pm_[:], C["idn"], T.c4[:], False, False, 512, ["idn", "c4"], [km])
        left = [0]
        for late in range(2):
            e0 = 0
            for i in range(32):
                q = i // 2
                n = 256 - 16 * q
                e1 = e0 + n
                wq_ = 2.0 ** (90 - 12 * q)
                if i % 2 == 0 and q < OPT["ww"]:
                    ke = ("ea%d", "eb%d")[late] % i
                    ts(T.eb[:, late, e0:e1], T.rr[:, late, 16 * q:256], T.xf[:, i:i + 1], wq_, A.is_equal, A.mult, n / 2, [("rrw", "rr")[late], "xfw"], [ke])
                    mma(left, [(pm_[:, q:16, late, :], C["bw"], T.eb[:, late, e0:e1])], n, ["bw", ke], [km])
                elif late:
                    ts(T.eb[:, :, e0:e1], T.rr[:, :, 16 * q:256], T.xf[:, i:i + 1], wq_, A.is_equal, A.mult, n, ["rr", "rrw", "xfw", "xfc"], ["eb%d" % i, "ea%d" % i])
                    mma(left, [(pm_[:, q:16, s, :], C["bw"], T.eb[:, s, e0:e1]) for s in range(2)], n, ["bw", "eb%d" % i], [km])
                e0 = e1
        if not last:
            act(sm("b1"), xc, ID, 16, ["xfc"], ["b1"], bias=float(TS))
            tt(T.bb[:, 0:16], sm("b1"), sm("p1"), A.min, 32, ["b1", "p1"], ["bba"])
        ts(sm("b2"), T.kj[:], -385.0 * 8192, None, A.add, None, 16, hk("kj"), ["b2"])
        tt(T.bb[:, 16:32], sm("b2"), T.xf[:, 0:32:2], A.max, 32, ["b2", "xfw"], ["bbb"])
        act(T.bb[:, 32:48], xc, ID, 16, ["xfc"], ["bbc"])
        lo = 16 if last else 0
        act(T.hm[:, lo:48], T.bb[:, lo:48], ID, 48, ["bba", "bbb", "bbc"], ["hm"], scale=2.0 ** -15)
        act(T.sn[:], pm_[:], AF.Sign, 512, [km], ["sn"])
        op("V", lambda: V.tensor_tensor_scan(T.sc[:], T.keep[:], T.sn[:], 0.0, A.mult, A.max), vc(256), ["keep", "sn"], ["sc"])
        tt(T.o1[:, lo:48], T.sc[:].indirect(T.hitl[:, 0:(48 - lo) // 16]), T.hm[:, lo:48], A.max, 100, ["sc", "hitl", "hm"], ["o1"])
        tt(T.o2[:, lo:48], T.o1[:, lo:48], T.d3[:, lo:48], A.min, 96, ["o1", "d30", "d31", "d32"], ["o2"])
        ts(T.ol[:, lo:48], T.o2[:, lo:48], 2.0 ** 15, None, A.mult, None, 48, ["o2"], ["ol"])
        def scatter(o, nt, l0, n, a, a0, b, b0, r, w, parts):
            for x in range(0, n, n // parts):
                m = n // parts
                out = win(o, nt).indirect(T.ol[:, l0 + x // 16:l0 + (x + m) // 16])
                if b is None:
                    cp(out, a[:, a0 + x:a0 + x + m], SCA * m, ["ol"] + r, w)
                else:
                    tt(out, a[:, a0 + x:a0 + x + m], b[:, b0 + x:b0 + x + m], A.add, SCA * m, ["ol"] + r, w)
        sp = OPT["split"]
        if not last:
            scatter(OY, 2, 0, 256, T.s1, 0, T.s1, 256, ["s1"], tk("Y", "G2"), 1)
            scatter(OG2, 1, 16, 256, T.g2c, 0, T.gn, 0, ["g2c", "gn"], tk("G2"), sp[0])
            scatter(OG1, 2, 0, 256, T.s3, 0, None, 0, ["s3"], tk("G1", "E1"), sp[0])
        scatter(OE2, 1, 16, 512, T.wx, 0, T.nx, 0, ["w2c", "wn", "nd", "yc"], tk("E2"), 1 if last else sp[1])
        scatter(OE1, 1, 16, 512 if last else 256, T.wx, 512, T.nx, 0, ["wn", "nd", "yc", "s3"], tk("E1"), 1 if last else sp[2])
        if not last:
            act(T.exf[:], T.o2[:, 32:48], AF.Sign, 16, ["o2"], ["exf"], bias=(NM - 0.5) * 2.0 ** -15, scale=-1.0)
            mms(4, 0, 16, [("ones", T.exf[:], ["exf"])])
            act(sm("b1"), ps[4][:, 0:16], ID, 16, ["ps4"], ["ac0", "b1"], acc=T.ac[:, 0:1])
            act(T.ac[:, 1:2], T.ac[:, 0:1], ID, 1, ["ac0"], ["ac1"], bias=1024 - 0.375, scale=0.5)
    dma(T.ys[:], tb[:, OE2:OE2 + NM], 1 << 20, tk("E2"), ["ys"])
    mmx([(ps[4][:, 0:64], C["id1"], tb[:, OE1 + 64 * j:OE1 + 64 * j + 64], j == 0, j == 63) for j in range(64)], 64, ["id1"] + tk("E1"), ["ps4"])
    act(T.yfo[:], ps[4][:, 0:64], ID, 64, ["ps4"], ["yfo"])
    dma(T.yf[:], T.yfo[:], 32768, ["yfo"], ["yf"])
    return ops


def depend(ops):
    lw, rd, acc = {}, {}, {}
    for i, o in enumerate(ops):
        raw, oth = set(), set()
        for k in o["r"]:
            if k in lw:
                raw.add(lw[k])
            raw.update(acc.get(k, ()))
        for k in o["w"]:
            if k in lw:
                oth.add(lw[k])
            oth.update(rd.get(k, ()))
            if not o.get("acc"):
                oth.update(acc.get(k, ()))
        for k in o["r"]:
            if k.startswith("ps"):
                oth.update(j for j in rd.get(k, ()) if ops[j]["e"] != o["e"])
        for k in o["r"]:
            rd.setdefault(k, []).append(i)
        for k in o["w"]:
            if o.get("acc"):
                acc.setdefault(k, []).append(i)
            else:
                lw[k] = i
                rd[k] = []
                acc[k] = []
        oth.discard(i)
        o["raw"], o["dep"] = raw, raw | oth


def schedule(ops):
    n = len(ops)
    fw = [[] for _ in ops]
    bw = [[] for _ in ops]
    for j, o in enumerate(ops):
        for i in sorted(o["dep"]):
            e = ops[i]["e"]
            same = o["e"] == e and ops[i]["k"] == "c" and e == "P"
            d = ops[i]["lat"] + (0 if same else OPT["hop"] if o["e"] == e else OPT["xhop"])
            fw[i].append((j, d))
            bw[j].append((i, d))
    cost = [o["c"] * OPT["mul"].get(o["e"], 1.0) for o in ops]
    eng = [o["e"] for o in ops]
    up = [1e9 - 1e6 * i if o["k"] == "d" and not o["r"] else OPT["boost"] if o["w"][0] in BOOST else 0.0 for i, o in enumerate(ops)]

    def sweep(succ, pred, pr, rdy, look):
        left = [len(p) for p in pred]
        free = {e: 0.0 for e in eng}
        cand = {e: set() for e in free}
        for i in range(n):
            if left[i] == 0:
                cand[eng[i]].add(i)
        order, t0 = [], [0.0] * n
        for _ in range(n):
            e, first = min(((e, min(max(rdy[i], free[e]) for i in c)) for e, c in cand.items() if c), key=lambda x: (x[1], str(x[0])))
            i = max((i for i in cand[e] if rdy[i] <= first + look), key=lambda i: (pr[i] - OPT["lam"] * max(0.0, rdy[i] - first), -i))
            cand[e].discard(i)
            t0[i] = max(rdy[i], free[e])
            fin = t0[i] + cost[i]
            if e is not None:
                free[e] = fin
            order.append(i)
            for j, d in succ[i]:
                rdy[j] = max(rdy[j], fin + d)
                left[j] -= 1
                if left[j] == 0:
                    cand[eng[j]].add(j)
        return order, t0
    pr = [0.0] * n
    for i in range(n - 1, -1, -1):
        pr[i] = cost[i] + max([pr[j] + d for j, d in fw[i]], default=ops[i]["lat"])
    rng = np.random.default_rng(OPT["seed"])
    best = None
    for it in range(OPT["iters"] + 1):
        order, t0 = sweep(fw, bw, [pr[i] + up[i] for i in range(n)], [0.0] * n, OPT["look"])
        end = max(t0[i] + cost[i] + ops[i]["lat"] for i in range(n))
        if best is None or end <= best[0]:
            best = (end, order, t0)
        nz = (rng.random(n) - 0.5) * OPT["noise"] * (rng.random(n) < OPT["frac"])
        t0 = best[2]
        _, b0 = sweep(bw, fw, [t0[i] + cost[i] + float(nz[i]) for i in range(n)], [0.0 if fw[i] else ops[i]["lat"] for i in range(n)], OPT["look"])
        pr = [b0[i] + cost[i] for i in range(n)]
    pred = [[(i, cost[i] + d) for i, d in p] for p in bw]
    deps = [o["dep"] for o in ops]

    def times(order):
        t, by, free, prev, end, tip = [0.0] * n, [-1] * n, {}, {}, 0.0, -1
        for j in order:
            s, b = 0.0, -1
            for i, d in pred[j]:
                if t[i] + d > s:
                    s, b = t[i] + d, i
            e = eng[j]
            if e is not None:
                if free.get(e, -1.0) >= s:
                    s, b = free[e], -2 - prev[e]
                free[e], prev[e] = s + cost[j], j
            t[j], by[j] = s, b
            if s + cost[j] + ops[j]["lat"] > end:
                end, tip = s + cost[j] + ops[j]["lat"], j
        return end, t, by, tip
    cur = list(best[1])
    end, t0, by, tip = times(cur)
    best = (end, list(cur), t0)
    for it, (r1, r2, r3, r4) in enumerate(rng.random((OPT["moves"], 4)).tolist()):
        links, j = [], tip
        while j != -1:
            if by[j] <= -2:
                links.append((-2 - by[j], j))
            j = by[j] if by[j] > -2 else -2 - by[j]
        a, b = links[int(r1 * len(links))]
        k = (1, 1, 2, 3, 5, 8)[int(r2 * 6)]
        pa, pb = cur.index(a), cur.index(b)
        if r3 < 0.5:
            while k > 1 and pa > 0:
                pa -= 1
                k -= eng[cur[pa]] == eng[b]
            seg, need = cur[pa:pb + 1], {b}
            for x in reversed(seg):
                if x in need:
                    need |= deps[x]
            new = [x for x in seg if x in need] + [x for x in seg if x not in need]
        else:
            while k > 1 and pb < n - 1:
                pb += 1
                k -= eng[cur[pb]] == eng[a]
            seg, aft = cur[pa:pb + 1], {a}
            for x in seg:
                if deps[x] & aft:
                    aft.add(x)
            new = [x for x in seg if x not in aft] + [x for x in seg if x in aft]
        new = cur[:pa] + new + cur[pb + 1:]
        res = times(new)
        if res[0] <= end - OPT["temp"] * math.log(1 - r4):
            cur = new
            end, t0, by, tip = res
            if it % 20 == 0:
                cur.sort(key=lambda x: t0[x])
            if end < best[0]:
                best = (end, list(cur), t0)
    INFO["end"] = best[0]
    for i, o in enumerate(ops):
        o["t0"] = best[2][i]
    loads = [i for i, o in enumerate(ops) if o["k"] == "d" and not o["dep"]]
    return loads + [i for i in best[1] if i not in loads]


def rank_program(g, core, T, topo):
    rank = T.rank_of(core)
    if rank is None:
        return
    cores = list(T.cores)
    to = cores[(rank + 1) % len(cores)]
    fro = cores[(rank - 1) % len(cores)]
    assert topo.may_write(core, to)
    ad = topo.addr(to)
    en = topo.engines(core, to)
    hf = len(en) // 2
    mk = [sum(1 << e for e in en[:hf]), sum(1 << e for e in en[hf:])]
    nin = len(topo.engines(fro, core))
    ops = build(g, T, DstId(rid=ad[0], pnc=ad[1]), mk)
    depend(ops)
    if "order" not in INFO:
        INFO["order"] = schedule(ops)
    order = INFO["order"]
    queue = {"V": g.vector, "S": g.scalar, "P": g.tensor, "G": g, "Y": g.sync}
    pos = {i: p for p, i in enumerate(order)}
    need = {}
    known = {e: {} for e in queue}
    clock = {}
    for i in order:
        o = ops[i]
        if o["k"] == "x":
            clock[i] = {i: 0}
            continue
        best = {}
        for j in o["dep"]:
            d = ops[j]
            if d["k"] == "r":
                continue
            if d["k"] != "c":
                best[j] = (0, j)
            elif d["e"] == o["e"] and o["k"] == "c" and o["e"] == "P":
                continue
            elif pos[j] > best.get(d["e"], (-1, 0))[0]:
                best[d["e"]] = (pos[j], j)
        kn = known[o["e"]]
        ws = []
        for e, (p, j) in sorted(best.items(), key=lambda x: -pos[x[1][1]]):
            if p > kn.get(e, -1):
                ws.append(j)
                for k, v in clock[j].items():
                    if v > kn.get(k, -1):
                        kn[k] = v
        need[i] = ws
        clock[i] = dict(kn)
        if o["k"] == "c":
            clock[i][o["e"]] = pos[i]
        else:
            clock[i][i] = 0
    wanted = set(j for ws in need.values() for j in ws)
    cnt = {}
    tok = {}
    nd = 0
    outs = []
    for i in order:
        o = ops[i]
        if o["k"] == "x":
            tok[i] = (T.sem[o["fn"]], nin)
            continue
        q = queue[o["e"]]
        for j in need[i]:
            q.wait_ge(tok[j][0], tok[j][1])
        ins = o["fn"]()
        if o["k"] == "d":
            tok[i] = (T.sem["d%d" % nd], 16)
            nd += 1
            ins.then_inc(tok[i][0], 16)
            if i not in wanted:
                outs.append(i)
        elif o["k"] == "c" and i in wanted:
            cnt[o["e"]] = cnt.get(o["e"], 0) + 1
            tok[i] = (T.sem["e" + o["e"]], cnt[o["e"]])
            ins.then_inc(tok[i][0], 1)
    for i in outs:
        g.sync.wait_ge(tok[i][0], 16)
    g.wait_ge(T.sem.sent, (NV - 1) * len(en))
